import numpy as np, ml_dtypes
CORES = [24,25,26,27,28,29,30,31]
N = 8
BF = ml_dtypes.bfloat16
def gentries(a):
    return np.ascontiguousarray(a.reshape(8, 16, -1).transpose(0, 2, 1)).reshape(8, -1)
def gtable(e):
    e = np.asarray(e); return np.ascontiguousarray(e.reshape(8, -1, 16).transpose(0, 2, 1)).reshape(128, -1).astype(np.int32)
NM, LN, T, S = 4096, 192, 3, 3
LIMS = (14, 11, 13)
WT = np.array([1, 16, 256, 37, 411, 93, 777, 165, 1029, 251, 1313, 339, 1583, 503, 1847, 618], np.int32)
KA = np.array([3, 61, 118, 207, 346, 419, 530, 677, 742, 895, 1011, 1164, 1283, 1450, 1629, 1874], np.int32)
LO = min(LIMS)
def parts(rng):
    lo = rng.choice(np.array([0.7, 0.85, 0.95], np.float32), (N, 8, 1, 1, 1)); h = lo + (1 - lo) * rng.random((N, 8, 1, 2, NM), dtype=np.float32)
    wr = np.minimum((16 * h * rng.random((N, 8, 16, 2, NM), dtype=np.float32)).astype(np.int32), 15)
    da = rng.integers(0, 16, (N, 8, 16, 2, NM), dtype=np.int32)
    ls = rng.integers(0, NM, (N, 8, LN, 16)); ls = np.where(rng.random((N, 8, LN, 1)) < 0.3, ls >> 3, ls)
    z = rng.integers(0, 16, (N, 8, 16, LN))
    ls[:, :, 1::8] = ls[:, :, 0::8]; z[..., 1::8] = z[..., 0::8]
    return wr, da, ls, z
def pack(wr, da, ls, z):
    return {"pg": np.ascontiguousarray((16 * wr + da).reshape(N, 128, 2 * NM)).astype(np.float32).astype(BF),
            "nm": np.stack([gtable(a.reshape(8, -1)) for a in ls]), "zv": np.ascontiguousarray(z.reshape(N, 128, LN)).astype(np.float32).astype(BF)}
def setup_inputs(rng):
    wr, da, ls, z = parts(rng)
    return pack(wr, da, ls, z)
def setup_inputs_spread(rng):
    wr, da, ls, z = parts(rng)
    p = np.exp2(rng.integers(-2, 3, (N, 8, 1, 2, NM))).astype(np.float32)
    wr = np.minimum((16 * rng.random((N, 8, 16, 2, NM), dtype=np.float32) ** p).astype(np.int32), 15)
    da = da & rng.choice(np.array([0, 1, 3, 8, 12, 15], np.int32), (N, 8, 16, 1, NM))
    ls = np.minimum((NM * rng.random((N, 8, LN, 16)) ** rng.choice(np.array([1.0, 2.0, 4.0]), (N, 8, LN, 1))).astype(np.int64), NM - 1)
    z = z & rng.choice(np.array([0, 1, 4, 7, 15, 15]), (N, 8, 16, LN))
    return pack(wr, da, ls, z)
def setup_inputs_ends(rng):
    kind = rng.choice(6, (N, 8, NM), p=np.array([0.12, 0.08, 0.06, 0.06, 0.38, 0.3])); k = kind[:, :, None, None, :]
    e = rng.integers(0, 2, (N, 8, 16, 2, NM), dtype=np.int16); both = rng.random((N, 8, 16, 1, NM), dtype=np.float32) < 0.4
    side = np.array([0, 1], np.int16).reshape(1, 1, 1, 2, 1)
    top = np.where(both, np.int16(1), e); top = np.where(k == 3, side, top); top = np.where(k == 2, 1 - side, top); top = np.where(k == 1, np.int16(1), top); top = np.where(k == 0, np.int16(0), top)
    under = np.where(rng.random((N, 8, 1, 1, NM)) < 0.5, LIMS[0] - 1, LO - 1).astype(np.int16)
    wr = np.where(k == 5, under, 15 * top).astype(np.int32); da = 15 * np.where(k == 5, e, top).astype(np.int32)
    u0 = int(15 * np.add.reduce(WT)) & (NM - 1); cm = ((u0 * u0 >> 5) + KA.astype(np.int64) * u0) & (NM - 1)
    for q in range(N):
        for g in range(8):
            if g in (2, 7): wr[q, g][:, :, cm] = LIMS[0] - 1
            a, b = (NM - 1, 0) if g in (1, 4) else (0, NM - 1)
            wr[q, g][:, :, a] = 0; da[q, g][:, :, a] = 0; wr[q, g][:, :, b] = 15; da[q, g][:, :, b] = 15
    wr[:, 6, :, :, 1:3] = 15; da[:, 6, :, :, 1:3] = 15
    pos = np.argsort(rng.random((N, 8, LN, 16)), axis=-1) < 10
    ls = np.where(pos, (NM - 1) * rng.integers(0, 2, pos.shape), rng.integers(0, NM, pos.shape))
    z = 15 * rng.integers(0, 2, (N, 8, 16, LN)); o = rng.integers(0, 8, (N, 8, 1, LN)); z = np.where(o == 0, 0, np.where(o == 1, 15, z))
    for q in range(N):
        some = np.setdiff1d(np.nonzero(kind[q, 7] == 5)[0], np.append(cm, [0, NM - 1]))
        ls[q, 7] = np.where(pos[q, 7], 0, rng.choice(some, (LN, 16)))
        ls[q, 7, LN - 1] = np.where(np.arange(16) % 2 == 1, NM - 1, 0)
        ls[q, 6, LN - 1, 0] = 2; ls[q, 6, LN - 1, 1] = 1; ls[q, 6, LN - 1, 2] = NM - 1
    z[:, 7, :, LN - 1] = 0; z[:, 6, :, LN - 1] = 0
    return pack(wr, da, ls, z)
def setup_inputs_corners(rng):
    wr, da, ls, z = parts(rng); rot = int(rng.integers(0, 8)); sh = (16, 2, NM)
    z[..., ::5] = 0; z[..., 2::5] = 15
    for q in range(N):
        for g in range(8):
            j = (g + q + rot) % 8; a = wr[q, g]; d = da[q, g]
            if j == 0:
                a[...] = rng.integers(0, LO, sh)
                n = np.append(np.sort(rng.permutation(NM - 1)[:3]), NM - 1); i = int(rng.integers(0, 16))
                d[:, :, n[:2]] = 15; d[i, :, n[0]] = 14; d[:, :, n[2:]] = 0; d[15 - i, :, n[2]] = 1
                ls[q, g, 0::10, 3] = n[0]; ls[q, g, 0::10, 15] = n[1]; ls[q, g, 2::10, 0] = n[3]; ls[q, g, 2::10, 9] = n[2]
            if j == 1:
                a[...] = 15; d[:, :, int(rng.integers(0, 64))::64] = 15
            if j == 2: a[...] = np.where(rng.random(sh) < 0.25, rng.choice(np.array([LO - 1, LO, LIMS[0] - 1, LIMS[0]]), sh), rng.integers(0, 4, sh))
            if j == 3:
                a[:, 0] = rng.integers(14, 16, (16, NM)); a[:, 1] = rng.integers(0, LO, (16, NM))
                d[:, :, ::2] = 0; z[q, g, :, ::2] = 0; ls[q, g, ::16] -= ls[q, g, ::16] & 1
            if j == 4: d[...] = rng.integers(0, 16, (16, 1, 1))
            if j == 5: a[:, 1] = a[:, 0]
            if j == 6:
                fresh = rng.permutation(NM)[:NM >> 4]; a[...] = 15; a[:, :, fresh] = rng.integers(0, LO, (16, 2, NM >> 4))
            if j == 7: ls[q, g] = rng.choice(np.array([0, 1, NM - 2, NM - 1]), (LN, 16))
    return pack(wr, da, ls, z)
def hang(rng, a, d, w, u):
    y = rng.integers(0, 16, (16, len(w))); y[:3] = 0
    v = (u - np.add.reduce(WT.astype(np.int64)[:, None] * y, axis=0)) & (NM - 1)
    y[0] = v & 15; y[1] = (v >> 4) & 15; y[2] = v >> 8
    a[:, :, w] = 15; d[:, :, w] = y[:, None, :]
def firsts():
    u = np.arange(NM, dtype=np.int64)
    return ((u * u >> 5)[:, None] + KA.astype(np.int64) * u[:, None]) & (NM - 1)
def mates(rng, a, w):
    v = np.add.reduce(a.reshape(32, NM), axis=0).astype(np.int64); v[w] = 1 << 20
    c = firsts()
    low = np.min(v[c] * NM + c, axis=1); b = np.where(low >= NM << 20, -1, low & (NM - 1))
    val, first = np.unique(b, return_index=True)
    return rng.permutation(first[val >= 0])
def setup_inputs_crowd(rng):
    wr, da, ls, z = parts(rng); pr = rng.permutation(N)
    for q in range(N):
        for g in range(8):
            a = wr[q, g]; d = da[q, g]; a[...] = rng.integers(0, 3, (16, 2, NM)); j = (g + q) % 8
            o = rng.permutation(NM)
            if j == 6: o = o[o > 0]
            w = o[:LN]
            if q == pr[0] or q == pr[1]:
                old = o[LN:LN + (NM >> 3)]; a[:, :, old] = 15; d[:, :, old] = 15 * rng.integers(0, 2, (16, 1, len(old)))
                hang(rng, a, d, w, np.resize(mates(rng, a, np.append(w, old)), LN)); ls[q, g] = w[:, None]
                if q == pr[1] and g == 7: ls[q, g, LN - 1] = w[0]
            elif j < 2:
                us = np.resize(mates(rng, a, w), LN); hang(rng, a, d, w[:2], us[:2]); ls[q, g] = w[0]
                if j == 1: ls[q, g, LN - 1] = w[1]
            elif j < 4:
                us = np.resize(mates(rng, a, w), LN); one = np.full(LN, us[0])
                if j == 3: one[LN - 1] = us[1]
                hang(rng, a, d, w, one); ls[q, g] = w[:, None]
            elif j < 6:
                ls[q, g] = w[:, None]
                if j == 5: ls[q, g, LN - 1] = w[0]
            elif j == 6:
                a[:, :, 0] = 0; us = np.nonzero(np.any(firsts() == 0, axis=1))[0]
                hang(rng, a, d, w, np.full(LN, int(rng.choice(us)))); ls[q, g] = w[:, None]
            else:
                a[...] = rng.integers(LIMS[0] - 2, LIMS[0], (16, 2, NM)); sp = o[LN:LN + (NM >> 2)]; a[:, :, sp] = 0
                a[rng.integers(0, 16, len(sp)), rng.integers(0, 2, len(sp)), sp] = 15
                hang(rng, a, d, w, rng.permutation(NM)[:LN]); ls[q, g] = w[:, None]
    return pack(wr, da, ls, z)
def check_inputs(d):
    bad = []
    for k, hi in (("pg", 255), ("nm", NM - 1), ("zv", 15)):
        x = np.asarray(d[k]).astype(np.float32)
        if not np.all((x >= 0) & (x <= hi) & (x == np.floor(x))): bad.append("range of " + k)
    return bad
def pick(a, ix):
    return np.take_along_axis(a, ix[:, :, None, :], 3)
def reference(pg, nm, zv):
    v = pg.astype(np.float32).astype(np.int32).reshape(N, 8, 16, 2, NM); wr = v >> 4; da = v & 15
    ls = np.stack([gentries(a) for a in nm]).astype(np.int32)
    z = zv.astype(np.float32).astype(np.int32).reshape(N, 8, 16, LN)
    A = np.zeros((N, 1, 1, 1), np.int32); low = np.tril(np.ones((LN, LN), bool), -1); NONE = 1 << 30
    for t in range(T):
        lim = LIMS[t]
        if t > 0: ls = np.roll(ls, S, axis=0); z = np.roll(z, S, axis=0)
        f = wr[:, :, :, 0]; s = wr[:, :, :, 1]
        y = np.where(f <= s, da[:, :, :, 0], da[:, :, :, 1])
        lk = ls.reshape(N, 8, LN, 16)
        sc = np.add.reduce(np.abs(pick(y, ls).reshape(N, 8, 16, LN, 16) - z[..., None]), axis=2).astype(np.int32)
        w = NM - 1 - (np.max(sc * NM + (NM - 1 - lk), axis=3) & (NM - 1))
        yw = pick(y, w); fw = pick(f, w); sw = pick(s, w)
        u = (np.add.reduce(WT[:, None] * yw, axis=2) & (NM - 1)).astype(np.int32)
        faulty = np.any((fw >= lim) & (sw >= lim), axis=2)
        c = ((u * u >> 5)[..., None] + KA * u[..., None] + A) & (NM - 1)
        cx = c.reshape(N, 8, LN * 16)
        m1 = np.minimum(fw[..., None], pick(s, cx).reshape(N, 8, 16, LN, 16)); m2 = np.minimum(pick(f, cx).reshape(N, 8, 16, LN, 16), sw[..., None])
        ok = np.max(np.maximum(m1, m2), axis=2) < lim
        best = np.min(np.where(ok, np.add.reduce(m1 + m2, axis=2) * NM + c, NONE), axis=3)
        has = faulty & (best < NONE); cl = np.where(has, best & (NM - 1), -1)
        wa, wb, ca, cb = w[:, :, :, None], w[:, :, None, :], cl[:, :, :, None], cl[:, :, None, :]
        hit = (wa == wb) | (wa == cb) | (ca == wb) | ((ca == cb) & (ca >= 0))
        com = ~np.any(hit & low, axis=3)
        q, g, l = np.nonzero(com & ~faulty); n = w[q, g, l]
        zn = z[q, g, :, l][:, :, None]; od = da[q, g, :, :, n]; ow = wr[q, g, :, :, n]
        nw = np.minimum(15, ow + (od != zn))
        ex = com & has; q2, g2, l2 = np.nonzero(ex); n2 = w[q2, g2, l2]; o2 = cl[q2, g2, l2]
        a1 = wr[q2, g2, :, 1, n2]; b1 = wr[q2, g2, :, 1, o2]; ya = y[q2, g2, :, n2]; yb = y[q2, g2, :, o2]
        wr[q, g, :, :, n] = nw; da[q, g, :, :, n] = zn
        wr[q2, g2, :, 1, n2] = b1; wr[q2, g2, :, 1, o2] = a1
        da[q2, g2, :, :, n2] = ya[:, :, None]; da[q2, g2, :, :, o2] = yb[:, :, None]
        A = np.add.reduce(ex.reshape(N, -1).astype(np.int32), axis=1).astype(np.int32).reshape(N, 1, 1, 1)
        k = np.arange(16 * LN, dtype=np.int32).reshape(LN, 16)
        ls = (((lk * (2 * (u & 1023) + 1)[..., None] >> 5) + lk + 37 * k) & (NM - 1)).reshape(N, 8, 16 * LN)
        z = np.abs(z - yw)
    e = 16 * wr + da
    return {"ys": np.ascontiguousarray(e[:, :, :, 1].reshape(N, 128, NM)).astype(np.float32).astype(BF),
            "yf": np.add.reduce(e[:, :, :, 0].reshape(N, 128, NM >> 6, 64), axis=2).astype(np.float32),
            "yn": np.stack([gtable(a) for a in ls]).astype(np.float32),
            "yz": np.ascontiguousarray(z.reshape(N, 128, LN)).astype(np.float32).astype(BF)}

@@ -1,0 +1,678 @@
+from concourse.bass import DstId, RemoteDMATransfer
+from concourse.mybir import AluOpType as ALU, AxisListType as AX, ActivationFunctionType as AF
+
+N, NM, LN, STEP = 8, 4096, 192, 3
+LIMS = (14, 11, 13)
+WT = (1, 16, 256, 37, 411, 93, 777, 165, 1029, 251, 1313, 339, 1583, 503, 1847, 618)
+KA = (3, 61, 118, 207, 346, 419, 530, 677, 742, 895, 1011, 1164, 1283, 1450, 1629, 1874)
+TW = NM + 2 * LN
+YO = 208.0
+FO = 204.0
+CH = (512, 512, 1024, 1024, 1024)
+HUGE = float(2 ** 98)
+
+B16, F32, I32, U16, F16 = "bfloat16", "float32", "int32", "uint16", "float16"
+SB = {
+    "E1": (TW, B16), "E2": (TW, B16), "Y": (TW, B16), "F": (TW, B16), "S": (TW, B16), "IO": (TW, I32),
+    "sel": (NM, B16), "At": (NM, B16), "S1": (NM, B16), "GB": (6144, B16), "EQ": (4992, B16),
+    "nmi": (192, I32), "nmf": (192, F32), "X1": (384, F32), "X2": (384, F32), "ynf": (192, F32),
+    "off0": (192, U16), "off1": (192, U16), "off2": (192, U16),
+    "Lf0": (192, F32), "Lf1": (192, F32), "Lf2": (192, F32),
+    "z0": (768, B16), "z1": (768, B16), "z2": (768, B16),
+    "so0": (192, U16), "so1": (192, U16), "sl0": (192, F32), "sl1": (192, F32), "sl2": (192, F32),
+    "sz0": (192, B16), "sz1": (192, B16), "sz2": (192, B16),
+    "ci": (16, I32), "cj": (16, I32), "cf": (16, F32), "ramp": (144, F32), "r128": (128, F32),
+    "ct": (96, F32), "cu": (192, F32), "cv": (192, F32),
+    "Z1": (144, B16), "Zn": (144, B16), "Zp": (144, B16), "Zw": (144, F16),
+    "I1": (128, B16), "In": (128, B16), "I16": (128, B16), "In16": (128, B16), "In32": (128, B16),
+    "Ipen": (128, B16), "Inf": (128, B16), "I512": (128, F16), "If": (128, F32), "BO": (128, B16), "ONE": (128, B16),
+    "dg": (32, F32), "dg2": (32, F32), "ndg": (32, F32), "wr": (16, F32), "wp": (16, F32), "h16": (16, F32),
+    "h17": (16, F32), "zer": (16, F32),
+    "wD": (16, F32), "tD": (16, F32), "thM": (384, F32), "sm": (384, B16),
+    "kap": (192, F32), "K37": (192, F32), "thX": (96, F32), "dW": (12, F32), "dC": (12, F32), "t1": (24, I32),
+    "oE": (12, U16), "oN1": (24, U16), "oN2": (12, U16), "oD1": (24, U16), "oD2": (12, U16),
+    "a96": (96, F32), "b96": (96, F32), "a48": (48, F32), "a24": (24, F32), "k12": (12, I32),
+    "wi": (12, I32), "woff": (12, U16), "yw": (192, B16), "FS": (384, B16), "EW": (384, B16), "FS2": (384, B16),
+    "FW4": (768, B16), "ui": (12, I32), "u": (16, I32), "u2": (12, I32), "q": (16, I32), "q2": (16, I32),
+    "ku": (192, F32), "c1": (192, I32), "c2": (192, I32), "coff": (192, U16), "cfl": (192, F32),
+    "m1": (12, I32), "m2": (16, F32), "p1": (192, F32), "p2": (192, I32), "p3": (192, I32),
+    "flag": (192, B16), "nf": (384, B16), "nfD": (16, B16), "nfX": (192, B16),
+    "rr": (192, F16), "dd": (192, B16), "cn": (12, I32), "nlo": (24, U16), "nlf": (24, F32), "cno": (12, U16),
+    "R": (384, U16), "fail": (384, B16), "fsc": (384, B16), "nh": (12, F32), "y1": (12, F32), "y2": (12, F32),
+    "wX": (12, F32), "fd": (24, F32), "of": (24, F32), "so": (24, U16), "mx": (12, B16), "Acol": (1, F32),
+    "ajk": (12, F32), "C3": (576, B16), "ab": (384, B16), "bb": (384, B16), "sat": (384, B16), "inc": (384, B16),
+    "r12": (384, B16), "vv": (192, B16), "se": (192, B16), "FN": (384, B16), "EN1": (384, B16), "EN2": (384, B16),
+    "yfs": (64, F32),
+}
+PS = {"pa": 1024, "pb": 1024, "pk": 512, "pK": 512, "pT": 512, "pm": 512}
+HOME = {}
+SCRATCH = {}
+for _k, (_n, _d) in SB.items():
+    if _n > 48:
+        HOME[_k] = (_k, 0)
+        SCRATCH[_k] = ("sbuf", [128, _n], _d)
+    else:
+        _o = SCRATCH.get("n" + _d, (0, [128, 0]))[1][1]
+        HOME[_k] = ("n" + _d, _o)
+        SCRATCH["n" + _d] = ("sbuf", [128, _o + (_n + 15) // 16 * 16], _d)
+HOME.update({k: (k, 0) for k in PS})
+SCRATCH.update({k: ("psum", [128, v], F32) for k, v in PS.items()})
+DMAS = (["dn", "dz0", "dz1", "dz2", "dz3"] + ["da%d" % i for i in range(len(CH))] + ["db%d" % i for i in range(len(CH))]
+        + ["s0", "s1", "s3", "s4"])
+SEMAPHORES = ["eV", "eA", "eP", "eG", "arr1", "arr2", "sent"] + DMAS
+CFG = {
+    "A": ((1, 1, 1, 3), (1, 1, 3, 3), (1, 1, 3, 3)),
+    "C": 2,
+    "S2V": (1, 3),
+    "S1V": (),
+    "theta": 0.5,
+    "up": (0.0, 0.0, 0.0),
+    "early": {"cno": 4000.0, "flag": 3000.0},
+}
+EST = {"cyc": 1.04, "pe": 0.52, "ga": 1.56, "sc": 3.8, "wake": 80.0, "afix": 60.0, "pefix": 10.0, "pelat": 60.0,
+       "dfix": 1800.0, "dbw": 250.0, "remote": 3500.0}
+
+
+def r(name, a=0, b=None, s=1):
+    if b is None:
+        b = SB[name][0] if name in SB else PS[name]
+    return (name, a, b, s)
+
+
+def width(x):
+    return (x[1][2] - x[1][1]) * 16 if len(x) == 2 else len(range(x[1], x[2], x[3]))
+
+
+def narrow(x):
+    n = x[0][0] if len(x) == 2 else x[0]
+    return n in SB and SB[n][1] in (B16, U16, F16)
+
+
+def vcost(o, ins, two=False):
+    if len(o) == 2:
+        return 50 + width(o) * EST["sc"] * EST["cyc"]
+    if ins and len(ins[0]) == 2:
+        return 50 + width(o) * EST["ga"] * EST["cyc"]
+    h = all(narrow(x) for x in [o] + ins)
+    c = 0.5 if h else 1.0
+    if two:
+        c = 1.0 if (h or any(x[0] in PS for x in ins)) else 2.0
+    return max(64, width(ins[0] if ins else o) * c) * EST["cyc"]
+
+
+def build(T, g, core, topo):
+    rank = T.rank_of(core)
+    ops = []
+    up = [0.0]
+
+    def ap(x):
+        if len(x) == 2:
+            return ap(x[0]).indirect(ap(x[1]))
+        h, o = HOME[x[0]]
+        return T[h][:, o + x[1]:o + x[2]] if x[3] == 1 else T[h][:, o + x[1]:o + x[2]:x[3]]
+
+    def isref(x):
+        return isinstance(x, tuple)
+
+    def op(eng, fn, outs, ins, dur, sem=None, inc=1, lat=0.0):
+        w, rd = [], []
+        for o in outs:
+            if len(o) == 2:
+                w.append(o[0]); rd.append(o[1])
+            else:
+                w.append(o)
+        for i in ins:
+            if isref(i):
+                rd.extend(list(i) if len(i) == 2 else [i])
+        ops.append({"e": eng, "f": fn, "w": w, "r": rd, "sem": sem, "inc": inc, "dur": dur, "lat": lat, "up": up[0]})
+
+    def sc(x):
+        return ap(x) if isref(x) else x
+
+    def cp(o, i):
+        op("V", lambda: g.vector.tensor_copy(ap(o), ap(i)), [o], [i], vcost(o, [i]))
+
+    def tt(o, a, b, f):
+        op("V", lambda: g.vector.tensor_tensor(ap(o), ap(a), ap(b), f), [o], [a, b], vcost(o, [a, b], True))
+
+    def ts(o, a, s1, f1, s2=None, f2=None):
+        if f2 is None:
+            op("V", lambda: g.vector.tensor_scalar(ap(o), ap(a), sc(s1), None, f1), [o], [a, s1], vcost(o, [a]))
+        else:
+            op("V", lambda: g.vector.tensor_scalar(ap(o), ap(a), sc(s1), sc(s2), f1, f2), [o], [a, s1, s2], vcost(o, [a]))
+
+    def ms(o, c):
+        op("V", lambda: g.vector.memset(ap(o), c), [o], [], vcost(o, []))
+
+    def red(o, i):
+        op("V", lambda: g.vector.tensor_reduce(ap(o), ap(i), AX.X, ALU.add), [o], [i], 67.0)
+
+    def turn(o, i):
+        op("V", lambda: g.vector.transpose(ap(o), ap(i)), [o], [i], vcost(o, [i]))
+
+    def scan(o, d0, d1, ini, f0, f1):
+        op("V", lambda: g.vector.tensor_tensor_scan(ap(o), ap(d0), ap(d1), sc(ini), f0, f1), [o], [d0, d1, ini],
+           vcost(o, [d0, d1]))
+
+    def act(o, i, f=AF.Identity, bias=0.0, scale=1.0, acc=None):
+        d = EST["afix"] + width(i) * (EST["ga"] if len(i) == 2 else 1.0) * EST["cyc"]
+        if acc is None:
+            op("A", lambda: g.scalar.activation(ap(o), ap(i), f, bias=sc(bias), scale=sc(scale)), [o], [i, bias, scale], d)
+        else:
+            op("A", lambda: g.scalar.activation(ap(o), ap(i), f, bias=sc(bias), scale=sc(scale), accum_out=ap(acc)),
+               [o, acc], [i, bias, scale], d)
+
+    def mm(o, l, x, st, sp):
+        op("P", lambda: g.tensor.matmul(ap(o), ap(l), ap(x), st, sp), [o], [l, x],
+           EST["pefix"] + max(64, width(x)) * EST["pe"] * (1 if narrow(x) else 4), lat=EST["pelat"])
+
+    def lin(o, terms):
+        for k, (l, x) in enumerate(terms):
+            mm(o, r(l), x, k == 0, k == len(terms) - 1)
+
+    def iota(o, pat, base, cm):
+        d = 130 + 2 * width(o) * EST["cyc"]
+        if SB[o[0]][1] != I32:
+            op("G", lambda: g.iota(ap(o), pat, base, cm, allow_small_or_imprecise_dtypes=True), [o], [], d)
+        else:
+            op("G", lambda: g.iota(ap(o), pat, base, cm), [o], [], d)
+
+    def nbytes(x):
+        return 128 * width(x) * (2 if narrow(x) else 4)
+
+    def load(o, src, sem):
+        op("S", lambda: g.sync.dma_start(ap(o), src), [o], [], 60.0, sem, 16, nbytes(o))
+
+    def store(dst, i, sem):
+        op("S", lambda: g.sync.dma_start(dst, ap(i)), [], [i], 60.0, sem, 16, nbytes(i))
+
+    def seg(o, zname, x0, n, first, last):
+        for p in range(16):
+            mm(o, r(zname, 16 - p, 144 - p), r(x0[0], x0[1] + p, x0[1] + n, 16), first and p == 0, last and p == 15)
+
+    c0 = 0
+    for i, n in enumerate(CH):
+        load(r("E1", c0, c0 + n), T.pg[:, c0:c0 + n], "da%d" % i)
+        load(r("E2", c0, c0 + n), T.pg[:, NM + c0:NM + c0 + n], "db%d" % i)
+        if i == 1:
+            load(r("nmi"), T.nm[:], "dn")
+        c0 += n
+    for k in range(4):
+        load(r("z0", 192 * k, 192 * k + 192), T.zv[:], "dz%d" % k)
+
+    iota(r("r128"), [[1, 128]], 0, -1)
+    iota(r("ci", 0, 1), [[0, 1]], 0, 1)
+    iota(r("ramp"), [[1, 144]], -16, 0)
+    ts(r("cj", 0, 1), r("ci", 0, 1), 112, ALU.bitwise_and)
+    ts(r("cj", 1, 2), r("ci", 0, 1), 15, ALU.bitwise_and)
+    ts(r("cj", 2, 3), r("ci", 0, 1), 16, ALU.bitwise_and)
+    cp(r("cf", 0, 3), r("cj", 0, 3))
+    g16, p16, par = r("cf", 0, 1), r("cf", 1, 2), r("cf", 2, 3)
+    ts(r("I1"), r("r128"), 0.0, ALU.is_equal)
+    ts(r("I16"), r("r128"), 0.0, ALU.is_equal, 16.0, ALU.mult)
+    ts(r("In16"), r("r128"), 0.0, ALU.is_equal, -16.0, ALU.mult)
+    ts(r("I512"), r("r128"), 0.0, ALU.is_equal, 512.0, ALU.mult)
+    for nme in ("E1", "E2", "Y", "F", "S"):
+        ms(r(nme, NM, TW), 0.0)
+    ts(r("Z1"), r("ramp"), g16, ALU.is_equal)
+    act(r("Zn"), r("Z1"), scale=-4096.0)
+    act(r("Zp"), r("Z1"), scale=16.0)
+    act(r("In"), r("I1"), scale=-1.0)
+    act(r("If"), r("I1"))
+    act(r("In32"), r("I1"), scale=-32.0)
+    act(r("Ipen"), r("I1"), scale=float(2 ** 26))
+    act(r("Inf"), r("I1"), scale=float(2 ** 23))
+    iota(r("ct", 0, 24), [[16, 12], [0, 2]], 0, 0)
+    ts(r("oN1"), r("ct", 0, 24), p16, ALU.add)
+    iota(r("ct", 24, 36), [[16, 12]], 0, 0)
+    ts(r("ct", 36, 48), r("ct", 24, 36), p16, ALU.add)
+    ts(r("t1", 0, 12), r("ct", 36, 48), -5.5, ALU.add, 1.0 / 12.0, ALU.mult)
+    ts(r("ct", 48, 60), r("t1", 0, 12), -12.0, ALU.mult)
+    tt(r("ct", 60, 72), r("ct", 48, 60), r("ct", 36, 48), ALU.add)
+    cp(r("oE"), r("ct", 60, 72))
+    ts(r("ct", 72, 84), r("ct", 60, 72), 32.0, ALU.mult, par, ALU.add)
+    tt(r("ct", 84, 96), r("ct", 72, 84), r("t1", 0, 12), ALU.add)
+    cp(r("oN2"), r("ct", 84, 96))
+    ts(r("dW"), r("ct", 36, 48), float(NM), ALU.add)
+    ts(r("dC"), r("ct", 36, 48), float(NM + LN), ALU.add)
+    cp(r("nmf"), r("nmi"))
+    act(r("X1"), (r("nmf"), r("oN1")))
+    turn(r("X2"), r("X1"))
+    act(r("Lf0"), (r("X2"), r("oN2")))
+    cp(r("off0"), r("Lf0"))
+    for m in range(16):
+        iota(r("wr", m, m + 1), [[0, 1]], WT[m], 0)
+    iota(r("dg"), [[0, 2], [1, 16]], 0, 0)
+    for m in range(16):
+        iota(r("kap", 12 * m, 12 * m + 12), [[0, 12]], KA[m], 0)
+    iota(r("K37"), [[1184, 16], [0, 12]], 0, 0)
+    iota(r("cu"), [[0, 16], [256, 12]], 0, 0)
+    iota(r("thX"), [[0, 8], [16, 12]], 2 ** 19 + NM + LN, 0)
+    iota(r("sm"), [[0, 12], [1, 32]], 0, 0)
+    iota(r("cv", 0, 128), [[16, 8], [0, 16]], 0, 0)
+    iota(r("cv", 128, 152), [[1, 12], [0, 2]], 0, 0)
+    iota(r("cv", 152, 164), [[32, 12]], 0, 0)
+    iota(r("IO"), [[1, TW]], 0, 0)
+    iota(r("ONE"), [[0, 128]], 1, 0)
+    for nme in ("u", "q", "q2", "m2", "nfD", "zer"):
+        iota(r(nme), [[0, 16]], 0, 0)
+    ts(r("ndg"), r("dg"), p16, ALU.not_equal, HUGE, ALU.mult)
+    ts(r("dg2"), r("dg"), p16, ALU.is_equal)
+    tt(r("wr"), r("wr"), r("dg2", 0, 16), ALU.mult)
+    red(r("cf", 3, 4), r("wr"))
+    ts(r("Zw"), r("ramp"), g16, ALU.is_equal, r("cf", 3, 4), ALU.mult)
+    ms(r("h16"), 0.5)
+    scan(r("wp"), r("h16"), r("zer"), 2.0, ALU.mult, ALU.add)
+    tt(r("wp"), r("wp"), r("dg2", 0, 16), ALU.mult)
+    red(r("cf", 4, 5), r("wp"))
+    ts(r("cf", 5, 6), r("cf", 4, 5), float(2 ** 95), ALU.mult, 65536.0, ALU.mult)
+    ms(r("h17"), 1.0 / 65536.0)
+    scan(r("wD"), r("h17"), r("zer"), r("cf", 5, 6), ALU.mult, ALU.add)
+    ts(r("tD"), r("wD"), 2.5, ALU.mult)
+    ts(r("cf", 6, 7), p16, 16.0, ALU.mult)
+    ts(r("cf", 7, 8), p16, 12.0, ALU.mult)
+    tt(r("cf", 8, 9), p16, par, ALU.add)
+    ts(r("cu"), r("cu"), r("cf", 6, 7), ALU.add, 1184.0, ALU.mult)
+    tt(r("K37"), r("K37"), r("cu"), ALU.add)
+    ts(r("thX"), r("thX"), p16, ALU.add)
+    ts(r("sm"), r("sm"), 0.0, ALU.is_gt)
+    ts(r("BO"), r("cv", 0, 128), g16, ALU.is_equal)
+    ts(r("oD1"), r("cv", 128, 152), r("cf", 7, 8), ALU.add)
+    ts(r("oD2"), r("cv", 152, 164), r("cf", 8, 9), ALU.add)
+    for b in range(12):
+        act(r("thM", 32 * b, 32 * b + 32), r("ndg"), bias=r("tD", b, b + 1))
+
+    RB = 192.0 - 7.5 / 16.0
+    c0, hb = 0, 0
+    for i, n in enumerate(CH):
+        ts(r("F", c0, c0 + n), r("E1", c0, c0 + n), 1.0 / 16.0, ALU.mult, RB, ALU.add)
+        if i in CFG["S1V"]:
+            ts(r("S1", c0, c0 + n), r("E2", c0, c0 + n), 1.0 / 16.0, ALU.mult, RB, ALU.add)
+        else:
+            act(r("S1", c0, c0 + n), r("E2", c0, c0 + n), bias=RB, scale=1.0 / 16.0)
+        tt(r("sel", c0, c0 + n), r("F", c0, c0 + n), r("S1", c0, c0 + n), ALU.is_gt)
+        if i in CFG["S2V"]:
+            ts(r("S", c0, c0 + n), r("S1", c0, c0 + n), -FO, ALU.add)
+        else:
+            act(r("S", c0, c0 + n), r("S1", c0, c0 + n), bias=-FO)
+        for a in range(c0, c0 + n, 512):
+            h = 512 * (hb % 2); hb += 1
+            lin(r("pa", h, h + 512), [("I1", r("E1", a, a + 512)), ("In16", r("F", a, a + 512)), ("In16", r("sel", a, a + 512))])
+            lin(r("pb", h, h + 512), [("I1", r("E2", a, a + 512)), ("In16", r("S", a, a + 512)), ("I16", r("sel", a, a + 512))])
+            act(r("At", a, a + 512), r("pa", h, h + 512), bias=16.0 + 16.0 * FO)
+            tt(r("Y", a, a + 512), r("pb", h, h + 512), r("At", a, a + 512), ALU.max)
+        c0 += n
+
+    def tree(src, o, extra):
+        if extra is None:
+            cp(r("a96"), r(src, 96, 192))
+        else:
+            tt(r("a96"), r(src, 96, 192), extra, ALU.min)
+        tt(r("b96"), r(src, 0, 96), r("a96"), ALU.min)
+        tt(r("a48"), r("b96", 0, 48), r("b96", 48, 96), ALU.min)
+        tt(r("a24"), r("a48", 0, 24), r("a48", 24, 48), ALU.min)
+        tt(o, r("a24", 0, 12), r("a24", 12, 24), ALU.min)
+
+    def of(nme, k):
+        return r(nme, 48 * k, 48 * k + 48)
+
+    def gs(k):
+        return r("GB", 768 * k, 768 * k + 768)
+
+    def gf(k):
+        return r("GB", 3072 + 768 * k, 3072 + 768 * k + 768)
+
+    for t in range(3):
+        last = t == 2
+        off, Lf, z = "off%d" % t, "Lf%d" % t, "z%d" % t
+        flagv = LIMS[t] - 12 - 1.0 / 128.0
+        if t > 0:
+            op("X", None, [r(off), r(Lf), r(z)], [], 0.0, "arr%d" % t, 14)
+        n3 = 0
+        for k in range(4):
+            if CFG["A"][t][k] == 1:
+                tt(gs(k), (r("Y"), of(off, k)), r(z), ALU.subtract)
+                act(gs(k), gs(k), AF.Abs, bias=-YO)
+            else:
+                pbuf = ("pa", "pb")[n3 % 2]; n3 += 1
+                act(gs(k), (r("Y"), of(off, k)))
+                for a, b in ((0, 512), (512, 768)):
+                    lin(r(pbuf, a, b), [("In", r(z, a, b)), ("I1", r("GB", 768 * k + a, 768 * k + b))])
+                act(gs(k), r(pbuf, 0, 768), AF.Abs, bias=-YO)
+            mm(r("pk", 48 * k, 48 * k + 48), r("If"), of(Lf, k), True, False)
+            seg(r("pk", 48 * k, 48 * k + 48), "Zn", ("GB", 768 * k), 768, False, True)
+        tree("pk", r("k12"), None)
+        ts(r("wi"), r("k12"), 4095, ALU.bitwise_and)
+        cp(r("woff"), r("wi"))
+        W = r("woff")
+        cp(r("yw"), (r("Y"), W))
+        act(r("FS", 0, 192), (r("F"), W), bias=-FO)
+        act(r("FS", 192, 384), (r("S"), W))
+        seg(r("pT", 0, 12), "Zw", ("yw", 0), 192, True, True)
+        lin(r("pm", 0, 192), [("In", r(z, 0, 192)), ("I1", r("yw"))])
+        cp(r("nlo", 0, 24, 2), r("wi"))
+        cp(r("nlf", 0, 24, 2), r("wi"))
+        ts(r("ui"), r("pT", 0, 12), -YO * sum(WT), ALU.add)
+        ts(r("u", 0, 12), r("ui"), 4095, ALU.bitwise_and)
+        ts(r("FS2", 0, 192), r("FS", 0, 192), flagv, ALU.min)
+        ts(r("FS2", 192, 384), r("FS", 192, 384), flagv, ALU.min)
+        tt(r("u2"), r("u", 0, 12), r("u", 0, 12), ALU.mult)
+        tt(r("ku"), (r("u"), r("oE")), r("kap"), ALU.mult)
+        ts(r("q", 0, 12), r("u2"), 5, ALU.arith_shift_right)
+        qn = "q"
+        if t > 0:
+            ts(r("q2", 0, 12), r("q", 0, 12), r("Acol"), ALU.add)
+            qn = "q2"
+        tt(r("c1"), (r(qn), r("oE")), r("ku"), ALU.add)
+        ts(r("c2"), r("c1"), 4095, ALU.bitwise_and)
+        cp(r("coff"), r("c2"))
+        act(r("sz%d" % t), r("pm", 0, 192), AF.Abs, bias=-YO)
+        for pbuf, s0 in (("pa", 0), ("pb", 192)):
+            for a, b, s in ((0, 192, 0), (192, 384, 0), (384, 512, 0), (512, 576, 128), (576, 768, 0)):
+                mm(r(pbuf, a, b), r("I1"), r("FS2", s0 + s, s0 + s + b - a), True, True)
+        act(r("FW4"), r("pa", 0, 768))
+        lin(r("pm", 0, 192), [("I1", r("FS2", 0, 192)), ("I1", r("FS2", 192, 384))])
+        act(r("flag"), r("pm", 0, 192), AF.Relu, bias=0.5 - 2 * flagv)
+        mm(r("pm", 0, 192), r("BO"), r("flag"), True, True)
+        mm(r("pm", 192, 384), r("BO"), r("flag"), True, True)
+        seg(r("pT", 0, 12), "Z1", ("flag", 0), 192, True, True)
+        act(r("nfD", 0, 12), r("pT", 0, 12), AF.Relu, bias=1.0, scale=-4.0)
+        act(r("nfX"), (r("nfD"), r("oE")))
+        act(r("nf"), r("pm", 0, 384), AF.Relu, bias=1.0, scale=-4.0)
+        cp(r("cfl"), r("c2"))
+        mm(r("pK", 0, 192), r("If"), r("cfl"), True, False)
+        mm(r("pK", 0, 192), r("Inf"), r("nfX"), False, False)
+        ts(r("m1"), r("u", 0, 12), 1023, ALU.bitwise_and)
+        ts(r("m2", 0, 12), r("m1"), 2.0, ALU.mult, 33.0, ALU.add)
+        tt(r("p1"), (r("m2"), r("oE")), r(Lf), ALU.mult)
+        tt(r("p2"), r("p1"), r("K37"), ALU.add)
+        ts(r("p3"), r("p2"), 5, ALU.arith_shift_right, 4095, ALU.bitwise_and)
+        cp(r("sl%d" % t), r("p3"))
+        if not last:
+            cp(r("so%d" % t), r("p3"))
+            dst = T.cores[(rank + STEP) % N]
+            rid, pid, _s = topo.addr(dst)
+            en = topo.engines(core, dst)
+            prs = [(r("so%d" % t), r("off%d" % (t + 1))), (r("sl%d" % t, 0, 96), r("Lf%d" % (t + 1), 0, 96)),
+                   (r("sl%d" % t, 96, 192), r("Lf%d" % (t + 1), 96, 192))]
+            prs += [(r("sz%d" % t), r("z%d" % (t + 1), 192 * k, 192 * k + 192)) for k in range(4)]
+
+            def send(prs=prs, rid=rid, pid=pid, en=en, t=t):
+                tr = [RemoteDMATransfer(dst_ids=[DstId(rid=rid, pnc=pid)],
+                                        dma_engine_mask=(1 << en[2 * k]) | (1 << en[2 * k + 1]),
+                                        remote_sem=T.sem["arr%d" % (t + 1)], src=ap(a), dst=ap(b))
+                      for k, (a, b) in enumerate(prs)]
+                g.remote_dma_fused(tr, local_sem=T.sem.sent)
+            op("R", send, [], [a for a, b in prs], 500.0, "sent", 14, EST["remote"])
+        else:
+            store(T.yz[:], r("sz2"), "s0")
+            act(r("X1"), (r("sl2"), r("oD1")))
+            turn(r("X2"), r("X1"))
+            act(r("ynf"), (r("X2"), r("oD2")))
+            store(T.yn[:], r("ynf"), "s3")
+        for k in range(4):
+            if k < CFG["C"]:
+                tt(gs(k), (r("S"), of("coff", k)), r("FW4"), ALU.min)
+            else:
+                act(gs(k), (r("S"), of("coff", k)))
+                tt(gs(k), gs(k), r("pa", 0, 768), ALU.min)
+            act(gf(k), (r("F"), of("coff", k)), bias=-FO)
+            tt(gf(k), gf(k), r("pb", 0, 768), ALU.min)
+        seg(r("pk", 0, 96), "Zp", ("GB", 0), 1536, True, False)
+        seg(r("pk", 0, 96), "Zp", ("GB", 3072), 1536, False, True)
+        for k in (2, 3):
+            seg(of("pk", k), "Zp", ("GB", 768 * k), 768, True, False)
+            seg(of("pk", k), "Zp", ("GB", 3072 + 768 * k), 768, False, True)
+        MG = 1.5 * 2 ** 27
+        ts(r("rr"), r("pk", 0, 192), MG, ALU.add, -MG, ALU.add)
+        tt(r("dd"), r("rr"), r("pk", 0, 192), ALU.subtract)
+        mm(r("pK", 0, 192), r("I512"), r("rr"), False, False)
+        mm(r("pK", 0, 192), r("Ipen"), r("dd"), False, True)
+        tree("pK", r("k12"), r("thX"))
+        ts(r("cn"), r("k12"), 8191, ALU.bitwise_and)
+        cp(r("nlo", 1, 24, 2), r("cn"))
+        cp(r("nlf", 1, 24, 2), r("cn"))
+        cp(r("R"), (r("IO"), r("nlo")))
+        cp(r("cno"), r("cn"))
+        nf1, fw, sw, z1 = r("nf", 0, 192), r("FS", 0, 192), r("FS", 192, 384), r(z, 0, 192)
+        act(r("EW", 0, 192), (r("E1"), W))
+        act(r("EW", 192, 384), (r("E2"), W))
+        lin(r("pm", 0, 192), [("I1", z1), ("I16", nf1)])
+        lin(r("pm", 192, 384), [("I1", r("yw")), ("In16", nf1)])
+        act(r("r12", 0, 192), r("pm", 0, 192), AF.Relu, bias=-16.0)
+        act(r("r12", 192, 384), r("pm", 192, 384), AF.Relu, bias=-YO)
+        lin(r("pm", 0, 192), [("I1", r("r12", 0, 192)), ("I1", r("r12", 192, 384))])
+        act(r("vv"), r("pm", 0, 192), bias=YO)
+        lin(r("pa", 0, 384), [("In16", r("FS")), ("In", r(z, 0, 384)), ("I1", r("EW"))])
+        act(r("ab"), r("pa", 0, 384), AF.Abs, bias=-192.0)
+        act(r("sat"), r("FS"), AF.Relu, bias=-2.0)
+        act(r("bb"), r("ab"), AF.Relu, bias=1.0, scale=-1.0)
+        C = r("cno")
+        yc, fc, scn = r("C3", 0, 192), r("C3", 192, 384), r("C3", 384, 576)
+        act(scn, (r("S"), C))
+        act(yc, (r("Y"), C))
+        act(fc, (r("F"), C), bias=-FO)
+        lin(r("pa", 512, 896), [("I1", r("nf")), ("In", r("sat")), ("In", r("bb"))])
+        act(r("inc"), r("pa", 512, 896), AF.Relu)
+        lin(r("pb", 0, 192), [("In", sw), ("In32", nf1), ("I1", scn)])
+        act(r("se"), r("pb", 0, 192), AF.Relu, bias=16.0)
+        lin(r("pb", 512, 704), [("I1", sw), ("I16", nf1), ("I1", r("inc", 192, 384)), ("I1", r("se"))])
+        act(r("FN", 192, 384), r("pb", 512, 704), bias=-16.0)
+        if not last:
+            lin(r("pa", 0, 192), [("I1", fw), ("I1", r("inc", 0, 192))])
+            act(r("FN", 0, 192), r("pa", 0, 192), bias=FO)
+        lin(r("pb", 192, 384), [("I16", sw), ("I1", yc)])
+        lin(r("pb", 0, 192), [("I1", r("vv")), ("I16", r("FN", 192, 384))])
+        up[0] = CFG["up"][t]
+        act(r("EN2"), r("pb", 0, 384), bias=-16.0)
+        up[0] = 0.0
+        lin(r("pa", 704, 896), [("I16", fc), ("I1", yc)])
+        lin(r("pa", 512, 704), [("I16", fw), ("I1", r("vv")), ("I16", r("inc", 0, 192))])
+        act(r("EN1"), r("pa", 512, 896), bias=-16.0)
+        e0 = 0
+        for b in range(12):
+            n = 384 - 32 * b
+            for k in range(2):
+                ts(r("EQ", e0, e0 + n), r("R", 32 * b, 384), r("nlf", 2 * b + k, 2 * b + k + 1), ALU.is_equal,
+                   r("wD", b, b + 1), ALU.mult)
+                mm(r("pT", 32 * b, 384), r("BO"), r("EQ", e0, e0 + n), b == 0 and k == 0, b == 11 and k == 1)
+                e0 += n
+        ts(r("nh"), r("cn"), float(NM), ALU.is_ge)
+        tt(r("y1"), r("nh"), r("nfD", 0, 12), ALU.subtract)
+        tt(r("y2"), r("y1"), r("dW"), ALU.mult)
+        tt(r("wX"), r("y2"), r("nlf", 0, 24, 2), ALU.max)
+        tt(r("fail"), r("pT", 0, 384), r("thM"), ALU.is_ge)
+        scan(r("fsc"), r("sm"), r("fail"), 0.0, ALU.mult, ALU.max)
+        fD = r("fsc", 31, 384, 32)
+        sw_, sc_ = r("so", 0, 12), r("so", 12, 24)
+        tt(r("fd", 0, 12), fD, r("dW"), ALU.mult)
+        tt(r("of", 0, 12), r("fd", 0, 12), r("wX"), ALU.max)
+        cp(sw_, r("of", 0, 12))
+        tt(r("fd", 12, 24), fD, r("dC"), ALU.mult)
+        tt(r("of", 12, 24), r("fd", 12, 24), r("nlf", 1, 24, 2), ALU.max)
+        cp(sc_, r("of", 12, 24))
+        if not last:
+            cp((r("Y"), sw_), r("vv"))
+            cp((r("F"), sw_), r("FN", 0, 192))
+            cp((r("S"), sw_), r("FN", 192, 384))
+            cp((r("S"), sc_), sw)
+            tt(r("mx"), fD, r("nh"), ALU.max)
+            mm(r("pm", 0, 12), r("ONE"), r("mx"), True, True)
+            act(r("ajk"), r("pm", 0, 12), bias=128.0, scale=-1.0, acc=r("Acol"))
+        cp((r("E2"), sw_), r("EN2", 0, 192))
+        cp((r("E2"), sc_), r("EN2", 192, 384))
+        if last:
+            store(T.ys[:], r("E2", 0, NM), "s1")
+        cp((r("E1"), sw_), r("EN1", 0, 192))
+        cp((r("E1"), sc_), r("EN1", 192, 384))
+        if last:
+            for j in range(64):
+                mm(r("pm", 0, 64), r("I1"), r("E1", 64 * j, 64 * j + 64), j == 0, j == 63)
+            cp(r("yfs"), r("pm", 0, 64))
+            store(T.yf[:], r("yfs"), "s4")
+    return ops
+
+
+def overlap(x, y):
+    if x[0] in PS:
+        return x[1] // 512 <= (y[2] - 1) // 512 and y[1] // 512 <= (x[2] - 1) // 512
+    return x[1] < y[2] and y[1] < x[2]
+
+
+QN = {"V": "V", "A": "A", "P": "P", "G": "G", "R": "G", "S": "S", "X": "X"}
+PLAN = {}
+
+
+def plan(ops):
+    n = len(ops)
+    hist, deps, soft = {}, [], []
+    lastr, lasts = None, None
+    for i, o in enumerate(ops):
+        d, s = set(), set()
+        for x in o["r"]:
+            for j, y, wr in hist.get(x[0], []):
+                if overlap(x, y) and (wr or (x[0] in PS and ops[j]["e"] != o["e"])):
+                    d.add(j)
+        for x in o["w"]:
+            for j, y, wr in hist.get(x[0], []):
+                if overlap(x, y):
+                    (s if o["e"] == "P" and ops[j]["e"] == "P" else d).add(j)
+        for x in o["w"]:
+            if x[3] == 1:
+                hist[x[0]] = [h for h in hist.get(x[0], []) if not (
+                    (x[1] <= h[1][1] and h[1][2] <= x[2]) and x[0] not in PS)]
+            if x[0] in PS:
+                hist[x[0]] = [h for h in hist.get(x[0], []) if not (
+                    x[1] // 512 <= h[1][1] // 512 and (h[1][2] - 1) // 512 <= (x[2] - 1) // 512
+                    and (ops[h[0]]["e"] == "P" or h[0] in d))]
+        for x in o["r"]:
+            hist.setdefault(x[0], []).append((i, x, False))
+        for x in o["w"]:
+            hist.setdefault(x[0], []).append((i, x, True))
+        if o["e"] == "X":
+            s.add(lastr)
+        if o["e"] == "R":
+            lastr = i
+        if o["e"] == "S" and o["w"]:
+            if lasts is not None:
+                s.add(lasts)
+            lasts = i
+        d.discard(i); s.discard(i)
+        deps.append(d); soft.append(s - d)
+    succ = [[] for _ in range(n)]
+    for i in range(n):
+        for j in deps[i] | soft[i]:
+            succ[j].append(i)
+
+    def tail(o):
+        return EST["dfix"] + o["lat"] / EST["dbw"] if o["e"] == "S" else o["lat"]
+    prio = [0.0] * n
+    for i in range(n - 1, -1, -1):
+        o = ops[i]
+        m = tail(o)
+        for k in succ[i]:
+            m = max(m, prio[k] + ((tail(o) + EST["wake"]) if (i in deps[k] or ops[k]["e"] == "X") else 0.0))
+        prio[i] = o["dur"] + m + o["up"] + (CFG["early"].get(o["w"][0][0], 0.0) if o["w"] else 0.0)
+    left = [len(deps[i] | soft[i]) for i in range(n)]
+    ready = [0.0] * n
+    cand = {q: [] for q in "VAPGSX"}
+    for i in range(n):
+        if left[i] == 0:
+            cand[QN[ops[i]["e"]]].append(i)
+    free = {q: 0.0 for q in cand}
+    dfree = 0.0
+    order = []
+    while len(order) < n:
+        best = None
+        for q, l in cand.items():
+            if l:
+                tq = max(free[q], min(ready[i] for i in l))
+                if best is None or tq < best[0]:
+                    best = (tq, q)
+        tq, q = best
+        l = cand[q]
+        c = max((i for i in l if ready[i] <= tq), key=lambda i: prio[i])
+        hs = [i for i in l if ready[i] > tq and prio[i] > prio[c] and tq + ops[c]["dur"] - ready[i] > CFG["theta"] * ops[c]["dur"]]
+        if hs:
+            th = min(ready[i] for i in hs)
+            fit = [i for i in l if ready[i] <= tq and tq + ops[i]["dur"] * (1 - CFG["theta"]) <= th]
+            if not fit:
+                free[q] = th
+                continue
+            c = max(fit, key=lambda i: prio[i])
+        l.remove(c)
+        o = ops[c]
+        free[q] = tq + o["dur"]
+        if o["e"] == "S":
+            dfree = max(dfree, free[q] + 0.6 * EST["dfix"]) + o["lat"] / EST["dbw"]
+            end = dfree + 0.4 * EST["dfix"]
+        else:
+            end = free[q] + o["lat"]
+        order.append(c)
+        for k in succ[c]:
+            if c in deps[k]:
+                ready[k] = max(ready[k], end + (0.0 if o["e"] == "X" else EST["wake"]))
+            elif ops[k]["e"] == "X":
+                ready[k] = max(ready[k], end)
+            left[k] -= 1
+            if left[k] == 0:
+                cand[QN[ops[k]["e"]]].append(k)
+    return deps, order
+
+
+def emit(ops, g, T):
+    if "p" not in PLAN:
+        PLAN["p"] = plan(ops)
+    deps, order = PLAN["p"]
+    queue = {"V": g.vector, "A": g.scalar, "P": g.tensor, "G": g, "R": g, "S": g.sync}
+    clock = {q: {} for q in "VAPGS"}
+    seq, at = {}, {}
+    for a, i in enumerate(order):
+        o = ops[i]
+        at[i] = a
+        key = o["sem"] or "e" + o["e"]
+        seq[key] = seq.get(key, 0) + 1
+        o["key"], o["pos"], o["need"], o["waits"] = key, seq[key], False, []
+        if o["e"] == "X":
+            o["clk"] = {key: o["pos"]}
+            continue
+        ck = clock[QN[o["e"]]]
+        for j in sorted(deps[i], key=lambda j: -at[j]):
+            d = ops[j]
+            if ck.get(d["key"], 0) >= d["pos"]:
+                continue
+            d["need"] = True
+            o["waits"].append(j)
+            for k, v in d["clk"].items():
+                if ck.get(k, 0) < v:
+                    ck[k] = v
+        o["clk"] = dict(ck)
+        o["clk"][key] = o["pos"]
+    total = {}
+    for i in order:
+        o = ops[i]
+        if o["sem"] or o["need"]:
+            total[o["key"]] = total.get(o["key"], 0) + o["inc"]
+            o["val"] = total[o["key"]]
+    seen = {}
+    for i in order:
+        o = ops[i]
+        if o["e"] == "X":
+            continue
+        q = queue[o["e"]]
+        for j in o["waits"]:
+            d = ops[j]
+            q.wait_ge(T.sem[d["key"]], d["val"])
+            seen[d["key"]] = max(seen.get(d["key"], 0), d["val"])
+        ins = o["f"]()
+        if o["e"] != "R" and (o["sem"] or o["need"]):
+            ins.then_inc(T.sem[o["key"]], o["inc"])
+    for k, v in total.items():
+        if seen.get(k, 0) < v:
+            g.sync.wait_ge(T.sem[k], v)
+
+
+def rank_program(g, core, T, topo):
+    if T.rank_of(core) is None:
+        return
+    emit(build(T, g, core, topo), g, T)

@@ -9,7 +9,7 @@ TW = NM + 2 * LN
 YO = 208.0
 FO = 204.0
 CH = (512, 512, 1024, 1024, 1024)
-HUGE = float(2 ** 98)
+HUGE = float(2 ** 99)
 
 B16, F32, I32, U16, F16 = "bfloat16", "float32", "int32", "uint16", "float16"
 SB = {
@@ -28,17 +28,17 @@ SB = {
     "Ipen": (128, B16), "Inf": (128, B16), "I512": (128, F16), "If": (128, F32), "BO": (128, B16), "ONE": (128, B16),
     "dg": (32, F32), "dg2": (32, F32), "ndg": (32, F32), "wr": (16, F32), "wp": (16, F32), "h16": (16, F32),
     "h17": (16, F32), "zer": (16, F32),
-    "wD": (16, F32), "tD": (16, F32), "thM": (384, F32), "sm": (384, B16),
+    "wD": (16, F32), "tD": (16, F32), "thM": (192, F32), "sm": (192, B16), "zz": (192, B16),
     "kap": (192, F32), "K37": (192, F32), "thX": (96, F32), "dW": (12, F32), "dC": (12, F32), "t1": (24, I32),
     "oE": (12, U16), "oN1": (24, U16), "oN2": (12, U16), "oD1": (24, U16), "oD2": (12, U16),
     "a96": (96, F32), "b96": (96, F32), "a48": (48, F32), "a24": (24, F32), "k12": (12, I32),
     "wi": (12, I32), "woff": (12, U16), "yw": (192, B16), "FS": (384, B16), "EW": (384, B16), "FS2": (384, B16),
     "FW4": (768, B16), "ui": (12, I32), "u": (16, I32), "u2": (12, I32), "q": (16, I32), "q2": (16, I32),
-    "ku": (192, F32), "c1": (192, I32), "c2": (192, I32), "coff": (192, U16), "cfl": (192, F32),
+    "ku": (192, F32), "ku2": (192, F32), "c1": (192, I32), "c2": (192, I32), "coff": (192, U16), "cfl": (192, F32),
     "m1": (12, I32), "m2": (16, F32), "p1": (192, F32), "p2": (192, I32), "p3": (192, I32),
     "flag": (192, B16), "nf": (384, B16), "nfD": (16, B16), "nfX": (192, B16),
     "rr": (192, F16), "dd": (192, B16), "cn": (12, I32), "nlo": (24, U16), "nlf": (24, F32), "cno": (12, U16),
-    "R": (384, U16), "fail": (384, B16), "fsc": (384, B16), "nh": (12, F32), "y1": (12, F32), "y2": (12, F32),
+    "R": (384, U16), "fail": (192, B16), "fsc": (192, B16), "nh": (12, F32), "y1": (12, F32), "y2": (12, F32),
     "wX": (12, F32), "fd": (24, F32), "of": (24, F32), "so": (24, U16), "mx": (12, B16), "Acol": (1, F32),
     "ajk": (12, F32), "C3": (576, B16), "ab": (384, B16), "bb": (384, B16), "sat": (384, B16), "inc": (384, B16),
     "r12": (384, B16), "vv": (192, B16), "se": (192, B16), "FN": (384, B16), "EN1": (384, B16), "EN2": (384, B16),
@@ -62,14 +62,20 @@ DMAS = (["dn", "dz0", "dz1", "dz2", "dz3"] + ["da%d" % i for i in range(len(CH))
 SEMAPHORES = ["eV", "eA", "eP", "eG", "arr1", "arr2", "sent"] + DMAS
 CFG = {
     "A": ((1, 1, 1, 3), (1, 1, 3, 3), (1, 1, 3, 3)),
-    "C": 2,
+    "C": 3,
     "S2V": (1, 3),
     "S1V": (),
-    "theta": 0.5,
+    "theta": 0.4,
+    "Aord": ((0, 3, 1, 2), (0, 1, 2, 3), (0, 1, 2, 3)),
+    "Cord": ((0, 2), (4, 2), (2, 1), (6, 1), (7, 1), (3, 1)),
+    "reduce": True,
+    "csplit": ((0, 96), (96, 192)),
+    "pe": 4, "pf": 12,
+    "inorder": False,
     "up": (0.0, 0.0, 0.0),
-    "early": {"cno": 4000.0, "flag": 3000.0},
+    "early": {"flag": 3000.0},
 }
-EST = {"cyc": 1.04, "pe": 0.52, "ga": 1.56, "sc": 3.8, "wake": 80.0, "afix": 60.0, "pefix": 10.0, "pelat": 60.0,
+EST = {"cyc": 0.9, "pe": 0.45, "ga": 1.56, "sc": 3.8, "wake": 210.0, "afix": 60.0, "pefix": 10.0, "pelat": 60.0,
        "dfix": 1800.0, "dbw": 250.0, "remote": 3500.0}
 
 
@@ -248,7 +254,8 @@ def build(T, g, core, topo):
     iota(r("K37"), [[1184, 16], [0, 12]], 0, 0)
     iota(r("cu"), [[0, 16], [256, 12]], 0, 0)
     iota(r("thX"), [[0, 8], [16, 12]], 2 ** 19 + NM + LN, 0)
-    iota(r("sm"), [[0, 12], [1, 32]], 0, 0)
+    iota(r("sm"), [[0, 12], [1, 16]], 0, 0)
+    iota(r("zz"), [[0, 192]], 0, 0)
     iota(r("cv", 0, 128), [[16, 8], [0, 16]], 0, 0)
     iota(r("cv", 128, 152), [[1, 12], [0, 2]], 0, 0)
     iota(r("cv", 152, 164), [[32, 12]], 0, 0)
@@ -268,7 +275,7 @@ def build(T, g, core, topo):
     ts(r("cf", 5, 6), r("cf", 4, 5), float(2 ** 95), ALU.mult, 65536.0, ALU.mult)
     ms(r("h17"), 1.0 / 65536.0)
     scan(r("wD"), r("h17"), r("zer"), r("cf", 5, 6), ALU.mult, ALU.add)
-    ts(r("tD"), r("wD"), 2.5, ALU.mult)
+    ts(r("tD"), r("wD"), 4.0, ALU.mult)
     ts(r("cf", 6, 7), p16, 16.0, ALU.mult)
     ts(r("cf", 7, 8), p16, 12.0, ALU.mult)
     tt(r("cf", 8, 9), p16, par, ALU.add)
@@ -280,7 +287,7 @@ def build(T, g, core, topo):
     ts(r("oD1"), r("cv", 128, 152), r("cf", 7, 8), ALU.add)
     ts(r("oD2"), r("cv", 152, 164), r("cf", 8, 9), ALU.add)
     for b in range(12):
-        act(r("thM", 32 * b, 32 * b + 32), r("ndg"), bias=r("tD", b, b + 1))
+        act(r("thM", 16 * b, 16 * b + 16), r("ndg", 0, 16), bias=r("tD", b, b + 1))
 
     RB = 192.0 - 7.5 / 16.0
     c0, hb = 0, 0
@@ -304,6 +311,12 @@ def build(T, g, core, topo):
         c0 += n
 
     def tree(src, o, extra):
+        if CFG["reduce"]:
+            hi = 192 if extra is None else 204
+            for b in range(12):
+                oo, ii = r(o[0], b, b + 1), r(src, b, hi, 12)
+                op("V", lambda oo=oo, ii=ii: g.vector.tensor_reduce(ap(oo), ap(ii), AX.X, ALU.min), [oo], [ii], 64 * EST["cyc"])
+            return
         if extra is None:
             cp(r("a96"), r(src, 96, 192))
         else:
@@ -312,6 +325,10 @@ def build(T, g, core, topo):
         tt(r("a48"), r("b96", 0, 48), r("b96", 48, 96), ALU.min)
         tt(r("a24"), r("a48", 0, 24), r("a48", 24, 48), ALU.min)
         tt(o, r("a24", 0, 12), r("a24", 12, 24), ALU.min)
+
+    def scat(tab, o0, src, s0, step):
+        for a in range(0, 12, step):
+            cp((r(tab), r("so", o0 + a, o0 + a + step)), r(src, s0 + 16 * a, s0 + 16 * (a + step)))
 
     def of(nme, k):
         return r(nme, 48 * k, 48 * k + 48)
@@ -339,8 +356,9 @@ def build(T, g, core, topo):
                 for a, b in ((0, 512), (512, 768)):
                     lin(r(pbuf, a, b), [("In", r(z, a, b)), ("I1", r("GB", 768 * k + a, 768 * k + b))])
                 act(gs(k), r(pbuf, 0, 768), AF.Abs, bias=-YO)
-            mm(r("pk", 48 * k, 48 * k + 48), r("If"), of(Lf, k), True, False)
-            seg(r("pk", 48 * k, 48 * k + 48), "Zn", ("GB", 768 * k), 768, False, True)
+        mm(r("pk", 0, 192), r("If"), r(Lf), True, False)
+        for i, k in enumerate(CFG["Aord"][t]):
+            seg(r("pk", 48 * k, 48 * k + 48), "Zn", ("GB", 768 * k), 768, False, i == 3)
         tree("pk", r("k12"), None)
         ts(r("wi"), r("k12"), 4095, ALU.bitwise_and)
         cp(r("woff"), r("wi"))
@@ -350,8 +368,8 @@ def build(T, g, core, topo):
         act(r("FS", 192, 384), (r("S"), W))
         seg(r("pT", 0, 12), "Zw", ("yw", 0), 192, True, True)
         lin(r("pm", 0, 192), [("In", r(z, 0, 192)), ("I1", r("yw"))])
-        cp(r("nlo", 0, 24, 2), r("wi"))
-        cp(r("nlf", 0, 24, 2), r("wi"))
+        cp(r("nlf", 0, 12), r("wi"))
+        cp(r("R", 0, 192), (r("IO"), W))
         ts(r("ui"), r("pT", 0, 12), -YO * sum(WT), ALU.add)
         ts(r("u", 0, 12), r("ui"), 4095, ALU.bitwise_and)
         ts(r("FS2", 0, 192), r("FS", 0, 192), flagv, ALU.min)
@@ -359,13 +377,14 @@ def build(T, g, core, topo):
         tt(r("u2"), r("u", 0, 12), r("u", 0, 12), ALU.mult)
         tt(r("ku"), (r("u"), r("oE")), r("kap"), ALU.mult)
         ts(r("q", 0, 12), r("u2"), 5, ALU.arith_shift_right)
-        qn = "q"
+        kn = "ku"
         if t > 0:
-            ts(r("q2", 0, 12), r("q", 0, 12), r("Acol"), ALU.add)
-            qn = "q2"
-        tt(r("c1"), (r(qn), r("oE")), r("ku"), ALU.add)
-        ts(r("c2"), r("c1"), 4095, ALU.bitwise_and)
-        cp(r("coff"), r("c2"))
+            ts(r("ku2"), r("ku"), r("Acol"), ALU.add)
+            kn = "ku2"
+        for a, b in CFG["csplit"]:
+            tt(r("c1", a, b), (r("q"), r("oE", a // 16, b // 16)), r(kn, a, b), ALU.add)
+            ts(r("c2", a, b), r("c1", a, b), 4095, ALU.bitwise_and)
+            cp(r("coff", a, b), r("c2", a, b))
         act(r("sz%d" % t), r("pm", 0, 192), AF.Abs, bias=-YO)
         for pbuf, s0 in (("pa", 0), ("pb", 192)):
             for a, b, s in ((0, 192, 0), (192, 384, 0), (384, 512, 0), (512, 576, 128), (576, 768, 0)):
@@ -375,11 +394,13 @@ def build(T, g, core, topo):
         act(r("flag"), r("pm", 0, 192), AF.Relu, bias=0.5 - 2 * flagv)
         mm(r("pm", 0, 192), r("BO"), r("flag"), True, True)
         mm(r("pm", 192, 384), r("BO"), r("flag"), True, True)
-        seg(r("pT", 0, 12), "Z1", ("flag", 0), 192, True, True)
-        act(r("nfD", 0, 12), r("pT", 0, 12), AF.Relu, bias=1.0, scale=-4.0)
+        seg(r("pm", 384, 396), "Z1", ("flag", 0), 192, True, True)
+        act(r("nfD", 0, 12), r("pm", 384, 396), AF.Relu, bias=1.0, scale=-4.0)
         act(r("nfX"), (r("nfD"), r("oE")))
         act(r("nf"), r("pm", 0, 384), AF.Relu, bias=1.0, scale=-4.0)
         cp(r("cfl"), r("c2"))
+        if CFG["reduce"]:
+            mm(r("pK", 192, 204), r("If"), r("thX", 0, 12), True, True)
         mm(r("pK", 0, 192), r("If"), r("cfl"), True, False)
         mm(r("pK", 0, 192), r("Inf"), r("nfX"), False, False)
         ts(r("m1"), r("u", 0, 12), 1023, ALU.bitwise_and)
@@ -418,11 +439,9 @@ def build(T, g, core, topo):
                 tt(gs(k), gs(k), r("pa", 0, 768), ALU.min)
             act(gf(k), (r("F"), of("coff", k)), bias=-FO)
             tt(gf(k), gf(k), r("pb", 0, 768), ALU.min)
-        seg(r("pk", 0, 96), "Zp", ("GB", 0), 1536, True, False)
-        seg(r("pk", 0, 96), "Zp", ("GB", 3072), 1536, False, True)
-        for k in (2, 3):
-            seg(of("pk", k), "Zp", ("GB", 768 * k), 768, True, False)
-            seg(of("pk", k), "Zp", ("GB", 3072 + 768 * k), 768, False, True)
+        mm(r("pk", 0, 192), r("I1"), r("zz"), True, False)
+        for i, (j, n) in enumerate(CFG["Cord"]):
+            seg(r("pk", 48 * (j % 4), 48 * (j % 4 + n)), "Zp", ("GB", 768 * j), 768 * n, False, i == len(CFG["Cord"]) - 1)
         MG = 1.5 * 2 ** 27
         ts(r("rr"), r("pk", 0, 192), MG, ALU.add, -MG, ALU.add)
         tt(r("dd"), r("rr"), r("pk", 0, 192), ALU.subtract)
@@ -430,10 +449,9 @@ def build(T, g, core, topo):
         mm(r("pK", 0, 192), r("Ipen"), r("dd"), False, True)
         tree("pK", r("k12"), r("thX"))
         ts(r("cn"), r("k12"), 8191, ALU.bitwise_and)
-        cp(r("nlo", 1, 24, 2), r("cn"))
-        cp(r("nlf", 1, 24, 2), r("cn"))
-        cp(r("R"), (r("IO"), r("nlo")))
+        cp(r("nlf", 12, 24), r("cn"))
         cp(r("cno"), r("cn"))
+        cp(r("R", 192, 384), (r("IO"), r("cno")))
         nf1, fw, sw, z1 = r("nf", 0, 192), r("FS", 0, 192), r("FS", 192, 384), r(z, 0, 192)
         act(r("EW", 0, 192), (r("E1"), W))
         act(r("EW", 192, 384), (r("E2"), W))
@@ -470,41 +488,47 @@ def build(T, g, core, topo):
         lin(r("pa", 512, 704), [("I16", fw), ("I1", r("vv")), ("I16", r("inc", 0, 192))])
         act(r("EN1"), r("pa", 512, 896), bias=-16.0)
         e0 = 0
-        for b in range(12):
-            n = 384 - 32 * b
-            for k in range(2):
-                ts(r("EQ", e0, e0 + n), r("R", 32 * b, 384), r("nlf", 2 * b + k, 2 * b + k + 1), ALU.is_equal,
+        for kind, (r0, k0) in enumerate(((0, 0), (0, 12), (192, 0), (192, 12))):
+            for b in range(12):
+                n = 192 - 16 * b
+                ts(r("EQ", e0, e0 + n), r("R", r0 + 16 * b, r0 + 192), r("nlf", k0 + b, k0 + b + 1), ALU.is_equal,
                    r("wD", b, b + 1), ALU.mult)
-                mm(r("pT", 32 * b, 384), r("BO"), r("EQ", e0, e0 + n), b == 0 and k == 0, b == 11 and k == 1)
+                mm(r("pT", 16 * b, 192), r("BO"), r("EQ", e0, e0 + n), kind == 0 and b == 0, kind == 3 and b == 11)
                 e0 += n
         ts(r("nh"), r("cn"), float(NM), ALU.is_ge)
         tt(r("y1"), r("nh"), r("nfD", 0, 12), ALU.subtract)
         tt(r("y2"), r("y1"), r("dW"), ALU.mult)
-        tt(r("wX"), r("y2"), r("nlf", 0, 24, 2), ALU.max)
-        tt(r("fail"), r("pT", 0, 384), r("thM"), ALU.is_ge)
+        tt(r("wX"), r("y2"), r("nlf", 0, 12), ALU.max)
+        tt(r("fail"), r("pT", 0, 192), r("thM"), ALU.is_ge)
         scan(r("fsc"), r("sm"), r("fail"), 0.0, ALU.mult, ALU.max)
-        fD = r("fsc", 31, 384, 32)
+        fD = r("fsc", 15, 192, 16)
         sw_, sc_ = r("so", 0, 12), r("so", 12, 24)
         tt(r("fd", 0, 12), fD, r("dW"), ALU.mult)
         tt(r("of", 0, 12), r("fd", 0, 12), r("wX"), ALU.max)
         cp(sw_, r("of", 0, 12))
         tt(r("fd", 12, 24), fD, r("dC"), ALU.mult)
-        tt(r("of", 12, 24), r("fd", 12, 24), r("nlf", 1, 24, 2), ALU.max)
+        tt(r("of", 12, 24), r("fd", 12, 24), r("nlf", 12, 24), ALU.max)
         cp(sc_, r("of", 12, 24))
         if not last:
             cp((r("Y"), sw_), r("vv"))
-            cp((r("F"), sw_), r("FN", 0, 192))
-            cp((r("S"), sw_), r("FN", 192, 384))
-            cp((r("S"), sc_), sw)
+            scat("F", 0, "FN", 0, CFG["pf"])
+            scat("S", 0, "FN", 192, CFG["pf"])
+            scat("S", 12, "FS", 192, CFG["pf"])
             tt(r("mx"), fD, r("nh"), ALU.max)
             mm(r("pm", 0, 12), r("ONE"), r("mx"), True, True)
             act(r("ajk"), r("pm", 0, 12), bias=128.0, scale=-1.0, acc=r("Acol"))
-        cp((r("E2"), sw_), r("EN2", 0, 192))
-        cp((r("E2"), sc_), r("EN2", 192, 384))
+        if last:
+            cp((r("E2"), r("so")), r("EN2"))
+        else:
+            scat("E2", 0, "EN2", 0, CFG["pe"])
+            scat("E2", 12, "EN2", 192, CFG["pe"])
         if last:
             store(T.ys[:], r("E2", 0, NM), "s1")
-        cp((r("E1"), sw_), r("EN1", 0, 192))
-        cp((r("E1"), sc_), r("EN1", 192, 384))
+        if last:
+            cp((r("E1"), r("so")), r("EN1"))
+        else:
+            scat("E1", 0, "EN1", 0, CFG["pe"])
+            scat("E1", 12, "EN1", 192, CFG["pe"])
         if last:
             for j in range(64):
                 mm(r("pm", 0, 64), r("I1"), r("E1", 64 * j, 64 * j + 64), j == 0, j == 63)
@@ -536,7 +560,8 @@ def plan(ops):
         for x in o["w"]:
             for j, y, wr in hist.get(x[0], []):
                 if overlap(x, y):
-                    (s if o["e"] == "P" and ops[j]["e"] == "P" else d).add(j)
+                    same = o["e"] == ops[j]["e"] and (o["e"] == "P" or (CFG["inorder"] and o["e"] in "VA"))
+                    (s if same else d).add(j)
         for x in o["w"]:
             if x[3] == 1:
                 hist[x[0]] = [h for h in hist.get(x[0], []) if not (

@@ -1,3 +1,4 @@
+import numpy as np
 from concourse.bass import DstId, RemoteDMATransfer
 from concourse.mybir import AluOpType as ALU, AxisListType as AX, ActivationFunctionType as AF
 
@@ -8,12 +9,14 @@ KA = (3, 61, 118, 207, 346, 419, 530, 677, 742, 895, 1011, 1164, 1283, 1450, 162
 TW = NM + 2 * LN
 YO = 208.0
 FO = 204.0
-CH = (512, 512, 1024, 1024, 1024)
+CH = (512,) * 8
 HUGE = float(2 ** 99)
 
 B16, F32, I32, U16, F16 = "bfloat16", "float32", "int32", "uint16", "float16"
 SB = {
-    "E1": (TW, B16), "E2": (TW, B16), "Y": (TW, B16), "F": (TW, B16), "S": (TW, B16), "IO": (TW, I32),
+    "FE": (2 * TW, B16), "E2": (TW, B16), "YS": (2 * TW, B16), "IO": (TW, I32),
+    "I256": (128, B16), "In512": (128, B16), "dA": (12, F32), "nfB": (12, F32), "la1": (12, F32), "la2": (12, F32),
+    "la3": (12, F32), "ra": (192, B16), "vA": (192, B16), "rb": (384, B16), "vB": (192, B16),
     "sel": (NM, B16), "At": (NM, B16), "S1": (NM, B16), "GB": (6144, B16), "EQ": (4992, B16),
     "nmi": (192, I32), "nmf": (192, F32), "X1": (384, F32), "X2": (384, F32), "ynf": (192, F32),
     "off0": (192, U16), "off1": (192, U16), "off2": (192, U16),
@@ -39,10 +42,10 @@ SB = {
     "flag": (192, B16), "nf": (384, B16), "nfD": (16, B16), "nfX": (192, B16),
     "rr": (192, F16), "dd": (192, B16), "cn": (12, I32), "nlo": (24, U16), "nlf": (24, F32), "cno": (12, U16),
     "R": (384, U16), "fail": (192, B16), "fsc": (192, B16), "nh": (12, F32), "y1": (12, F32), "y2": (12, F32),
-    "wX": (12, F32), "fd": (24, F32), "of": (24, F32), "so": (24, U16), "mx": (12, B16), "Acol": (1, F32),
+    "wX": (12, F32), "fd": (36, F32), "of": (36, F32), "so": (36, U16), "mx": (12, B16), "Acol": (1, F32),
     "ajk": (12, F32), "C3": (576, B16), "ab": (384, B16), "bb": (384, B16), "sat": (384, B16), "inc": (384, B16),
     "r12": (384, B16), "vv": (192, B16), "se": (192, B16), "FN": (384, B16), "EN1": (384, B16), "EN2": (384, B16),
-    "yfs": (64, F32),
+    "yfs": (64, F32), "k25": (512, B16), "fo": (768, F16),
 }
 PS = {"pa": 1024, "pb": 1024, "pk": 512, "pK": 512, "pT": 512, "pm": 512}
 HOME = {}
@@ -61,25 +64,32 @@ DMAS = (["dn", "dz0", "dz1", "dz2", "dz3"] + ["da%d" % i for i in range(len(CH))
         + ["s0", "s1", "s3", "s4"])
 SEMAPHORES = ["eV", "eA", "eP", "eG", "arr1", "arr2", "sent"] + DMAS
 CFG = {
-    "A": ((1, 1, 1, 3), (1, 1, 3, 3), (1, 1, 3, 3)),
+    "A": ((1, 1, 1, 3), (1, 1, 1, 3), (1, 1, 1, 3)),
     "C": 3,
-    "S2V": (1, 3),
+    "late": (), "seed": 0, "amp": 0.0,
+    "S2V": (0, 2, 4, 6, 7),
     "S1V": (),
     "theta": 0.4,
-    "Aord": ((0, 3, 1, 2), (0, 1, 2, 3), (0, 1, 2, 3)),
-    "Cord": ((0, 2), (4, 2), (2, 1), (6, 1), (7, 1), (3, 1)),
+    "Aord": ((0, 3, 1, 2), (0, 3, 1, 2), (0, 3, 1, 2)),
+    "Cord": ((0, 2), (4, 1), (2, 1), (5, 1), (3, 1), (6, 1), (7, 1)),
     "reduce": True,
-    "csplit": ((0, 96), (96, 192)),
+    "csplit": ((0, 64), (64, 192)),
     "pe": 4, "pf": 12,
     "inorder": False,
     "up": (0.0, 0.0, 0.0),
-    "early": {"flag": 3000.0},
+    "early": {"flag": 3000.0, "ynf": 5000.0, "vA": 1500.0},
 }
-EST = {"cyc": 0.9, "pe": 0.45, "ga": 1.56, "sc": 3.8, "wake": 210.0, "afix": 60.0, "pefix": 10.0, "pelat": 60.0,
+EST = {"cyc": 0.85, "pe": 0.43, "ga": 1.56, "sc": 3.8, "wake": 210.0, "afix": 60.0, "pefix": 10.0, "pelat": 60.0,
        "dfix": 1800.0, "dbw": 250.0, "remote": 3500.0}
 
 
+PAIR = {"Y": ("YS", 0), "S": ("YS", TW), "F": ("FE", 0), "E1": ("FE", TW)}
+
+
 def r(name, a=0, b=None, s=1):
+    if name in PAIR:
+        h, o = PAIR[name]
+        return (h, o + a, o + (TW if b is None else b), s)
     if b is None:
         b = SB[name][0] if name in SB else PS[name]
     return (name, a, b, s)
@@ -225,7 +235,8 @@ def build(T, g, core, topo):
     act(r("Zp"), r("Z1"), scale=16.0)
     act(r("In"), r("I1"), scale=-1.0)
     act(r("If"), r("I1"))
-    act(r("In32"), r("I1"), scale=-32.0)
+    act(r("I256"), r("I1"), scale=256.0)
+    act(r("In512"), r("I1"), scale=-512.0)
     act(r("Ipen"), r("I1"), scale=float(2 ** 26))
     act(r("Inf"), r("I1"), scale=float(2 ** 23))
     iota(r("ct", 0, 24), [[16, 12], [0, 2]], 0, 0)
@@ -241,6 +252,7 @@ def build(T, g, core, topo):
     cp(r("oN2"), r("ct", 84, 96))
     ts(r("dW"), r("ct", 36, 48), float(NM), ALU.add)
     ts(r("dC"), r("ct", 36, 48), float(NM + LN), ALU.add)
+    ts(r("dA"), r("ct", 36, 48), float(NM + LN + TW), ALU.add)
     cp(r("nmf"), r("nmi"))
     act(r("X1"), (r("nmf"), r("oN1")))
     turn(r("X2"), r("X1"))
@@ -290,6 +302,8 @@ def build(T, g, core, topo):
         act(r("thM", 16 * b, 16 * b + 16), r("ndg", 0, 16), bias=r("tD", b, b + 1))
 
     RB = 192.0 - 7.5 / 16.0
+    if CFG["late"]:
+        ms(r("k25"), 25.5)
     c0, hb = 0, 0
     for i, n in enumerate(CH):
         ts(r("F", c0, c0 + n), r("E1", c0, c0 + n), 1.0 / 16.0, ALU.mult, RB, ALU.add)
@@ -303,11 +317,16 @@ def build(T, g, core, topo):
         else:
             act(r("S", c0, c0 + n), r("S1", c0, c0 + n), bias=-FO)
         for a in range(c0, c0 + n, 512):
-            h = 512 * (hb % 2); hb += 1
-            lin(r("pa", h, h + 512), [("I1", r("E1", a, a + 512)), ("In16", r("F", a, a + 512)), ("In16", r("sel", a, a + 512))])
-            lin(r("pb", h, h + 512), [("I1", r("E2", a, a + 512)), ("In16", r("S", a, a + 512)), ("I16", r("sel", a, a + 512))])
-            act(r("At", a, a + 512), r("pa", h, h + 512), bias=16.0 + 16.0 * FO)
-            tt(r("Y", a, a + 512), r("pb", h, h + 512), r("At", a, a + 512), ALU.max)
+            b1 = (r("pk"), r("pK"), r("pa", 0, 512), r("pa", 512, 1024))[hb % 4]
+            b2 = (r("pT"), r("pm"), r("pb", 0, 512), r("pb", 512, 1024))[hb % 4]
+            hb += 1
+            lin(b1, [("I1", r("E1", a, a + 512)), ("In16", r("F", a, a + 512)), ("In16", r("sel", a, a + 512))])
+            if i in CFG["late"]:
+                lin(b2, [("ONE", r("k25")), ("I1", r("E2", a, a + 512)), ("In16", r("S1", a, a + 512)), ("I16", r("sel", a, a + 512))])
+            else:
+                lin(b2, [("I1", r("E2", a, a + 512)), ("I16", r("sel", a, a + 512)), ("In16", r("S", a, a + 512))])
+            act(r("At", a, a + 512), b1, bias=16.0 + 16.0 * FO)
+            tt(r("Y", a, a + 512), b2, r("At", a, a + 512), ALU.max)
         c0 += n
 
     def tree(src, o, extra):
@@ -350,6 +369,19 @@ def build(T, g, core, topo):
             if CFG["A"][t][k] == 1:
                 tt(gs(k), (r("Y"), of(off, k)), r(z), ALU.subtract)
                 act(gs(k), gs(k), AF.Abs, bias=-YO)
+            elif CFG["A"][t][k] == 4:
+                for a in (0, 24):
+                    h0 = r("GB", 768 * k + 16 * a, 768 * k + 16 * a + 384)
+                    tt(h0, (r("Y"), r(off, 48 * k + a, 48 * k + a + 24)), r(z, 0, 384), ALU.subtract)
+                    act(h0, h0, AF.Abs, bias=-YO)
+            elif CFG["A"][t][k] == 2:
+                pbuf = ("pa", "pb")[n3 % 2]; n3 += 1
+                h0, h1 = r("GB", 768 * k, 768 * k + 384), r("GB", 768 * k + 384, 768 * k + 768)
+                tt(h0, (r("Y"), r(off, 48 * k, 48 * k + 24)), r(z, 0, 384), ALU.subtract)
+                act(h0, h0, AF.Abs, bias=-YO)
+                act(h1, (r("Y"), r(off, 48 * k + 24, 48 * k + 48)))
+                lin(r(pbuf, 0, 384), [("In", r(z, 0, 384)), ("I1", h1)])
+                act(h1, r(pbuf, 0, 384), AF.Abs, bias=-YO)
             else:
                 pbuf = ("pa", "pb")[n3 % 2]; n3 += 1
                 act(gs(k), (r("Y"), of(off, k)))
@@ -396,6 +428,8 @@ def build(T, g, core, topo):
         mm(r("pm", 192, 384), r("BO"), r("flag"), True, True)
         seg(r("pm", 384, 396), "Z1", ("flag", 0), 192, True, True)
         act(r("nfD", 0, 12), r("pm", 384, 396), AF.Relu, bias=1.0, scale=-4.0)
+        if not last:
+            act(r("nfB"), r("pm", 384, 396), AF.Relu, bias=16384.0, scale=-65536.0)
         act(r("nfX"), (r("nfD"), r("oE")))
         act(r("nf"), r("pm", 0, 384), AF.Relu, bias=1.0, scale=-4.0)
         cp(r("cfl"), r("c2"))
@@ -432,11 +466,13 @@ def build(T, g, core, topo):
             act(r("ynf"), (r("X2"), r("oD2")))
             store(T.yn[:], r("ynf"), "s3")
         for k in range(4):
-            if k < CFG["C"]:
-                tt(gs(k), (r("S"), of("coff", k)), r("FW4"), ALU.min)
-            else:
-                act(gs(k), (r("S"), of("coff", k)))
-                tt(gs(k), gs(k), r("pa", 0, 768), ALU.min)
+            cut = min(max(int(48 * CFG["C"]) - 48 * k, 0), 48)
+            if cut > 0:
+                tt(r("GB", 768 * k, 768 * k + 16 * cut), (r("S"), r("coff", 48 * k, 48 * k + cut)), r("FW4", 0, 16 * cut), ALU.min)
+            if cut < 48:
+                rest = r("GB", 768 * k + 16 * cut, 768 * k + 768)
+                act(rest, (r("S"), r("coff", 48 * k + cut, 48 * k + 48)))
+                tt(rest, rest, r("pa", 16 * cut, 768), ALU.min)
             act(gf(k), (r("F"), of("coff", k)), bias=-FO)
             tt(gf(k), gf(k), r("pb", 0, 768), ALU.min)
         mm(r("pk", 0, 192), r("I1"), r("zz"), True, False)
@@ -472,21 +508,31 @@ def build(T, g, core, topo):
         act(fc, (r("F"), C), bias=-FO)
         lin(r("pa", 512, 896), [("I1", r("nf")), ("In", r("sat")), ("In", r("bb"))])
         act(r("inc"), r("pa", 512, 896), AF.Relu)
-        lin(r("pb", 0, 192), [("In", sw), ("In32", nf1), ("I1", scn)])
+        lin(r("pb", 0, 192), [("In", sw), ("In512", nf1), ("I1", scn)])
         act(r("se"), r("pb", 0, 192), AF.Relu, bias=16.0)
         lin(r("pb", 512, 704), [("I1", sw), ("I16", nf1), ("I1", r("inc", 192, 384)), ("I1", r("se"))])
         act(r("FN", 192, 384), r("pb", 512, 704), bias=-16.0)
         if not last:
-            lin(r("pa", 0, 192), [("I1", fw), ("I1", r("inc", 0, 192))])
-            act(r("FN", 0, 192), r("pa", 0, 192), bias=FO)
+            lin(r("pm", 0, 192), [("I1", sw), ("In", r("yw")), ("In512", nf1)])
+            act(r("ra"), r("pm", 0, 192), AF.Relu, bias=256.0)
+            lin(r("pm", 0, 192), [("I256", nf1), ("I1", r("vv")), ("I1", r("ra"))])
+            act(r("vA"), r("pm", 0, 192), bias=-256.0)
+            lin(r("pa", 0, 192), [("I1", fw), ("I256", nf1), ("I1", r("inc", 0, 192))])
+            act(r("rb", 0, 192), r("pa", 0, 192), AF.Relu, bias=FO - 256.0)
+            lin(r("pa", 192, 384), [("In512", nf1), ("I16", fc), ("I1", yc)])
+            act(r("rb", 192, 384), r("pa", 192, 384), AF.Relu, bias=-16.0)
+            lin(r("pa", 0, 192), [("I1", r("rb", 0, 192)), ("I1", r("rb", 192, 384))])
+            act(r("vB"), r("pa", 0, 192))
         lin(r("pb", 192, 384), [("I16", sw), ("I1", yc)])
         lin(r("pb", 0, 192), [("I1", r("vv")), ("I16", r("FN", 192, 384))])
         up[0] = CFG["up"][t]
         act(r("EN2"), r("pb", 0, 384), bias=-16.0)
         up[0] = 0.0
-        lin(r("pa", 704, 896), [("I16", fc), ("I1", yc)])
+        if last:
+            lin(r("pa", 704, 896), [("I16", fc), ("I1", yc)])
         lin(r("pa", 512, 704), [("I16", fw), ("I1", r("vv")), ("I16", r("inc", 0, 192))])
-        act(r("EN1"), r("pa", 512, 896), bias=-16.0)
+        ne = 384 if last else 192
+        act(r("EN1", 0, ne), r("pa", 512, 512 + ne), bias=-16.0)
         e0 = 0
         for kind, (r0, k0) in enumerate(((0, 0), (0, 12), (192, 0), (192, 12))):
             for b in range(12):
@@ -503,6 +549,13 @@ def build(T, g, core, topo):
         scan(r("fsc"), r("sm"), r("fail"), 0.0, ALU.mult, ALU.max)
         fD = r("fsc", 15, 192, 16)
         sw_, sc_ = r("so", 0, 12), r("so", 12, 24)
+        if not last:
+            ts(r("la1"), r("cn"), float(TW), ALU.add)
+            tt(r("la2"), r("la1"), r("nfB"), ALU.subtract)
+            tt(r("la3"), r("la2"), r("nlf", 0, 12), ALU.max)
+            tt(r("fd", 24, 36), fD, r("dA"), ALU.mult)
+            tt(r("of", 24, 36), r("fd", 24, 36), r("la3"), ALU.max)
+            cp(r("so", 24, 36), r("of", 24, 36))
         tt(r("fd", 0, 12), fD, r("dW"), ALU.mult)
         tt(r("of", 0, 12), r("fd", 0, 12), r("wX"), ALU.max)
         cp(sw_, r("of", 0, 12))
@@ -510,28 +563,29 @@ def build(T, g, core, topo):
         tt(r("of", 12, 24), r("fd", 12, 24), r("nlf", 12, 24), ALU.max)
         cp(sc_, r("of", 12, 24))
         if not last:
-            cp((r("Y"), sw_), r("vv"))
-            scat("F", 0, "FN", 0, CFG["pf"])
+            scat("YS", 24, "vA", 0, 12)
+            scat("FE", 24, "vB", 0, CFG["pf"])
             scat("S", 0, "FN", 192, CFG["pf"])
-            scat("S", 12, "FS", 192, CFG["pf"])
             tt(r("mx"), fD, r("nh"), ALU.max)
             mm(r("pm", 0, 12), r("ONE"), r("mx"), True, True)
             act(r("ajk"), r("pm", 0, 12), bias=128.0, scale=-1.0, acc=r("Acol"))
         if last:
-            cp((r("E2"), r("so")), r("EN2"))
+            cp((r("E2"), r("so", 0, 24)), r("EN2"))
         else:
             scat("E2", 0, "EN2", 0, CFG["pe"])
             scat("E2", 12, "EN2", 192, CFG["pe"])
         if last:
             store(T.ys[:], r("E2", 0, NM), "s1")
         if last:
-            cp((r("E1"), r("so")), r("EN1"))
+            cp((r("E1"), r("so", 0, 24)), r("EN1"))
         else:
             scat("E1", 0, "EN1", 0, CFG["pe"])
-            scat("E1", 12, "EN1", 192, CFG["pe"])
         if last:
-            for j in range(64):
-                mm(r("pm", 0, 64), r("I1"), r("E1", 64 * j, 64 * j + 64), j == 0, j == 63)
+            tt(r("fo"), r("E1", 0, 768), r("E1", 768, 1536), ALU.add)
+            for j in range(24, 64):
+                mm(r("pm", 0, 64), r("I1"), r("E1", 64 * j, 64 * j + 64), j == 24, False)
+            for j in range(12):
+                mm(r("pm", 0, 64), r("I1"), r("fo", 64 * j, 64 * j + 64), False, j == 11)
             cp(r("yfs"), r("pm", 0, 64))
             store(T.yf[:], r("yfs"), "s4")
     return ops
@@ -598,6 +652,8 @@ def plan(ops):
         for k in succ[i]:
             m = max(m, prio[k] + ((tail(o) + EST["wake"]) if (i in deps[k] or ops[k]["e"] == "X") else 0.0))
         prio[i] = o["dur"] + m + o["up"] + (CFG["early"].get(o["w"][0][0], 0.0) if o["w"] else 0.0)
+    jit = np.random.RandomState(CFG["seed"]).uniform(0.0, CFG["amp"], n)
+    prio = [p + float(j) for p, j in zip(prio, jit)]
     left = [len(deps[i] | soft[i]) for i in range(n)]
     ready = [0.0] * n
     cand = {q: [] for q in "VAPGSX"}
@@ -634,6 +690,7 @@ def plan(ops):
         else:
             end = free[q] + o["lat"]
         order.append(c)
+        PLAN["end"] = max(PLAN.get("end", 0.0), end)
         for k in succ[c]:
             if c in deps[k]:
                 ready[k] = max(ready[k], end + (0.0 if o["e"] == "X" else EST["wake"]))

@@ -10,44 +10,53 @@ TW = NM + 2 * LN
 YO = 208.0
 FO = 204.0
 CH = (512,) * 8
+H = 2
+NB = 12 // H
+CW = 16 * NB
+ZP = 3 * CW * (H - 1)
+SP = CW * (H - 1)
+RF, RS = 4, 2
 HUGE = float(2 ** 99)
 
 B16, F32, I32, U16, F16 = "bfloat16", "float32", "int32", "uint16", "float16"
 SB = {
-    "FE": (2 * TW, B16), "E2": (TW, B16), "YS": (2 * TW, B16), "IO": (TW, I32),
-    "I256": (128, B16), "In512": (128, B16), "dA": (12, F32), "nfB": (12, F32), "la1": (12, F32), "la2": (12, F32),
-    "la3": (12, F32), "ra": (192, B16), "vA": (192, B16), "rb": (384, B16), "vB": (192, B16),
-    "sel": (NM, B16), "At": (NM, B16), "S1": (NM, B16), "GB": (6144, B16), "EQ": (4992, B16),
+    "FE": (2 * TW, B16), "YS": (2 * TW, B16), "E2": (TW, B16), "IO": (TW, I32),
+    "sel": (NM, B16), "At": (NM, B16), "S1": (NM, B16), "GA": (3072, B16), "GS": (3072, B16), "GF": (3072, B16),
+    "EQ": (4992, B16),
     "nmi": (192, I32), "nmf": (192, F32), "X1": (384, F32), "X2": (384, F32), "ynf": (192, F32),
-    "off0": (192, U16), "off1": (192, U16), "off2": (192, U16),
-    "Lf0": (192, F32), "Lf1": (192, F32), "Lf2": (192, F32),
+    "off0": (192, U16), "off1": (192, U16), "off2": (192, U16), "Lf": (192, F32),
     "z0": (768, B16), "z1": (768, B16), "z2": (768, B16),
-    "so0": (192, U16), "so1": (192, U16), "sl0": (192, F32), "sl1": (192, F32), "sl2": (192, F32),
-    "sz0": (192, B16), "sz1": (192, B16), "sz2": (192, B16),
+    "so0": (192, U16), "so1": (192, U16), "sl2": (192, F32),
+    "sz0": (192 * H, B16), "sz1": (192 * H, B16), "sz2": (192 * H, B16),
     "ci": (16, I32), "cj": (16, I32), "cf": (16, F32), "ramp": (144, F32), "r128": (128, F32),
-    "ct": (96, F32), "cu": (192, F32), "cv": (192, F32),
+    "ct": (144, F32), "cu": (192, F32), "cv": (192, F32),
     "Z1": (144, B16), "Zn": (144, B16), "Zp": (144, B16), "Zw": (144, F16),
-    "I1": (128, B16), "In": (128, B16), "I16": (128, B16), "In16": (128, B16), "In32": (128, B16),
-    "Ipen": (128, B16), "Inf": (128, B16), "I512": (128, F16), "If": (128, F32), "BO": (128, B16), "ONE": (128, B16),
-    "dg": (32, F32), "dg2": (32, F32), "ndg": (32, F32), "wr": (16, F32), "wp": (16, F32), "h16": (16, F32),
-    "h17": (16, F32), "zer": (16, F32),
-    "wD": (16, F32), "tD": (16, F32), "thM": (192, F32), "sm": (192, B16), "zz": (192, B16),
-    "kap": (192, F32), "K37": (192, F32), "thX": (96, F32), "dW": (12, F32), "dC": (12, F32), "t1": (24, I32),
-    "oE": (12, U16), "oN1": (24, U16), "oN2": (12, U16), "oD1": (24, U16), "oD2": (12, U16),
-    "a96": (96, F32), "b96": (96, F32), "a48": (48, F32), "a24": (24, F32), "k12": (12, I32),
-    "wi": (12, I32), "woff": (12, U16), "yw": (192, B16), "FS": (384, B16), "EW": (384, B16), "FS2": (384, B16),
-    "FW4": (768, B16), "ui": (12, I32), "u": (16, I32), "u2": (12, I32), "q": (16, I32), "q2": (16, I32),
-    "ku": (192, F32), "ku2": (192, F32), "c1": (192, I32), "c2": (192, I32), "coff": (192, U16), "cfl": (192, F32),
-    "m1": (12, I32), "m2": (16, F32), "p1": (192, F32), "p2": (192, I32), "p3": (192, I32),
-    "flag": (192, B16), "nf": (384, B16), "nfD": (16, B16), "nfX": (192, B16),
-    "rr": (192, F16), "dd": (192, B16), "cn": (12, I32), "nlo": (24, U16), "nlf": (24, F32), "cno": (12, U16),
-    "R": (384, U16), "fail": (192, B16), "fsc": (192, B16), "nh": (12, F32), "y1": (12, F32), "y2": (12, F32),
-    "wX": (12, F32), "fd": (36, F32), "of": (36, F32), "so": (36, U16), "mx": (12, B16), "Acol": (1, F32),
-    "ajk": (12, F32), "C3": (576, B16), "ab": (384, B16), "bb": (384, B16), "sat": (384, B16), "inc": (384, B16),
-    "r12": (384, B16), "vv": (192, B16), "se": (192, B16), "FN": (384, B16), "EN1": (384, B16), "EN2": (384, B16),
-    "yfs": (64, F32), "k25": (512, B16), "fo": (768, F16),
+    "I1": (128, B16), "In": (128, B16), "I16": (128, B16), "In16": (128, B16), "I64": (128, B16), "I256": (128, B16),
+    "In512": (128, B16), "Ipen": (128, B16), "Inf": (128, B16), "Ihg": (128, B16), "I512": (128, F16), "If": (128, F32),
+    "BO": (128, B16), "ONE": (128, B16),
+    "dg": (16, F32), "dg2": (16, F32), "wr": (16, F32), "wp": (16, F32), "h16": (16, F32), "h17": (16, F32), "zer": (16, F32),
+    "wD": (16, F32), "th2": (192, B16), "thM": (192, B16), "thL": (192, B16), "nd": (192, B16), "hlf": (192, B16),
+    "sm": (192, B16), "zz": (192, B16),
+    "kap": (CW, F32), "K37": (192, F32), "thX": (12, F32), "dS": (48, F32), "t1": (12, I32), "t2": (4, I32),
+    "tF": (12, F32), "oF": (4, U16),
+    "oE": (12, U16), "oG": (12, U16), "oN1": (24, U16), "oN2": (12, U16), "oD1": (24, U16), "oD2": (12, U16),
+    "k12": (12, I32), "kc": (12, I32), "wi": (12, I32), "woff": (12, U16), "yw": (192, B16), "W2": (384, B16), "EW": (384, B16),
+    "FW": (192 * RF, B16), "SW": (192 * RS, B16),
+    "ui": (12, I32), "u": (32, I32), "u2": (12, F32), "q": (32, I32), "ku": (192, F32), "c1": (192, I32), "c2": (192, I32),
+    "coff": (192, U16), "cfl": (192, F32),
+    "m1": (32, I32), "m2": (32, F32), "p1": (192, F32), "p2": (192, I32), "p3": (192, I32),
+    "flag": (192, B16), "nf": (192, B16), "nfD": (12, B16), "nfB": (12, F32), "D": (192, B16),
+    "rr": (192, F16), "dd": (192, B16), "cn": (12, I32), "nlf": (64, F32), "cno": (12, U16),
+    "R": (384, U16), "f1": (192, B16), "f1s": (192, B16), "fk": (192, B16), "gk": (192, B16), "fail": (192, B16), "fsc": (192, B16),
+    "ya": (12, F32), "yb": (12, F32), "yc": (12, F32), "sy": (12, U16),
+    "nh": (12, F32), "y1": (12, F32), "y2": (12, F32), "la1": (12, F32), "la2": (12, F32),
+    "fd": (48, F32), "of": (48, F32), "so": (48, U16), "mx": (12, B16), "Acol": (1, F32), "ajk": (12, F32),
+    "C3": (576, B16), "ab": (384, B16), "bb": (384, B16), "sat": (384, B16), "inc": (384, B16),
+    "rv": (192, B16), "vv": (192, B16), "se": (192, B16), "SN": (192, B16), "rb": (384, B16), "vB": (192, B16),
+    "ra": (192, B16), "vA": (192, B16),
+    "EN1": (384, B16), "EN2": (384, B16), "yfs": (64, F32), "fo": (768, F16),
 }
-PS = {"pa": 1024, "pb": 1024, "pk": 512, "pK": 512, "pT": 512, "pm": 512}
+PS = {"pa": 512, "pb": 512, "pk0": 512, "pk1": 512, "pK": 512, "pT": 512, "pU": 512, "pm": 512}
 HOME = {}
 SCRATCH = {}
 for _k, (_n, _d) in SB.items():
@@ -60,24 +69,22 @@ for _k, (_n, _d) in SB.items():
         SCRATCH["n" + _d] = ("sbuf", [128, _o + (_n + 15) // 16 * 16], _d)
 HOME.update({k: (k, 0) for k in PS})
 SCRATCH.update({k: ("psum", [128, v], F32) for k, v in PS.items()})
-DMAS = (["dn", "dz0", "dz1", "dz2", "dz3"] + ["da%d" % i for i in range(len(CH))] + ["db%d" % i for i in range(len(CH))]
+DMAS = (["dn"] + ["dz%d" % i for i in range(4 * H)] + ["da%d" % i for i in range(len(CH))] + ["db%d" % i for i in range(len(CH))]
         + ["s0", "s1", "s3", "s4"])
 SEMAPHORES = ["eV", "eA", "eP", "eG", "arr1", "arr2", "sent"] + DMAS
 CFG = {
-    "A": ((1, 1, 1, 3), (1, 1, 1, 3), (1, 1, 1, 3)),
-    "C": 3,
-    "late": (), "seed": 0, "amp": 0.0,
+    "sep": True, "split": (False, False, True), "vsplit": (False, False, True), "wide": True,
+    "G": ("Lf", "cfl", "FW", "SW", "nlf", "so0", "so1", "sl2"),
+    "A": (("bbbd", "bbbd"), ("bbdD", "bbdD"), ("bbdD", "bbdD")),
+    "Aseg": ((0, 2), (2, 2)),
+    "C": ("eeff", "eeff"),
+    "Cseg": (("GS", 0, 4), ("GF", 0, 2), ("GF", 2, 2)),
+    "Fw": 2,
     "S2V": (0, 2, 4, 6, 7),
-    "S1V": (),
-    "theta": 0.4,
-    "Aord": ((0, 3, 1, 2), (0, 3, 1, 2), (0, 3, 1, 2)),
-    "Cord": ((0, 2), (4, 1), (2, 1), (5, 1), (3, 1), (6, 1), (7, 1)),
-    "reduce": True,
-    "csplit": ((0, 64), (64, 192)),
-    "pe": 4, "pf": 12,
-    "inorder": False,
-    "up": (0.0, 0.0, 0.0),
-    "early": {"flag": 3000.0, "ynf": 5000.0, "vA": 1500.0},
+    "theta": 0.8, "seed": 0, "amp": 0.0,
+    "pe": 12, "pf": 12,
+    "ywA": True,
+    "rounds": 4000, "turns": 60, "jit": 300.0, "units": "P", "give": 1e9, "tjit": 0.0, "mean": 0.0, "crit": 1.0, "slack": 20.0, "dbank": ("pK", "pU"),
 }
 EST = {"cyc": 0.85, "pe": 0.43, "ga": 1.56, "sc": 3.8, "wake": 210.0, "afix": 60.0, "pefix": 10.0, "pelat": 60.0,
        "dfix": 1800.0, "dbw": 250.0, "remote": 3500.0}
@@ -119,7 +126,8 @@ def vcost(o, ins, two=False):
 def build(T, g, core, topo):
     rank = T.rank_of(core)
     ops = []
-    up = [0.0]
+    tag = ["start", 0]
+    bun = [0]
 
     def ap(x):
         if len(x) == 2:
@@ -140,7 +148,7 @@ def build(T, g, core, topo):
         for i in ins:
             if isref(i):
                 rd.extend(list(i) if len(i) == 2 else [i])
-        ops.append({"e": eng, "f": fn, "w": w, "r": rd, "sem": sem, "inc": inc, "dur": dur, "lat": lat, "up": up[0]})
+        ops.append({"e": eng, "f": fn, "w": w, "r": rd, "sem": sem, "inc": inc, "dur": dur, "lat": lat, "tag": tag[0] + str(tag[1]), "bun": bun[0]})
 
     def sc(x):
         return ap(x) if isref(x) else x
@@ -160,8 +168,8 @@ def build(T, g, core, topo):
     def ms(o, c):
         op("V", lambda: g.vector.memset(ap(o), c), [o], [], vcost(o, []))
 
-    def red(o, i):
-        op("V", lambda: g.vector.tensor_reduce(ap(o), ap(i), AX.X, ALU.add), [o], [i], 67.0)
+    def red(o, i, f):
+        op("V", lambda: g.vector.tensor_reduce(ap(o), ap(i), AX.X, f), [o], [i], 64 * EST["cyc"])
 
     def turn(o, i):
         op("V", lambda: g.vector.transpose(ap(o), ap(i)), [o], [i], vcost(o, [i]))
@@ -183,8 +191,12 @@ def build(T, g, core, topo):
            EST["pefix"] + max(64, width(x)) * EST["pe"] * (1 if narrow(x) else 4), lat=EST["pelat"])
 
     def lin(o, terms):
-        for k, (l, x) in enumerate(terms):
-            mm(o, r(l), x, k == 0, k == len(terms) - 1)
+        n = width(o)
+        calls = [(l, x, a) for l, x in terms for a in range(0, n, width(x))]
+        bun[0] = len(ops) + 1
+        for k, (l, x, a) in enumerate(calls):
+            mm(r(o[0], o[1] + a, o[1] + a + width(x)), r(l), x, k == 0, k == len(calls) - 1)
+        bun[0] = 0
 
     def iota(o, pat, base, cm):
         d = 130 + 2 * width(o) * EST["cyc"]
@@ -192,6 +204,11 @@ def build(T, g, core, topo):
             op("G", lambda: g.iota(ap(o), pat, base, cm, allow_small_or_imprecise_dtypes=True), [o], [], d)
         else:
             op("G", lambda: g.iota(ap(o), pat, base, cm), [o], [], d)
+
+    def side(o, i):
+        if o[0] not in CFG["G"]:
+            return cp(o, i)
+        op("G", lambda: g.affine_select(ap(o), ap(i), [[0, width(o)]], ALU.is_ge, 0.0, 0, 0), [o], [i], 170 + 2 * width(o) * EST["cyc"])
 
     def nbytes(x):
         return 128 * width(x) * (2 if narrow(x) else 4)
@@ -204,7 +221,9 @@ def build(T, g, core, topo):
 
     def seg(o, zname, x0, n, first, last):
         for p in range(16):
+            bun[0] = len(ops) - p % 8 + 1
             mm(o, r(zname, 16 - p, 144 - p), r(x0[0], x0[1] + p, x0[1] + n, 16), first and p == 0, last and p == 15)
+        bun[0] = 0
 
     c0 = 0
     for i, n in enumerate(CH):
@@ -213,8 +232,8 @@ def build(T, g, core, topo):
         if i == 1:
             load(r("nmi"), T.nm[:], "dn")
         c0 += n
-    for k in range(4):
-        load(r("z0", 192 * k, 192 * k + 192), T.zv[:], "dz%d" % k)
+    for k in range(4 * H):
+        load(r("z0", CW * k, CW * k + CW), T.zv[:, CW * (k // 4):CW * (k // 4) + CW], "dz%d" % k)
 
     iota(r("r128"), [[1, 128]], 0, -1)
     iota(r("ci", 0, 1), [[0, 1]], 0, 1)
@@ -229,228 +248,239 @@ def build(T, g, core, topo):
     ts(r("In16"), r("r128"), 0.0, ALU.is_equal, -16.0, ALU.mult)
     ts(r("I512"), r("r128"), 0.0, ALU.is_equal, 512.0, ALU.mult)
     for nme in ("E1", "E2", "Y", "F", "S"):
-        ms(r(nme, NM, TW), 0.0)
+        ms(r(nme, NM, TW), FO if nme == "F" else 0.0)
     ts(r("Z1"), r("ramp"), g16, ALU.is_equal)
     act(r("Zn"), r("Z1"), scale=-4096.0)
     act(r("Zp"), r("Z1"), scale=16.0)
-    act(r("In"), r("I1"), scale=-1.0)
-    act(r("If"), r("I1"))
-    act(r("I256"), r("I1"), scale=256.0)
-    act(r("In512"), r("I1"), scale=-512.0)
-    act(r("Ipen"), r("I1"), scale=float(2 ** 26))
-    act(r("Inf"), r("I1"), scale=float(2 ** 23))
+    for nme, v in (("In", -1), ("If", 1), ("I64", 64), ("I256", 256), ("In512", -512), ("Ipen", 2 ** 26), ("Inf", -2 ** 23),
+                   ("Ihg", 2 ** 97)):
+        act(r(nme), r("I1"), scale=float(v))
     iota(r("ct", 0, 24), [[16, 12], [0, 2]], 0, 0)
     ts(r("oN1"), r("ct", 0, 24), p16, ALU.add)
-    iota(r("ct", 24, 36), [[16, 12]], 0, 0)
+    iota(r("ct", 24, 36), [[0, H], [16, NB]], 0, 0)
+    iota(r("ct", 96, 108), [[32 * NB, H], [0, NB]], 0, 0)
+    iota(r("ct", 108, 120), [[16, H], [0, NB]], 0, 0)
+    iota(r("ct", 120, 132), [[16, 12]], 0, 0)
     ts(r("ct", 36, 48), r("ct", 24, 36), p16, ALU.add)
-    ts(r("t1", 0, 12), r("ct", 36, 48), -5.5, ALU.add, 1.0 / 12.0, ALU.mult)
-    ts(r("ct", 48, 60), r("t1", 0, 12), -12.0, ALU.mult)
+    ts(r("t1"), r("ct", 36, 48), -(NB - 1) / 2.0, ALU.add, 1.0 / NB, ALU.mult)
+    ts(r("ct", 48, 60), r("t1"), -float(NB), ALU.mult)
     tt(r("ct", 60, 72), r("ct", 48, 60), r("ct", 36, 48), ALU.add)
     cp(r("oE"), r("ct", 60, 72))
+    tt(r("ct", 132, 144), r("ct", 60, 72), r("ct", 108, 120), ALU.add)
+    cp(r("oG"), r("ct", 132, 144))
     ts(r("ct", 72, 84), r("ct", 60, 72), 32.0, ALU.mult, par, ALU.add)
-    tt(r("ct", 84, 96), r("ct", 72, 84), r("t1", 0, 12), ALU.add)
-    cp(r("oN2"), r("ct", 84, 96))
-    ts(r("dW"), r("ct", 36, 48), float(NM), ALU.add)
-    ts(r("dC"), r("ct", 36, 48), float(NM + LN), ALU.add)
-    ts(r("dA"), r("ct", 36, 48), float(NM + LN + TW), ALU.add)
+    tt(r("ct", 84, 96), r("ct", 72, 84), r("t1"), ALU.add)
+    tt(r("ct", 72, 84), r("ct", 84, 96), r("ct", 96, 108), ALU.add)
+    cp(r("oN2"), r("ct", 72, 84))
+    ms(r("dS"), 0.0)
+    ms(r("nlf"), 0.0)
+    for x, v in ((r("dS", 0, 12), NM), (r("dS", 12, 24), NM + LN), (r("dS", 24, 36), NM + LN + TW), (r("thX"), 2 ** 19 + NM + LN)):
+        ts(x, r("ct", 120, 132), p16, ALU.add, float(v), ALU.add)
+    if CFG["wide"]:
+        ts(r("tF", 0, 4), r("ct", 120, 124), p16, ALU.add)
+        ts(r("t2"), r("tF", 0, 4), -5.5, ALU.add, 1.0 / 12.0, ALU.mult)
+        ts(r("tF", 4, 8), r("t2"), -12.0, ALU.mult)
+        tt(r("tF", 8, 12), r("tF", 4, 8), r("tF", 0, 4), ALU.add)
+        ts(r("oF"), r("tF", 8, 12), 16.0, ALU.mult, 15.0, ALU.add)
     cp(r("nmf"), r("nmi"))
     act(r("X1"), (r("nmf"), r("oN1")))
     turn(r("X2"), r("X1"))
-    act(r("Lf0"), (r("X2"), r("oN2")))
-    cp(r("off0"), r("Lf0"))
+    act(r("Lf"), (r("X2"), r("oN2")))
+    cp(r("off0"), r("Lf"))
     for m in range(16):
         iota(r("wr", m, m + 1), [[0, 1]], WT[m], 0)
-    iota(r("dg"), [[0, 2], [1, 16]], 0, 0)
+    iota(r("dg"), [[1, 16]], 0, 0)
     for m in range(16):
-        iota(r("kap", 12 * m, 12 * m + 12), [[0, 12]], KA[m], 0)
-    iota(r("K37"), [[1184, 16], [0, 12]], 0, 0)
-    iota(r("cu"), [[0, 16], [256, 12]], 0, 0)
-    iota(r("thX"), [[0, 8], [16, 12]], 2 ** 19 + NM + LN, 0)
+        iota(r("kap", NB * m, NB * m + NB), [[0, NB]], KA[m], 0)
+    iota(r("K37"), [[0, H], [1184, 16], [0, NB]], 0, 0)
+    iota(r("cu"), [[256 * NB, H], [0, 16], [256, NB]], 0, 0)
     iota(r("sm"), [[0, 12], [1, 16]], 0, 0)
     iota(r("zz"), [[0, 192]], 0, 0)
     iota(r("cv", 0, 128), [[16, 8], [0, 16]], 0, 0)
-    iota(r("cv", 128, 152), [[1, 12], [0, 2]], 0, 0)
+    iota(r("cv", 128, 152), [[16 * NB, H], [1, NB], [0, 2]], 0, 0)
     iota(r("cv", 152, 164), [[32, 12]], 0, 0)
     iota(r("IO"), [[1, TW]], 0, 0)
     iota(r("ONE"), [[0, 128]], 1, 0)
-    for nme in ("u", "q", "q2", "m2", "nfD", "zer"):
-        iota(r(nme), [[0, 16]], 0, 0)
-    ts(r("ndg"), r("dg"), p16, ALU.not_equal, HUGE, ALU.mult)
+    for nme in ("u", "zer"):
+        iota(r(nme), [[0, SB[nme][0]]], 0, 0)
     ts(r("dg2"), r("dg"), p16, ALU.is_equal)
-    tt(r("wr"), r("wr"), r("dg2", 0, 16), ALU.mult)
-    red(r("cf", 3, 4), r("wr"))
+    tt(r("wr"), r("wr"), r("dg2"), ALU.mult)
+    red(r("cf", 3, 4), r("wr"), ALU.add)
     ts(r("Zw"), r("ramp"), g16, ALU.is_equal, r("cf", 3, 4), ALU.mult)
     ms(r("h16"), 0.5)
     scan(r("wp"), r("h16"), r("zer"), 2.0, ALU.mult, ALU.add)
-    tt(r("wp"), r("wp"), r("dg2", 0, 16), ALU.mult)
-    red(r("cf", 4, 5), r("wp"))
+    tt(r("wp"), r("wp"), r("dg2"), ALU.mult)
+    red(r("cf", 4, 5), r("wp"), ALU.add)
     ts(r("cf", 5, 6), r("cf", 4, 5), float(2 ** 95), ALU.mult, 65536.0, ALU.mult)
     ms(r("h17"), 1.0 / 65536.0)
     scan(r("wD"), r("h17"), r("zer"), r("cf", 5, 6), ALU.mult, ALU.add)
-    ts(r("tD"), r("wD"), 4.0, ALU.mult)
+    ms(r("hlf"), 0.5)
+    scan(r("th2"), r("hlf"), r("zz"), float(2 ** 97), ALU.mult, ALU.add)
+    ts(r("nd"), r("sm"), p16, ALU.not_equal, HUGE, ALU.mult)
+    tt(r("thM"), r("th2"), r("nd"), ALU.max)
+    act(r("thL"), r("thM"), scale=2.0)
     ts(r("cf", 6, 7), p16, 16.0, ALU.mult)
-    ts(r("cf", 7, 8), p16, 12.0, ALU.mult)
+    ts(r("cf", 7, 8), p16, float(NB), ALU.mult)
     tt(r("cf", 8, 9), p16, par, ALU.add)
     ts(r("cu"), r("cu"), r("cf", 6, 7), ALU.add, 1184.0, ALU.mult)
     tt(r("K37"), r("K37"), r("cu"), ALU.add)
-    ts(r("thX"), r("thX"), p16, ALU.add)
     ts(r("sm"), r("sm"), 0.0, ALU.is_gt)
     ts(r("BO"), r("cv", 0, 128), g16, ALU.is_equal)
     ts(r("oD1"), r("cv", 128, 152), r("cf", 7, 8), ALU.add)
     ts(r("oD2"), r("cv", 152, 164), r("cf", 8, 9), ALU.add)
-    for b in range(12):
-        act(r("thM", 16 * b, 16 * b + 16), r("ndg", 0, 16), bias=r("tD", b, b + 1))
 
     RB = 192.0 - 7.5 / 16.0
-    if CFG["late"]:
-        ms(r("k25"), 25.5)
     c0, hb = 0, 0
     for i, n in enumerate(CH):
         ts(r("F", c0, c0 + n), r("E1", c0, c0 + n), 1.0 / 16.0, ALU.mult, RB, ALU.add)
-        if i in CFG["S1V"]:
-            ts(r("S1", c0, c0 + n), r("E2", c0, c0 + n), 1.0 / 16.0, ALU.mult, RB, ALU.add)
-        else:
-            act(r("S1", c0, c0 + n), r("E2", c0, c0 + n), bias=RB, scale=1.0 / 16.0)
+        act(r("S1", c0, c0 + n), r("E2", c0, c0 + n), bias=RB, scale=1.0 / 16.0)
         tt(r("sel", c0, c0 + n), r("F", c0, c0 + n), r("S1", c0, c0 + n), ALU.is_gt)
         if i in CFG["S2V"]:
             ts(r("S", c0, c0 + n), r("S1", c0, c0 + n), -FO, ALU.add)
         else:
             act(r("S", c0, c0 + n), r("S1", c0, c0 + n), bias=-FO)
         for a in range(c0, c0 + n, 512):
-            b1 = (r("pk"), r("pK"), r("pa", 0, 512), r("pa", 512, 1024))[hb % 4]
-            b2 = (r("pT"), r("pm"), r("pb", 0, 512), r("pb", 512, 1024))[hb % 4]
+            e = min(a + 512, c0 + n)
+            b1 = r(("pk0", "pk1", "pa", "pU")[hb % 4], 0, e - a)
+            b2 = r(("pT", "pm", "pb", "pK")[hb % 4], 0, e - a)
             hb += 1
-            lin(b1, [("I1", r("E1", a, a + 512)), ("In16", r("F", a, a + 512)), ("In16", r("sel", a, a + 512))])
-            if i in CFG["late"]:
-                lin(b2, [("ONE", r("k25")), ("I1", r("E2", a, a + 512)), ("In16", r("S1", a, a + 512)), ("I16", r("sel", a, a + 512))])
-            else:
-                lin(b2, [("I1", r("E2", a, a + 512)), ("I16", r("sel", a, a + 512)), ("In16", r("S", a, a + 512))])
-            act(r("At", a, a + 512), b1, bias=16.0 + 16.0 * FO)
-            tt(r("Y", a, a + 512), b2, r("At", a, a + 512), ALU.max)
+            lin(b1, [("I1", r("E1", a, e)), ("In16", r("F", a, e)), ("In16", r("sel", a, e))])
+            lin(b2, [("I1", r("E2", a, e)), ("I16", r("sel", a, e)), ("In16", r("S", a, e))])
+            act(r("At", a, e), b1, bias=16.0 + 16.0 * FO)
+            tt(r("Y", a, e), b2, r("At", a, e), ALU.max)
         c0 += n
 
-    def tree(src, o, extra):
-        if CFG["reduce"]:
-            hi = 192 if extra is None else 204
-            for b in range(12):
-                oo, ii = r(o[0], b, b + 1), r(src, b, hi, 12)
-                op("V", lambda oo=oo, ii=ii: g.vector.tensor_reduce(ap(oo), ap(ii), AX.X, ALU.min), [oo], [ii], 64 * EST["cyc"])
-            return
-        if extra is None:
-            cp(r("a96"), r(src, 96, 192))
-        else:
-            tt(r("a96"), r(src, 96, 192), extra, ALU.min)
-        tt(r("b96"), r(src, 0, 96), r("a96"), ALU.min)
-        tt(r("a48"), r("b96", 0, 48), r("b96", 48, 96), ALU.min)
-        tt(r("a24"), r("a48", 0, 24), r("a48", 24, 48), ALU.min)
-        tt(o, r("a24", 0, 12), r("a24", 12, 24), ALU.min)
+    def scat(tab, o0, src, s0, b0, b1, step):
+        for a in range(b0, b1, step):
+            e = min(a + step, b1)
+            cp((r(tab), r("so", o0 + a, o0 + e)), r(src, s0 + 16 * a, s0 + 16 * e))
 
-    def scat(tab, o0, src, s0, step):
-        for a in range(0, 12, step):
-            cp((r(tab), r("so", o0 + a, o0 + a + step)), r(src, s0 + 16 * a, s0 + 16 * (a + step)))
+    QW = CW // 4
 
-    def of(nme, k):
-        return r(nme, 48 * k, 48 * k + 48)
+    def of(nme, h, k, n=1):
+        return r(nme, CW * h + QW * k, CW * h + QW * (k + n))
 
-    def gs(k):
-        return r("GB", 768 * k, 768 * k + 768)
+    def gq(nme, h, k, n=1):
+        return r(nme, 16 * CW * h + 16 * QW * k, 16 * CW * h + 16 * QW * (k + n))
 
-    def gf(k):
-        return r("GB", 3072 + 768 * k, 3072 + 768 * k + 768)
+    def bl(nme, h, o=0):
+        return r(nme, o + NB * h, o + NB * h + NB)
+
+    def ln(nme, h, o=0):
+        return r(nme, o + CW * h, o + CW * h + CW)
 
     for t in range(3):
         last = t == 2
-        off, Lf, z = "off%d" % t, "Lf%d" % t, "z%d" % t
+        sep = CFG["sep"] and not last
+        off, z, sz = "off%d" % t, "z%d" % t, "sz%d" % t
+        z1 = r(z, ZP, ZP + LN)
         flagv = LIMS[t] - 12 - 1.0 / 128.0
+        e0 = [0]
+
+        def hits(r0, k0, b, a, e):
+            x = r("EQ", e0[0], e0[0] + e - a)
+            ts(x, r("R", r0 + a, r0 + e), r("nlf", k0 + b, k0 + b + 1), ALU.is_equal, r("wD", b, b + 1), ALU.mult)
+            e0[0] += e - a
+            return x[1]
+        tag[0], tag[1] = "L", t
         if t > 0:
-            op("X", None, [r(off), r(Lf), r(z)], [], 0.0, "arr%d" % t, 14)
+            op("X", None, [r(off), r(z)], [], 0.0, "arr%d" % t, 10)
+            side(r("Lf"), r(off))
         n3 = 0
-        for k in range(4):
-            if CFG["A"][t][k] == 1:
-                tt(gs(k), (r("Y"), of(off, k)), r(z), ALU.subtract)
-                act(gs(k), gs(k), AF.Abs, bias=-YO)
-            elif CFG["A"][t][k] == 4:
-                for a in (0, 24):
-                    h0 = r("GB", 768 * k + 16 * a, 768 * k + 16 * a + 384)
-                    tt(h0, (r("Y"), r(off, 48 * k + a, 48 * k + a + 24)), r(z, 0, 384), ALU.subtract)
-                    act(h0, h0, AF.Abs, bias=-YO)
-            elif CFG["A"][t][k] == 2:
-                pbuf = ("pa", "pb")[n3 % 2]; n3 += 1
-                h0, h1 = r("GB", 768 * k, 768 * k + 384), r("GB", 768 * k + 384, 768 * k + 768)
-                tt(h0, (r("Y"), r(off, 48 * k, 48 * k + 24)), r(z, 0, 384), ALU.subtract)
-                act(h0, h0, AF.Abs, bias=-YO)
-                act(h1, (r("Y"), r(off, 48 * k + 24, 48 * k + 48)))
-                lin(r(pbuf, 0, 384), [("In", r(z, 0, 384)), ("I1", h1)])
-                act(h1, r(pbuf, 0, 384), AF.Abs, bias=-YO)
+        for h in range(H):
+            pk = "pk%d" % h
+            zh = r(z, 4 * CW * h, 4 * CW * h + 4 * CW)
+            tag[0] = "A%d" % h
+            way = CFG["A"][t][h]
+            for k in range(4):
+                x = gq("GA", h, k)
+                if way[k] == "b":
+                    tt(x, (r("Y", 0, NM), of(off, h, k)), zh, ALU.subtract)
+                    act(x, x, AF.Abs, bias=-YO)
+                else:
+                    if way[k] == "d":
+                        n = 2 if way[k + 1:k + 2] == "D" else 1
+                        act(gq("GA", h, k, n), (r("Y", 0, NM), of(off, h, k, n)))
+                    for a in range(0, 4 * CW, 384):
+                        pbuf = r(CFG["dbank"][n3 % 2], 0, 384); n3 += 1
+                        xa = r("GA", x[1] + a, x[1] + a + 384)
+                        lin(pbuf, [("In", r(z, zh[1] + a, zh[1] + a + 384)), ("I1", xa)])
+                        act(xa, pbuf, AF.Abs, bias=-YO)
+            mm(r(pk, 0, CW), r("If"), ln("Lf", h), True, False)
+            for i, (k, n) in enumerate(CFG["Aseg"]):
+                seg(r(pk, QW * k, QW * (k + n)), "Zn", gq("GA", h, k), 16 * QW * n, False, i == len(CFG["Aseg"]) - 1)
+            tag[0] = "U%d" % h
+            for b in range(NB):
+                red(r("k12", NB * h + b, NB * h + b + 1), r(pk, b, CW, NB), ALU.min)
+            ts(bl("wi", h), bl("k12", h), 4095, ALU.bitwise_and)
+            cp(bl("woff", h), bl("wi", h))
+            W = bl("woff", h)
+            if CFG["ywA"]:
+                act(ln("yw", h), (r("Y", 0, NM), W))
             else:
-                pbuf = ("pa", "pb")[n3 % 2]; n3 += 1
-                act(gs(k), (r("Y"), of(off, k)))
-                for a, b in ((0, 512), (512, 768)):
-                    lin(r(pbuf, a, b), [("In", r(z, a, b)), ("I1", r("GB", 768 * k + a, 768 * k + b))])
-                act(gs(k), r(pbuf, 0, 768), AF.Abs, bias=-YO)
-        mm(r("pk", 0, 192), r("If"), r(Lf), True, False)
-        for i, k in enumerate(CFG["Aord"][t]):
-            seg(r("pk", 48 * k, 48 * k + 48), "Zn", ("GB", 768 * k), 768, False, i == 3)
-        tree("pk", r("k12"), None)
-        ts(r("wi"), r("k12"), 4095, ALU.bitwise_and)
-        cp(r("woff"), r("wi"))
-        W = r("woff")
-        cp(r("yw"), (r("Y"), W))
-        act(r("FS", 0, 192), (r("F"), W), bias=-FO)
-        act(r("FS", 192, 384), (r("S"), W))
-        seg(r("pT", 0, 12), "Zw", ("yw", 0), 192, True, True)
-        lin(r("pm", 0, 192), [("In", r(z, 0, 192)), ("I1", r("yw"))])
-        cp(r("nlf", 0, 12), r("wi"))
-        cp(r("R", 0, 192), (r("IO"), W))
-        ts(r("ui"), r("pT", 0, 12), -YO * sum(WT), ALU.add)
-        ts(r("u", 0, 12), r("ui"), 4095, ALU.bitwise_and)
-        ts(r("FS2", 0, 192), r("FS", 0, 192), flagv, ALU.min)
-        ts(r("FS2", 192, 384), r("FS", 192, 384), flagv, ALU.min)
-        tt(r("u2"), r("u", 0, 12), r("u", 0, 12), ALU.mult)
-        tt(r("ku"), (r("u"), r("oE")), r("kap"), ALU.mult)
-        ts(r("q", 0, 12), r("u2"), 5, ALU.arith_shift_right)
-        kn = "ku"
-        if t > 0:
-            ts(r("ku2"), r("ku"), r("Acol"), ALU.add)
-            kn = "ku2"
-        for a, b in CFG["csplit"]:
-            tt(r("c1", a, b), (r("q"), r("oE", a // 16, b // 16)), r(kn, a, b), ALU.add)
-            ts(r("c2", a, b), r("c1", a, b), 4095, ALU.bitwise_and)
-            cp(r("coff", a, b), r("c2", a, b))
-        act(r("sz%d" % t), r("pm", 0, 192), AF.Abs, bias=-YO)
-        for pbuf, s0 in (("pa", 0), ("pb", 192)):
-            for a, b, s in ((0, 192, 0), (192, 384, 0), (384, 512, 0), (512, 576, 128), (576, 768, 0)):
-                mm(r(pbuf, a, b), r("I1"), r("FS2", s0 + s, s0 + s + b - a), True, True)
-        act(r("FW4"), r("pa", 0, 768))
-        lin(r("pm", 0, 192), [("I1", r("FS2", 0, 192)), ("I1", r("FS2", 192, 384))])
-        act(r("flag"), r("pm", 0, 192), AF.Relu, bias=0.5 - 2 * flagv)
-        mm(r("pm", 0, 192), r("BO"), r("flag"), True, True)
-        mm(r("pm", 192, 384), r("BO"), r("flag"), True, True)
-        seg(r("pm", 384, 396), "Z1", ("flag", 0), 192, True, True)
-        act(r("nfD", 0, 12), r("pm", 384, 396), AF.Relu, bias=1.0, scale=-4.0)
-        if not last:
-            act(r("nfB"), r("pm", 384, 396), AF.Relu, bias=16384.0, scale=-65536.0)
-        act(r("nfX"), (r("nfD"), r("oE")))
-        act(r("nf"), r("pm", 0, 384), AF.Relu, bias=1.0, scale=-4.0)
-        cp(r("cfl"), r("c2"))
-        if CFG["reduce"]:
-            mm(r("pK", 192, 204), r("If"), r("thX", 0, 12), True, True)
-        mm(r("pK", 0, 192), r("If"), r("cfl"), True, False)
-        mm(r("pK", 0, 192), r("Inf"), r("nfX"), False, False)
-        ts(r("m1"), r("u", 0, 12), 1023, ALU.bitwise_and)
-        ts(r("m2", 0, 12), r("m1"), 2.0, ALU.mult, 33.0, ALU.add)
-        tt(r("p1"), (r("m2"), r("oE")), r(Lf), ALU.mult)
+                cp(ln("yw", h), (r("Y", 0, NM), W))
+            act(ln("W2", h), (r("F", 0, NM), W), bias=-FO)
+            act(ln("W2", h, LN), (r("S", 0, NM), W))
+            seg(r(pk, 256, 256 + NB), "Zw", ("yw", CW * h), CW, True, True)
+            uh, qh = r("u", 16 * h, 16 * h + NB), r("q", 16 * h, 16 * h + NB)
+            ts(bl("ui", h), r(pk, 256, 256 + NB), -YO * sum(WT), ALU.add)
+            ts(uh, bl("ui", h), 4095, ALU.bitwise_and)
+            tt(bl("u2", h), uh, uh, ALU.mult)
+            tt(ln("ku", h), (uh, bl("oE", h)), r("kap"), ALU.mult)
+            ts(qh, bl("u2", h), 1.0 / 32.0, ALU.mult, r("Acol") if t > 0 else -0.375, ALU.add)
+            tt(ln("c1", h), (qh, bl("oE", h)), ln("ku", h), ALU.add)
+            ts(ln("c2", h), ln("c1", h), 4095, ALU.bitwise_and)
+            cp(ln("coff", h), ln("c2", h))
+            side(ln("cfl", h), ln("c2", h))
+            for nme, n, o in (("FW", RF, 0), ("SW", RS, LN)):
+                a = CW * n * h
+                for k in range(n):
+                    if nme not in CFG["G"] or k == 0:
+                        ts(r(nme, a + CW * k, a + CW * (k + 1)), ln("W2", h, o), flagv, ALU.min)
+                    elif k in (1, 2):
+                        side(r(nme, a + CW * k, a + CW * 2 * k), r(nme, a, a + CW * k))
+            tag[0] = "R%d" % h
+            side(bl("nlf", h), bl("wi", h))
+            cp(ln("R", h), (r("IO"), W))
+            tag[0] = "G%d" % h
+            lin(r("pm", 0, CW), [("I1", r("FW", CW * RF * h, CW * RF * h + CW)), ("I1", r("SW", CW * RS * h, CW * RS * h + CW))])
+            act(ln("flag", h), r("pm", 0, CW), AF.Relu, bias=0.5 - 2 * flagv)
+            seg(r("pm", 256, 256 + NB), "Z1", ("flag", CW * h), CW, True, True)
+            act(bl("nfD", h), r("pm", 256, 256 + NB), AF.Relu, bias=1.0, scale=-4.0)
+            if not last:
+                act(bl("nfB", h), r("pm", 256, 256 + NB), AF.Relu, bias=16384.0, scale=-65536.0)
+            zl = r(z, 4 * CW * h, 4 * CW * h + CW)
+            for k in range(H):
+                lin(r("pa", CW * k, CW * k + CW), [("I1", ln("yw", h)), ("In", zl)])
+            tag[0] = "Z%d" % h
+            act(r(sz, H * CW * h, H * CW * (h + 1)), r("pa", 0, H * CW), AF.Abs, bias=-YO)
+            if sep:
+                act(ln("D", h), r("pa", 0, CW), bias=-YO)
+        tag[0] = "W"
+        same = {b: hits(0, 0, b, 16 * b, LN) for b in range(12)}
+        if sep:
+            for b in range(12):
+                mm(r("pT", 256 + 16 * b, 256 + LN), r("BO"), r("EQ", same[b], same[b] + LN - 16 * b), b == 0, b == 11)
+            tt(r("f1"), r("pT", 256, 256 + LN), r("thM"), ALU.is_ge)
+            scan(r("f1s"), r("sm"), r("f1"), 0.0, ALU.mult, ALU.max)
+            tt(r("ya"), r("f1s", 15, LN, 16), r("nfD"), ALU.is_ge)
+            tt(r("yb"), r("ya"), r("dS", 0, 12), ALU.mult)
+            tt(r("yc"), r("yb"), r("nlf", 0, 12), ALU.max)
+            cp(r("sy"), r("yc"))
+        tag[0] = "N"
+        ue = 16 * (H - 1) + NB
+        ts(r("m1", 0, ue), r("u", 0, ue), 1023, ALU.bitwise_and)
+        ts(r("m2", 0, ue), r("m1", 0, ue), 2.0, ALU.mult, 33.0, ALU.add)
+        tt(r("p1"), (r("m2", 0, ue), r("oG")), r("Lf"), ALU.mult)
         tt(r("p2"), r("p1"), r("K37"), ALU.add)
         ts(r("p3"), r("p2"), 5, ALU.arith_shift_right, 4095, ALU.bitwise_and)
-        cp(r("sl%d" % t), r("p3"))
         if not last:
-            cp(r("so%d" % t), r("p3"))
+            side(r("so%d" % t), r("p3"))
             dst = T.cores[(rank + STEP) % N]
             rid, pid, _s = topo.addr(dst)
             en = topo.engines(core, dst)
-            prs = [(r("so%d" % t), r("off%d" % (t + 1))), (r("sl%d" % t, 0, 96), r("Lf%d" % (t + 1), 0, 96)),
-                   (r("sl%d" % t, 96, 192), r("Lf%d" % (t + 1), 96, 192))]
-            prs += [(r("sz%d" % t), r("z%d" % (t + 1), 192 * k, 192 * k + 192)) for k in range(4)]
+            prs = [(r("so%d" % t), r("off%d" % (t + 1)))]
+            prs += [(r(sz, LN * (k * H // 4), LN * (k * H // 4) + LN), r("z%d" % (t + 1), LN * k, LN * k + LN)) for k in range(4)]
 
             def send(prs=prs, rid=rid, pid=pid, en=en, t=t):
                 tr = [RemoteDMATransfer(dst_ids=[DstId(rid=rid, pnc=pid)],
@@ -458,129 +488,104 @@ def build(T, g, core, topo):
                                         remote_sem=T.sem["arr%d" % (t + 1)], src=ap(a), dst=ap(b))
                       for k, (a, b) in enumerate(prs)]
                 g.remote_dma_fused(tr, local_sem=T.sem.sent)
-            op("R", send, [], [a for a, b in prs], 500.0, "sent", 14, EST["remote"])
+            op("R", send, [], [a for a, b in prs], 500.0, "sent", 2 * len(prs), EST["remote"])
         else:
-            store(T.yz[:], r("sz2"), "s0")
+            side(r("sl2"), r("p3"))
+            store(T.yz[:], r(sz, SP, SP + LN), "s0")
             act(r("X1"), (r("sl2"), r("oD1")))
             turn(r("X2"), r("X1"))
             act(r("ynf"), (r("X2"), r("oD2")))
             store(T.yn[:], r("ynf"), "s3")
-        for k in range(4):
-            cut = min(max(int(48 * CFG["C"]) - 48 * k, 0), 48)
-            if cut > 0:
-                tt(r("GB", 768 * k, 768 * k + 16 * cut), (r("S"), r("coff", 48 * k, 48 * k + cut)), r("FW4", 0, 16 * cut), ALU.min)
-            if cut < 48:
-                rest = r("GB", 768 * k + 16 * cut, 768 * k + 768)
-                act(rest, (r("S"), r("coff", 48 * k + cut, 48 * k + 48)))
-                tt(rest, rest, r("pa", 16 * cut, 768), ALU.min)
-            act(gf(k), (r("F"), of("coff", k)), bias=-FO)
-            tt(gf(k), gf(k), r("pb", 0, 768), ALU.min)
-        mm(r("pk", 0, 192), r("I1"), r("zz"), True, False)
-        for i, (j, n) in enumerate(CFG["Cord"]):
-            seg(r("pk", 48 * (j % 4), 48 * (j % 4 + n)), "Zp", ("GB", 768 * j), 768 * n, False, i == len(CFG["Cord"]) - 1)
-        MG = 1.5 * 2 ** 27
-        ts(r("rr"), r("pk", 0, 192), MG, ALU.add, -MG, ALU.add)
-        tt(r("dd"), r("rr"), r("pk", 0, 192), ALU.subtract)
-        mm(r("pK", 0, 192), r("I512"), r("rr"), False, False)
-        mm(r("pK", 0, 192), r("Ipen"), r("dd"), False, True)
-        tree("pK", r("k12"), r("thX"))
-        ts(r("cn"), r("k12"), 8191, ALU.bitwise_and)
-        cp(r("nlf", 12, 24), r("cn"))
-        cp(r("cno"), r("cn"))
-        cp(r("R", 192, 384), (r("IO"), r("cno")))
-        nf1, fw, sw, z1 = r("nf", 0, 192), r("FS", 0, 192), r("FS", 192, 384), r(z, 0, 192)
-        act(r("EW", 0, 192), (r("E1"), W))
-        act(r("EW", 192, 384), (r("E2"), W))
-        lin(r("pm", 0, 192), [("I1", z1), ("I16", nf1)])
-        lin(r("pm", 192, 384), [("I1", r("yw")), ("In16", nf1)])
-        act(r("r12", 0, 192), r("pm", 0, 192), AF.Relu, bias=-16.0)
-        act(r("r12", 192, 384), r("pm", 192, 384), AF.Relu, bias=-YO)
-        lin(r("pm", 0, 192), [("I1", r("r12", 0, 192)), ("I1", r("r12", 192, 384))])
-        act(r("vv"), r("pm", 0, 192), bias=YO)
-        lin(r("pa", 0, 384), [("In16", r("FS")), ("In", r(z, 0, 384)), ("I1", r("EW"))])
+        tag[0] = "V"
+        nf, fw, sw, W = r("nf"), r("W2", 0, LN), r("W2", LN, 2 * LN), r("woff")
+        mm(r("pb", 0, LN), r("BO"), r("flag"), True, True)
+        act(nf, r("pb", 0, LN), AF.Relu, bias=1.0, scale=-4.0)
+        lin(r("pb", 0, LN), [("I1", r("yw")), ("In", z1), ("I64", nf)])
+        act(r("rv"), r("pb", 0, LN), AF.Relu, bias=-YO - 48.0)
+        if sep:
+            act(r("vv"), z1, bias=YO)
+        tag[0] = "I"
+        act(r("EW", 0, LN), (r("E1", 0, NM), W))
+        act(r("EW", LN, 2 * LN), (r("E2", 0, NM), W))
+        lin(r("pa", 0, 384), [("In16", r("W2")), ("In", z1), ("I1", r("EW"))])
         act(r("ab"), r("pa", 0, 384), AF.Abs, bias=-192.0)
-        act(r("sat"), r("FS"), AF.Relu, bias=-2.0)
+        act(r("sat"), r("W2"), AF.Relu, bias=-2.0)
         act(r("bb"), r("ab"), AF.Relu, bias=1.0, scale=-1.0)
-        C = r("cno")
-        yc, fc, scn = r("C3", 0, 192), r("C3", 192, 384), r("C3", 384, 576)
-        act(scn, (r("S"), C))
-        act(yc, (r("Y"), C))
-        act(fc, (r("F"), C), bias=-FO)
-        lin(r("pa", 512, 896), [("I1", r("nf")), ("In", r("sat")), ("In", r("bb"))])
-        act(r("inc"), r("pa", 512, 896), AF.Relu)
-        lin(r("pb", 0, 192), [("In", sw), ("In512", nf1), ("I1", scn)])
-        act(r("se"), r("pb", 0, 192), AF.Relu, bias=16.0)
-        lin(r("pb", 512, 704), [("I1", sw), ("I16", nf1), ("I1", r("inc", 192, 384)), ("I1", r("se"))])
-        act(r("FN", 192, 384), r("pb", 512, 704), bias=-16.0)
+        lin(r("pb", 0, 384), [("In", r("sat")), ("I1", nf), ("In", r("bb"))])
+        act(r("inc"), r("pb", 0, 384), AF.Relu)
+        lin(r("pb", 0, LN), [("I1", sw), ("I1", r("inc", LN, 2 * LN))])
+        act(r("S", NM + LN, TW), r("pb", 0, LN))
         if not last:
-            lin(r("pm", 0, 192), [("I1", sw), ("In", r("yw")), ("In512", nf1)])
-            act(r("ra"), r("pm", 0, 192), AF.Relu, bias=256.0)
-            lin(r("pm", 0, 192), [("I256", nf1), ("I1", r("vv")), ("I1", r("ra"))])
-            act(r("vA"), r("pm", 0, 192), bias=-256.0)
-            lin(r("pa", 0, 192), [("I1", fw), ("I256", nf1), ("I1", r("inc", 0, 192))])
-            act(r("rb", 0, 192), r("pa", 0, 192), AF.Relu, bias=FO - 256.0)
-            lin(r("pa", 192, 384), [("In512", nf1), ("I16", fc), ("I1", yc)])
-            act(r("rb", 192, 384), r("pa", 192, 384), AF.Relu, bias=-16.0)
-            lin(r("pa", 0, 192), [("I1", r("rb", 0, 192)), ("I1", r("rb", 192, 384))])
-            act(r("vB"), r("pa", 0, 192))
-        lin(r("pb", 192, 384), [("I16", sw), ("I1", yc)])
-        lin(r("pb", 0, 192), [("I1", r("vv")), ("I16", r("FN", 192, 384))])
-        up[0] = CFG["up"][t]
-        act(r("EN2"), r("pb", 0, 384), bias=-16.0)
-        up[0] = 0.0
-        if last:
-            lin(r("pa", 704, 896), [("I16", fc), ("I1", yc)])
-        lin(r("pa", 512, 704), [("I16", fw), ("I1", r("vv")), ("I16", r("inc", 0, 192))])
-        ne = 384 if last else 192
-        act(r("EN1", 0, ne), r("pa", 512, 512 + ne), bias=-16.0)
-        e0 = 0
-        for kind, (r0, k0) in enumerate(((0, 0), (0, 12), (192, 0), (192, 12))):
-            for b in range(12):
-                n = 192 - 16 * b
-                ts(r("EQ", e0, e0 + n), r("R", r0 + 16 * b, r0 + 192), r("nlf", k0 + b, k0 + b + 1), ALU.is_equal,
-                   r("wD", b, b + 1), ALU.mult)
-                mm(r("pT", 16 * b, 192), r("BO"), r("EQ", e0, e0 + n), kind == 0 and b == 0, kind == 3 and b == 11)
-                e0 += n
-        ts(r("nh"), r("cn"), float(NM), ALU.is_ge)
-        tt(r("y1"), r("nh"), r("nfD", 0, 12), ALU.subtract)
-        tt(r("y2"), r("y1"), r("dW"), ALU.mult)
-        tt(r("wX"), r("y2"), r("nlf", 0, 12), ALU.max)
-        tt(r("fail"), r("pT", 0, 192), r("thM"), ALU.is_ge)
-        scan(r("fsc"), r("sm"), r("fail"), 0.0, ALU.mult, ALU.max)
-        fD = r("fsc", 15, 192, 16)
-        sw_, sc_ = r("so", 0, 12), r("so", 12, 24)
-        if not last:
-            ts(r("la1"), r("cn"), float(TW), ALU.add)
-            tt(r("la2"), r("la1"), r("nfB"), ALU.subtract)
-            tt(r("la3"), r("la2"), r("nlf", 0, 12), ALU.max)
-            tt(r("fd", 24, 36), fD, r("dA"), ALU.mult)
-            tt(r("of", 24, 36), r("fd", 24, 36), r("la3"), ALU.max)
-            cp(r("so", 24, 36), r("of", 24, 36))
-        tt(r("fd", 0, 12), fD, r("dW"), ALU.mult)
-        tt(r("of", 0, 12), r("fd", 0, 12), r("wX"), ALU.max)
-        cp(sw_, r("of", 0, 12))
-        tt(r("fd", 12, 24), fD, r("dC"), ALU.mult)
-        tt(r("of", 12, 24), r("fd", 12, 24), r("nlf", 12, 24), ALU.max)
-        cp(sc_, r("of", 12, 24))
-        if not last:
-            scat("YS", 24, "vA", 0, 12)
-            scat("FE", 24, "vB", 0, CFG["pf"])
-            scat("S", 0, "FN", 192, CFG["pf"])
-            tt(r("mx"), fD, r("nh"), ALU.max)
-            mm(r("pm", 0, 12), r("ONE"), r("mx"), True, True)
-            act(r("ajk"), r("pm", 0, 12), bias=128.0, scale=-1.0, acc=r("Acol"))
-        if last:
-            cp((r("E2"), r("so", 0, 24)), r("EN2"))
-        else:
-            scat("E2", 0, "EN2", 0, CFG["pe"])
-            scat("E2", 12, "EN2", 192, CFG["pe"])
+            lin(r("pm", 0, LN), [("I1", fw), ("I1", r("inc", 0, LN))])
+            act(r("Y", NM + LN, TW), r("pm", 0, LN), bias=FO + 16.0)
+        if not last and not sep:
+            lin(r("pm", 0, LN), [("I1", z1), ("In", sw), ("I256", nf)])
+            act(r("ra"), r("pm", 0, LN), AF.Relu, bias=YO - 256.0)
+            lin(r("pm", 0, LN), [("I1", sw), ("I1", r("ra"))])
+            act(r("vA"), r("pm", 0, LN))
+        lin(r("pa", 0, LN), [("I16", fw), ("I1", r("yw")), ("In", r("rv")), ("I16", nf), ("I16", r("inc", 0, LN))])
+        act(r("EN1", 0, LN), r("pa", 0, LN), bias=-16.0)
+        kill = {}
+        MG = 1.5 * 2 ** 27
+        for h in range(H):
+            pk, kb = "pk%d" % h, 256 * h
+            tag[0] = "C%d" % h
+            fwh = r("FW", CW * RF * h, CW * RF * (h + 1))
+            swh = r("SW", CW * RS * h, CW * RS * (h + 1))
+            for k in range(4):
+                x = gq("GS", h, k)
+                if CFG["C"][h][k] == "f":
+                    act(x, (r("S", 0, NM), of("coff", h, k)))
+                for a in range(0, 4, RF):
+                    xa = r("GS", x[1] + CW * a, x[1] + CW * (a + RF))
+                    o = of("coff", h, k)
+                    oa = r("coff", o[1] + NB * a, o[1] + NB * (a + RF))
+                    tt(xa, (r("S", 0, NM), oa) if CFG["C"][h][k] == "e" else xa, fwh, ALU.min)
+            for k in range(0, 4, CFG["Fw"]):
+                x = gq("GF", h, k, CFG["Fw"])
+                act(x, (r("F", 0, NM), of("coff", h, k, CFG["Fw"])), bias=-FO)
+                for a in range(0, width(x), CW * RS):
+                    xa = r("GF", x[1] + a, x[1] + a + CW * RS)
+                    tt(xa, xa, swh, ALU.min)
+            ext = r("pK", kb + CW, kb + CW + NB)
+            lin(ext, [("If", bl("thX", h)), ("Inf", bl("nfD", h))])
+            mm(r("pK", kb, kb + CW), r("If"), ln("cfl", h), True, False)
+            whole = CFG["Cseg"][0][2] == 4
+            if not whole:
+                mm(r(pk, 0, CW), r("I1"), r("zz", 0, CW), True, False)
+            for i, (gb, k, n) in enumerate(CFG["Cseg"]):
+                seg(r(pk, QW * k, QW * (k + n)), "Zp", gq(gb, h, k), 16 * QW * n, whole and i == 0, i == len(CFG["Cseg"]) - 1)
+            tag[0] = "K%d" % h
+            ts(ln("rr", h), r(pk, 0, CW), MG, ALU.add, -MG, ALU.add)
+            tt(ln("dd", h), ln("rr", h), r(pk, 0, CW), ALU.subtract)
+            mm(r("pK", kb, kb + CW), r("I512"), ln("rr", h), False, False)
+            mm(r("pK", kb, kb + CW), r("Ipen"), ln("dd", h), False, True)
+            for b in range(NB):
+                red(r("kc", NB * h + b, NB * h + b + 1), r("pK", kb + b, kb + CW + NB, NB), ALU.min)
+            ts(bl("cn", h), bl("kc", h), 8191, ALU.bitwise_and)
+            cp(bl("nlf", h, 28), bl("cn", h))
+            cp(bl("cno", h), bl("cn", h))
+            for b in range(NB * h, NB * h + NB):
+                kill[b] = hits(0, 28, b, 16 * b, LN)
+                if sep:
+                    for h2 in range(h, H):
+                        a, e = max(16 * b, CW * h2), CW * h2 + CW
+                        mm(r(("pT", "pU")[h2], a - CW * h2, CW), r("BO"), r("EQ", kill[b] + a - 16 * b, kill[b] + e - 16 * b),
+                           b == 0, b == NB * h2 + NB - 1)
+            calls = (cp, tt, ts, act, mm, lin, scan, scat)
+            if CFG["vsplit"][t] or h == H - 1:
+                values(t, (h, h + 1) if CFG["vsplit"][t] else (0, H), tag, calls)
+            tag[0] = "K%d" % h
+            if sep:
+                tt(ln("fk", h), r(("pT", "pU")[h], 0, CW), ln("th2", h), ALU.is_ge)
+                tt(ln("gk", h), ln("fk", h), ln("D", h), ALU.mult)
+                tt((r("Y", 0, NM + LN), bl("sy", h)), ln("gk", h), ln("vv", h), ALU.add)
+            cp(ln("R", h, LN), (r("IO"), bl("cno", h)))
+            if CFG["split"][t] or h == H - 1:
+                part(t, (h, h + 1) if CFG["split"][t] else (0, H), same, kill, hits, tag, calls)
+        tag[0] = "end"
         if last:
             store(T.ys[:], r("E2", 0, NM), "s1")
-        if last:
-            cp((r("E1"), r("so", 0, 24)), r("EN1"))
-        else:
-            scat("E1", 0, "EN1", 0, CFG["pe"])
-        if last:
             tt(r("fo"), r("E1", 0, 768), r("E1", 768, 1536), ALU.add)
             for j in range(24, 64):
                 mm(r("pm", 0, 64), r("I1"), r("E1", 64 * j, 64 * j + 64), j == 24, False)
@@ -591,9 +596,106 @@ def build(T, g, core, topo):
     return ops
 
 
+def values(t, hs, tag, c):
+    cp, tt, ts, act, mm, lin, scan, scat = c
+    last = t == 2
+    tag[0] = "X%d" % hs[0]
+    b0, b1 = NB * hs[0], NB * hs[1]
+    l0, l1 = 16 * b0, 16 * b1
+    n = l1 - l0
+
+    def bl(nme, o=0):
+        return r(nme, o + b0, o + b1)
+
+    def ln(nme, o=0):
+        return r(nme, o + l0, o + l1)
+    C = bl("cno")
+    nf, sw = ln("nf"), ln("W2", LN)
+    yc, fc = ln("C3"), ln("C3", LN)
+    act(yc, (r("Y"), C))
+    act(ln("SN"), (r("S"), C))
+    act(fc, (r("F"), C), bias=-FO)
+    lin(r("pb", n, 2 * n), [("I16", sw), ("I1", yc)])
+    lin(r("pb", 0, n), [("I1", ln("yw")), ("In", ln("rv")), ("I16", nf), ("I16", ln("SN"))])
+    act(r("EN2", 2 * l0, 2 * l1), r("pb", 0, 2 * n), bias=-16.0)
+    lin(r("pa", 0, n), [("I16", fc), ("I1", yc)])
+    act(ln("EN1", LN), r("pa", 0, n), bias=-16.0)
+
+
+def part(t, hs, same, kill, hits, tag, c):
+    cp, tt, ts, act, mm, lin, scan, scat = c
+    last = t == 2
+    sep = CFG["sep"] and not last
+    b0, b1 = NB * hs[0], NB * hs[1]
+    l0, l1 = 16 * b0, 16 * b1
+    n = l1 - l0
+
+    def bl(nme, o=0):
+        return r(nme, o + b0, o + b1)
+
+    def ln(nme, o=0):
+        return r(nme, o + l0, o + l1)
+    tag[0] = "Q%d" % hs[0]
+    bank, o = ("pT", 256) if sep else (("pT", "pU")[hs[0]], 0)
+    if sep:
+        mm(r(bank, o, o + n), r("Ihg"), ln("f1"), True, False)
+        mm(r(bank, o, o + n), r("Ihg"), ln("fk"), False, False)
+    else:
+        for done in (same, kill):
+            for b in range(b1):
+                a = max(16 * b, l0)
+                mm(r(bank, o + a - l0, o + n), r("BO"), r("EQ", done[b] + a - 16 * b, done[b] + l1 - 16 * b),
+                   done is same and b == 0, False)
+    for k0 in (0, 28):
+        for b in range(b1):
+            a = max(16 * b, l0)
+            x = hits(LN, k0, b, a, l1)
+            mm(r(bank, o + a - l0, o + n), r("BO"), r("EQ", x, x + l1 - a), False, k0 > 0 and b == b1 - 1)
+    ts(bl("nh"), bl("cn"), float(NM), ALU.is_ge)
+    tt(bl("y1"), bl("nh"), bl("nfD"), ALU.subtract)
+    tt(bl("y2"), bl("y1"), bl("dS"), ALU.mult)
+    tt(bl("nlf", 16), bl("y2"), bl("nlf"), ALU.max)
+    tt(ln("fail"), r(bank, o, o + n), ln("thM" if sep else "thL"), ALU.is_ge)
+    scan(ln("fsc"), ln("sm"), ln("fail"), 0.0, ALU.mult, ALU.max)
+    fD = r("fsc", l0 + 15, l1, 16)
+    if not last:
+        ts(bl("la1"), bl("cn"), float(TW), ALU.add)
+        tt(bl("la2"), bl("la1"), bl("nfB"), ALU.subtract)
+        tt(bl("nlf", 40), bl("la2"), bl("nlf"), ALU.max)
+    if n == LN and CFG["wide"]:
+        tt(r("fd"), (r("fsc"), r("oF", 0, 3)), r("dS"), ALU.mult)
+        tt(r("of"), r("fd"), r("nlf", 16, 64), ALU.max)
+        cp(r("so"), r("of"))
+    else:
+        for o in (12, 0) if last else (24, 0, 12):
+            tt(bl("fd", o), fD, bl("dS", o), ALU.mult)
+            tt(bl("of", o), bl("fd", o), bl("nlf", 16 + o), ALU.max)
+            cp(bl("so", o), bl("of", o))
+    if not last:
+        if not sep:
+            scat("YS", 24, "vA", 0, b0, b1, 12)
+        tag[0] = "S"
+        scat("FE", 24, "EN1", LN, b0, b1, CFG["pf"])
+        scat("S", 0, "SN", 0, b0, b1, CFG["pf"])
+        if sep:
+            scat("S", 12, "W2", LN, b0, b1, CFG["pf"])
+        tt(bl("mx"), fD, bl("nh"), ALU.max)
+        if b1 == 12:
+            mm(r("pm", 0, 12), r("ONE"), r("mx"), True, True)
+            act(r("ajk"), r("pm", 0, 12), bias=128.0 - 0.375 / 12, scale=-1.0, acc=r("Acol"))
+    tag[0] = "E"
+    step = 12 if last else CFG["pe"]
+    for h0, h1 in [(h, h + 1) for h in range(hs[0], hs[1])] if CFG["vsplit"][t] else [hs]:
+        scat("E2", 0, "EN2", CW * h0, NB * h0, NB * h1, step)
+        scat("E2", 12, "EN2", CW * h1, NB * h0, NB * h1, step)
+    scat("E1", 0, "EN1", 0, b0, b1, step)
+    if last:
+        scat("E1", 12, "EN1", LN, b0, b1, step)
+
+
 def overlap(x, y):
     if x[0] in PS:
-        return x[1] // 512 <= (y[2] - 1) // 512 and y[1] // 512 <= (x[2] - 1) // 512
+        return True
     return x[1] < y[2] and y[1] < x[2]
 
 
@@ -614,16 +716,13 @@ def plan(ops):
         for x in o["w"]:
             for j, y, wr in hist.get(x[0], []):
                 if overlap(x, y):
-                    same = o["e"] == ops[j]["e"] and (o["e"] == "P" or (CFG["inorder"] and o["e"] in "VA"))
-                    (s if same else d).add(j)
+                    (s if o["e"] == ops[j]["e"] == "P" else d).add(j)
         for x in o["w"]:
             if x[3] == 1:
                 hist[x[0]] = [h for h in hist.get(x[0], []) if not (
                     (x[1] <= h[1][1] and h[1][2] <= x[2]) and x[0] not in PS)]
             if x[0] in PS:
-                hist[x[0]] = [h for h in hist.get(x[0], []) if not (
-                    x[1] // 512 <= h[1][1] // 512 and (h[1][2] - 1) // 512 <= (x[2] - 1) // 512
-                    and (ops[h[0]]["e"] == "P" or h[0] in d))]
+                hist[x[0]] = [h for h in hist.get(x[0], []) if not (ops[h[0]]["e"] == "P" or h[0] in d)]
         for x in o["r"]:
             hist.setdefault(x[0], []).append((i, x, False))
         for x in o["w"]:
@@ -638,68 +737,141 @@ def plan(ops):
             lasts = i
         d.discard(i); s.discard(i)
         deps.append(d); soft.append(s - d)
-    succ = [[] for _ in range(n)]
-    for i in range(n):
-        for j in deps[i] | soft[i]:
-            succ[j].append(i)
+    tail, dfree, t0 = [o["lat"] for o in ops], 0.0, 0.0
+    for i, o in enumerate(ops):
+        if o["e"] == "S":
+            tail[i] = EST["dfix"] + o["lat"] / EST["dbw"]
+            if o["w"]:
+                t0 += o["dur"]
+                dfree = max(dfree, t0 + 0.6 * EST["dfix"]) + o["lat"] / EST["dbw"]
+                tail[i] = dfree + 0.4 * EST["dfix"] - t0
+    units, uof, begin = [], [], []
+    for i, o in enumerate(ops):
+        p = ops[i - 1]
+        if i and o["e"] == p["e"] and o["e"] in CFG["units"] and o["tag"] == p["tag"] and o["w"][0][0] == p["w"][0][0] and (
+                (o["bun"] and o["bun"] == p["bun"]) or (o["e"] == "V" and deps[i] <= deps[i - 1] and begin[-1] + p["dur"] + o["dur"] < 350)):
+            units[-1].append(i)
+            begin.append(begin[-1] + p["dur"])
+        else:
+            units.append([i])
+            begin.append(0.0)
+        uof.append(len(units) - 1)
+    dur = [begin[u[-1]] + ops[u[-1]]["dur"] for u in units]
+    edge = {}
+    for k in range(n):
+        for j in deps[k] | soft[k]:
+            if uof[j] != uof[k]:
+                lag = tail[j] + EST["wake"] if j in deps[k] else (tail[j] if ops[k]["e"] == "X" else 0.0)
+                lag -= dur[uof[j]] - begin[j] - ops[j]["dur"] + begin[k]
+                if ops[j]["e"] == ops[k]["e"]:
+                    lag = max(lag, 0.0)
+                edge[uof[j], uof[k]] = max(edge.get((uof[j], uof[k]), lag), lag)
+    n = len(units)
+    succ, pred = [[] for _ in range(n)], [[] for _ in range(n)]
+    for (j, k), lag in sorted(edge.items()):
+        succ[j].append((k, lag)); pred[k].append((j, lag))
+    tail = [tail[u[-1]] for u in units]
+    qn = [QN[ops[u[0]]["e"]] for u in units]
 
-    def tail(o):
-        return EST["dfix"] + o["lat"] / EST["dbw"] if o["e"] == "S" else o["lat"]
+    def listed(after, before, ready, prio):
+        left = [len(x) for x in before]
+        cand = {q: [] for q in "VAPGSX"}
+        for i in range(n):
+            if left[i] == 0:
+                cand[qn[i]].append(i)
+        free = {q: 0.0 for q in cand}
+        order, end = [], [0.0] * n
+        while len(order) < n:
+            tq, q = min((max(free[q], min(ready[i] for i in l)), q) for q, l in cand.items() if l)
+            l = cand[q]
+            c = max((i for i in l if ready[i] <= tq), key=lambda i: prio[i])
+            hs = [i for i in l if ready[i] > tq and prio[i] > prio[c] and tq + dur[c] - ready[i] > CFG["theta"] * dur[c]]
+            if hs:
+                th = min(ready[i] for i in hs)
+                fit = [i for i in l if ready[i] <= tq and tq + dur[i] * (1 - CFG["theta"]) <= th]
+                if not fit:
+                    free[q] = th
+                    continue
+                c = max(fit, key=lambda i: prio[i])
+            l.remove(c)
+            free[q] = end[c] = tq + dur[c]
+            order.append(c)
+            for k, lag in after[c]:
+                ready[k] = max(ready[k], end[c] + lag)
+                left[k] -= 1
+                if left[k] == 0:
+                    cand[qn[k]].append(k)
+        return order, end
     prio = [0.0] * n
     for i in range(n - 1, -1, -1):
-        o = ops[i]
-        m = tail(o)
-        for k in succ[i]:
-            m = max(m, prio[k] + ((tail(o) + EST["wake"]) if (i in deps[k] or ops[k]["e"] == "X") else 0.0))
-        prio[i] = o["dur"] + m + o["up"] + (CFG["early"].get(o["w"][0][0], 0.0) if o["w"] else 0.0)
-    jit = np.random.RandomState(CFG["seed"]).uniform(0.0, CFG["amp"], n)
-    prio = [p + float(j) for p, j in zip(prio, jit)]
-    left = [len(deps[i] | soft[i]) for i in range(n)]
-    ready = [0.0] * n
-    cand = {q: [] for q in "VAPGSX"}
-    for i in range(n):
-        if left[i] == 0:
-            cand[QN[ops[i]["e"]]].append(i)
-    free = {q: 0.0 for q in cand}
-    dfree = 0.0
-    order = []
-    while len(order) < n:
-        best = None
-        for q, l in cand.items():
-            if l:
-                tq = max(free[q], min(ready[i] for i in l))
-                if best is None or tq < best[0]:
-                    best = (tq, q)
-        tq, q = best
-        l = cand[q]
-        c = max((i for i in l if ready[i] <= tq), key=lambda i: prio[i])
-        hs = [i for i in l if ready[i] > tq and prio[i] > prio[c] and tq + ops[c]["dur"] - ready[i] > CFG["theta"] * ops[c]["dur"]]
-        if hs:
-            th = min(ready[i] for i in hs)
-            fit = [i for i in l if ready[i] <= tq and tq + ops[i]["dur"] * (1 - CFG["theta"]) <= th]
-            if not fit:
-                free[q] = th
-                continue
-            c = max(fit, key=lambda i: prio[i])
-        l.remove(c)
-        o = ops[c]
-        free[q] = tq + o["dur"]
-        if o["e"] == "S":
-            dfree = max(dfree, free[q] + 0.6 * EST["dfix"]) + o["lat"] / EST["dbw"]
-            end = dfree + 0.4 * EST["dfix"]
-        else:
-            end = free[q] + o["lat"]
-        order.append(c)
-        PLAN["end"] = max(PLAN.get("end", 0.0), end)
-        for k in succ[c]:
-            if c in deps[k]:
-                ready[k] = max(ready[k], end + (0.0 if o["e"] == "X" else EST["wake"]))
-            elif ops[k]["e"] == "X":
-                ready[k] = max(ready[k], end)
-            left[k] -= 1
-            if left[k] == 0:
-                cand[QN[ops[k]["e"]]].append(k)
-    return deps, order
+        prio[i] = dur[i] + max([tail[i]] + [prio[k] + lag for k, lag in succ[i]])
+    tags = [ops[u[0]]["tag"] + ops[u[0]]["e"] for u in units]
+    rnd = np.random.RandomState(CFG["seed"])
+    best, cur = None, None
+    for it in range(CFG["turns"]):
+        order, end = listed(succ, pred, [0.0] * n, prio)
+        span = max(e + x for e, x in zip(end, tail))
+        if best is None or span < best[0]:
+            best = (span, order)
+        if cur is None or span < cur + CFG["give"] * rnd.exponential():
+            cur, back = span, listed(pred, succ, list(tail), [e + x for e, x in zip(end, tail)])[1]
+        step = {k: rnd.normal(0.0, CFG["tjit"]) for k in sorted(set(tags))}
+        prio = [b + float(j) + step[k] for b, j, k in zip(back, rnd.uniform(0.0, CFG["jit"], n), tags)]
+    new, cur = best[1], None
+    for it in range(CFG["rounds"]):
+        free, end, ready, span = {q: 0.0 for q in "VAPGSX"}, [0.0] * n, [0.0] * n, 0.0
+        for i in new:
+            m = 0.0
+            for j, lag in pred[i]:
+                if end[j] + lag > m:
+                    m = end[j] + lag
+            ready[i] = m
+            free[qn[i]] = end[i] = max(m, free[qn[i]]) + dur[i]
+            if end[i] + tail[i] > span:
+                span = end[i] + tail[i]
+        if span <= best[0]:
+            best = (span, new)
+            PLAN["span"] = span
+        val = span + CFG["mean"] * sum(end) / n
+        if cur is None or val <= cur + CFG["amp"] * (1.0 - it / CFG["rounds"]) * rnd.exponential():
+            begun = {}
+            for i in new:
+                begun[i] = max([end[i] - dur[i]] + [begun[j] for j, lag in pred[i]])
+            cur, order, seen = val, sorted(new, key=lambda i: begun[i]), (ready, end)
+            late, nxt, held = [0.0] * n, {}, []
+            for a in range(n - 1, -1, -1):
+                i = order[a]
+                m = span - tail[i]
+                for k, lag in succ[i]:
+                    if late[k] - dur[k] - lag < m:
+                        m = late[k] - dur[k] - lag
+                if qn[i] in nxt:
+                    m = min(m, late[nxt[qn[i]]] - dur[nxt[qn[i]]])
+                late[i] = m
+                nxt[qn[i]] = i
+                if m - end[i] < CFG["slack"] and end[i] - dur[i] > ready[i] + 1.0:
+                    held.append(a)
+        b = held[rnd.randint(len(held))] if rnd.uniform() < CFG["crit"] else rnd.randint(1, n)
+        i = order[b]
+        ahead = [a for a in range(max(0, b - 150), b) if qn[order[a]] == qn[i] and seen[1][order[a]] > seen[0][i]]
+        new = order
+        if ahead:
+            a = ahead[rnd.randint(len(ahead))]
+            if rnd.randint(2):
+                moved = {order[a]}
+                for k in order[a + 1:b + 1]:
+                    if any(j in moved for j, lag in pred[k]):
+                        moved.add(k)
+                if i not in moved:
+                    new = order[:a] + [k for k in order[a:b + 1] if k not in moved] + [k for k in order[a:b + 1] if k in moved] + order[b + 1:]
+            else:
+                moved = {i}
+                for k in order[b - 1:a - 1 if a else None:-1]:
+                    if any(j in moved for j, lag in succ[k]):
+                        moved.add(k)
+                if order[a] not in moved:
+                    new = order[:a] + [k for k in order[a:b + 1] if k in moved] + [k for k in order[a:b + 1] if k not in moved] + order[b + 1:]
+    return deps, [i for u in best[1] for i in units[u]]
 
 
 def emit(ops, g, T):

import numpy as np
from concourse.bass import DstId, RemoteDMATransfer
from concourse.mybir import AluOpType as ALU, AxisListType as AX, ActivationFunctionType as AF

N, NM, LN, STEP = 8, 4096, 192, 3
LIMS = (14, 11, 13)
WT = (1, 16, 256, 37, 411, 93, 777, 165, 1029, 251, 1313, 339, 1583, 503, 1847, 618)
KA = (3, 61, 118, 207, 346, 419, 530, 677, 742, 895, 1011, 1164, 1283, 1450, 1629, 1874)
TW = NM + 2 * LN
YO = 208.0
FO = 204.0
CH = (512,) * 8
H = 2
NB = 12 // H
CW = 16 * NB
ZP = 3 * CW * (H - 1)
SP = CW * (H - 1)
RF, RS = 4, 2
HUGE = float(2 ** 99)

B16, F32, I32, U16, F16 = "bfloat16", "float32", "int32", "uint16", "float16"
SB = {
    "FE": (2 * TW, B16), "YS": (2 * TW, B16), "E2": (TW, B16), "IO": (TW, I32),
    "sel": (NM, B16), "At": (NM, B16), "S1": (NM, B16), "GA": (3072, B16), "GS": (3072, B16), "GF": (3072, B16),
    "EQ": (4992, B16),
    "nmi": (192, I32), "nmf": (192, F32), "X1": (384, F32), "X2": (384, F32), "ynf": (192, F32),
    "off0": (192, U16), "off1": (192, U16), "off2": (192, U16), "Lf": (192, F32),
    "z0": (768, B16), "z1": (768, B16), "z2": (768, B16),
    "so0": (192, U16), "so1": (192, U16), "sl2": (192, F32),
    "sz0": (192 * H, B16), "sz1": (192 * H, B16), "sz2": (192 * H, B16),
    "ci": (16, I32), "cj": (16, I32), "cf": (16, F32), "ramp": (144, F32), "r128": (128, F32),
    "ct": (144, F32), "cu": (192, F32), "cv": (192, F32),
    "Z1": (144, B16), "Zn": (144, B16), "Zp": (144, B16), "Zw": (144, F16),
    "I1": (128, B16), "In": (128, B16), "I16": (128, B16), "In16": (128, B16), "I64": (128, B16), "I256": (128, B16),
    "In512": (128, B16), "Ipen": (128, B16), "Inf": (128, B16), "Ihg": (128, B16), "I512": (128, F16), "If": (128, F32),
    "BO": (128, B16), "ONE": (128, B16),
    "dg": (16, F32), "dg2": (16, F32), "wr": (16, F32), "wp": (16, F32), "h16": (16, F32), "h17": (16, F32), "zer": (16, F32),
    "wD": (16, F32), "th2": (192, B16), "thM": (192, B16), "thL": (192, B16), "nd": (192, B16), "hlf": (192, B16),
    "sm": (192, B16), "zz": (192, B16),
    "kap": (CW, F32), "K37": (192, F32), "thX": (12, F32), "dS": (48, F32), "t1": (12, I32), "t2": (4, I32),
    "tF": (12, F32), "oF": (4, U16),
    "oE": (12, U16), "oG": (12, U16), "oN1": (24, U16), "oN2": (12, U16), "oD1": (24, U16), "oD2": (12, U16),
    "k12": (12, I32), "kc": (12, I32), "wi": (12, I32), "woff": (12, U16), "yw": (192, B16), "W2": (384, B16), "EW": (384, B16),
    "FW": (192 * RF, B16), "SW": (192 * RS, B16),
    "ui": (12, I32), "u": (32, I32), "u2": (12, F32), "q": (32, I32), "ku": (192, F32), "c1": (192, I32), "c2": (192, I32),
    "coff": (192, U16), "cfl": (192, F32),
    "m1": (32, I32), "m2": (32, F32), "p1": (192, F32), "p2": (192, I32), "p3": (192, I32),
    "flag": (192, B16), "nf": (192, B16), "nfD": (12, B16), "nfB": (12, F32), "D": (192, B16),
    "rr": (192, F16), "dd": (192, B16), "cn": (12, I32), "nlf": (64, F32), "cno": (12, U16),
    "R": (384, U16), "f1": (192, B16), "f1s": (192, B16), "fk": (192, B16), "gk": (192, B16), "fail": (192, B16), "fsc": (192, B16),
    "ya": (12, F32), "yb": (12, F32), "yc": (12, F32), "sy": (12, U16),
    "nh": (12, F32), "y1": (12, F32), "y2": (12, F32), "la1": (12, F32), "la2": (12, F32),
    "fd": (48, F32), "of": (48, F32), "so": (48, U16), "mx": (12, B16), "Acol": (1, F32), "ajk": (12, F32),
    "C3": (576, B16), "ab": (384, B16), "bb": (384, B16), "sat": (384, B16), "inc": (384, B16),
    "rv": (192, B16), "vv": (192, B16), "se": (192, B16), "SN": (192, B16), "rb": (384, B16), "vB": (192, B16),
    "ra": (192, B16), "vA": (192, B16),
    "EN1": (384, B16), "EN2": (384, B16), "yfs": (64, F32), "fo": (768, F16),
}
PS = {"pa": 512, "pb": 512, "pk0": 512, "pk1": 512, "pK": 512, "pT": 512, "pU": 512, "pm": 512}
HOME = {}
SCRATCH = {}
for _k, (_n, _d) in SB.items():
    if _n > 48:
        HOME[_k] = (_k, 0)
        SCRATCH[_k] = ("sbuf", [128, _n], _d)
    else:
        _o = SCRATCH.get("n" + _d, (0, [128, 0]))[1][1]
        HOME[_k] = ("n" + _d, _o)
        SCRATCH["n" + _d] = ("sbuf", [128, _o + (_n + 15) // 16 * 16], _d)
HOME.update({k: (k, 0) for k in PS})
SCRATCH.update({k: ("psum", [128, v], F32) for k, v in PS.items()})
DMAS = (["dn"] + ["dz%d" % i for i in range(4 * H)] + ["da%d" % i for i in range(len(CH))] + ["db%d" % i for i in range(len(CH))]
        + ["s0", "s1", "s3", "s4"])
SEMAPHORES = ["eV", "eA", "eP", "eG", "arr1", "arr2", "sent"] + DMAS
CFG = {
    "sep": True, "split": (False, False, True), "vsplit": (False, False, True), "wide": True,
    "G": ("Lf", "cfl", "FW", "SW", "nlf", "so0", "so1", "sl2"),
    "A": (("bbbd", "bbbd"), ("bbdD", "bbdD"), ("bbdD", "bbdD")),
    "Aseg": ((0, 2), (2, 2)),
    "C": ("eeff", "eeff"),
    "Cseg": (("GS", 0, 4), ("GF", 0, 2), ("GF", 2, 2)),
    "Fw": 2,
    "S2V": (0, 2, 4, 6, 7),
    "theta": 0.8, "seed": 0, "amp": 0.0,
    "pe": 12, "pf": 12,
    "ywA": True,
    "rounds": 4000, "turns": 60, "jit": 300.0, "units": "P", "give": 1e9, "tjit": 0.0, "mean": 0.0, "crit": 1.0, "slack": 20.0, "dbank": ("pK", "pU"),
}
EST = {"cyc": 0.85, "pe": 0.43, "ga": 1.56, "sc": 3.8, "wake": 210.0, "afix": 60.0, "pefix": 10.0, "pelat": 60.0,
       "dfix": 1800.0, "dbw": 250.0, "remote": 3500.0}


PAIR = {"Y": ("YS", 0), "S": ("YS", TW), "F": ("FE", 0), "E1": ("FE", TW)}


def r(name, a=0, b=None, s=1):
    if name in PAIR:
        h, o = PAIR[name]
        return (h, o + a, o + (TW if b is None else b), s)
    if b is None:
        b = SB[name][0] if name in SB else PS[name]
    return (name, a, b, s)


def width(x):
    return (x[1][2] - x[1][1]) * 16 if len(x) == 2 else len(range(x[1], x[2], x[3]))


def narrow(x):
    n = x[0][0] if len(x) == 2 else x[0]
    return n in SB and SB[n][1] in (B16, U16, F16)


def vcost(o, ins, two=False):
    if len(o) == 2:
        return 50 + width(o) * EST["sc"] * EST["cyc"]
    if ins and len(ins[0]) == 2:
        return 50 + width(o) * EST["ga"] * EST["cyc"]
    h = all(narrow(x) for x in [o] + ins)
    c = 0.5 if h else 1.0
    if two:
        c = 1.0 if (h or any(x[0] in PS for x in ins)) else 2.0
    return max(64, width(ins[0] if ins else o) * c) * EST["cyc"]


def build(T, g, core, topo):
    rank = T.rank_of(core)
    ops = []
    tag = ["start", 0]
    bun = [0]

    def ap(x):
        if len(x) == 2:
            return ap(x[0]).indirect(ap(x[1]))
        h, o = HOME[x[0]]
        return T[h][:, o + x[1]:o + x[2]] if x[3] == 1 else T[h][:, o + x[1]:o + x[2]:x[3]]

    def isref(x):
        return isinstance(x, tuple)

    def op(eng, fn, outs, ins, dur, sem=None, inc=1, lat=0.0):
        w, rd = [], []
        for o in outs:
            if len(o) == 2:
                w.append(o[0]); rd.append(o[1])
            else:
                w.append(o)
        for i in ins:
            if isref(i):
                rd.extend(list(i) if len(i) == 2 else [i])
        ops.append({"e": eng, "f": fn, "w": w, "r": rd, "sem": sem, "inc": inc, "dur": dur, "lat": lat, "tag": tag[0] + str(tag[1]), "bun": bun[0]})

    def sc(x):
        return ap(x) if isref(x) else x

    def cp(o, i):
        op("V", lambda: g.vector.tensor_copy(ap(o), ap(i)), [o], [i], vcost(o, [i]))

    def tt(o, a, b, f):
        op("V", lambda: g.vector.tensor_tensor(ap(o), ap(a), ap(b), f), [o], [a, b], vcost(o, [a, b], True))

    def ts(o, a, s1, f1, s2=None, f2=None):
        if f2 is None:
            op("V", lambda: g.vector.tensor_scalar(ap(o), ap(a), sc(s1), None, f1), [o], [a, s1], vcost(o, [a]))
        else:
            op("V", lambda: g.vector.tensor_scalar(ap(o), ap(a), sc(s1), sc(s2), f1, f2), [o], [a, s1, s2], vcost(o, [a]))

    def ms(o, c):
        op("V", lambda: g.vector.memset(ap(o), c), [o], [], vcost(o, []))

    def red(o, i, f):
        op("V", lambda: g.vector.tensor_reduce(ap(o), ap(i), AX.X, f), [o], [i], 64 * EST["cyc"])

    def turn(o, i):
        op("V", lambda: g.vector.transpose(ap(o), ap(i)), [o], [i], vcost(o, [i]))

    def scan(o, d0, d1, ini, f0, f1):
        op("V", lambda: g.vector.tensor_tensor_scan(ap(o), ap(d0), ap(d1), sc(ini), f0, f1), [o], [d0, d1, ini],
           vcost(o, [d0, d1]))

    def act(o, i, f=AF.Identity, bias=0.0, scale=1.0, acc=None):
        d = EST["afix"] + width(i) * (EST["ga"] if len(i) == 2 else 1.0) * EST["cyc"]
        if acc is None:
            op("A", lambda: g.scalar.activation(ap(o), ap(i), f, bias=sc(bias), scale=sc(scale)), [o], [i, bias, scale], d)
        else:
            op("A", lambda: g.scalar.activation(ap(o), ap(i), f, bias=sc(bias), scale=sc(scale), accum_out=ap(acc)),
               [o, acc], [i, bias, scale], d)

    def mm(o, l, x, st, sp):
        op("P", lambda: g.tensor.matmul(ap(o), ap(l), ap(x), st, sp), [o], [l, x],
           EST["pefix"] + max(64, width(x)) * EST["pe"] * (1 if narrow(x) else 4), lat=EST["pelat"])

    def lin(o, terms):
        n = width(o)
        calls = [(l, x, a) for l, x in terms for a in range(0, n, width(x))]
        bun[0] = len(ops) + 1
        for k, (l, x, a) in enumerate(calls):
            mm(r(o[0], o[1] + a, o[1] + a + width(x)), r(l), x, k == 0, k == len(calls) - 1)
        bun[0] = 0

    def iota(o, pat, base, cm):
        d = 130 + 2 * width(o) * EST["cyc"]
        if SB[o[0]][1] != I32:
            op("G", lambda: g.iota(ap(o), pat, base, cm, allow_small_or_imprecise_dtypes=True), [o], [], d)
        else:
            op("G", lambda: g.iota(ap(o), pat, base, cm), [o], [], d)

    def side(o, i):
        if o[0] not in CFG["G"]:
            return cp(o, i)
        op("G", lambda: g.affine_select(ap(o), ap(i), [[0, width(o)]], ALU.is_ge, 0.0, 0, 0), [o], [i], 170 + 2 * width(o) * EST["cyc"])

    def nbytes(x):
        return 128 * width(x) * (2 if narrow(x) else 4)

    def load(o, src, sem):
        op("S", lambda: g.sync.dma_start(ap(o), src), [o], [], 60.0, sem, 16, nbytes(o))

    def store(dst, i, sem):
        op("S", lambda: g.sync.dma_start(dst, ap(i)), [], [i], 60.0, sem, 16, nbytes(i))

    def seg(o, zname, x0, n, first, last):
        for p in range(16):
            bun[0] = len(ops) - p % 8 + 1
            mm(o, r(zname, 16 - p, 144 - p), r(x0[0], x0[1] + p, x0[1] + n, 16), first and p == 0, last and p == 15)
        bun[0] = 0

    c0 = 0
    for i, n in enumerate(CH):
        load(r("E1", c0, c0 + n), T.pg[:, c0:c0 + n], "da%d" % i)
        load(r("E2", c0, c0 + n), T.pg[:, NM + c0:NM + c0 + n], "db%d" % i)
        if i == 1:
            load(r("nmi"), T.nm[:], "dn")
        c0 += n
    for k in range(4 * H):
        load(r("z0", CW * k, CW * k + CW), T.zv[:, CW * (k // 4):CW * (k // 4) + CW], "dz%d" % k)

    iota(r("r128"), [[1, 128]], 0, -1)
    iota(r("ci", 0, 1), [[0, 1]], 0, 1)
    iota(r("ramp"), [[1, 144]], -16, 0)
    ts(r("cj", 0, 1), r("ci", 0, 1), 112, ALU.bitwise_and)
    ts(r("cj", 1, 2), r("ci", 0, 1), 15, ALU.bitwise_and)
    ts(r("cj", 2, 3), r("ci", 0, 1), 16, ALU.bitwise_and)
    cp(r("cf", 0, 3), r("cj", 0, 3))
    g16, p16, par = r("cf", 0, 1), r("cf", 1, 2), r("cf", 2, 3)
    ts(r("I1"), r("r128"), 0.0, ALU.is_equal)
    ts(r("I16"), r("r128"), 0.0, ALU.is_equal, 16.0, ALU.mult)
    ts(r("In16"), r("r128"), 0.0, ALU.is_equal, -16.0, ALU.mult)
    ts(r("I512"), r("r128"), 0.0, ALU.is_equal, 512.0, ALU.mult)
    for nme in ("E1", "E2", "Y", "F", "S"):
        ms(r(nme, NM, TW), FO if nme == "F" else 0.0)
    ts(r("Z1"), r("ramp"), g16, ALU.is_equal)
    act(r("Zn"), r("Z1"), scale=-4096.0)
    act(r("Zp"), r("Z1"), scale=16.0)
    for nme, v in (("In", -1), ("If", 1), ("I64", 64), ("I256", 256), ("In512", -512), ("Ipen", 2 ** 26), ("Inf", -2 ** 23),
                   ("Ihg", 2 ** 97)):
        act(r(nme), r("I1"), scale=float(v))
    iota(r("ct", 0, 24), [[16, 12], [0, 2]], 0, 0)
    ts(r("oN1"), r("ct", 0, 24), p16, ALU.add)
    iota(r("ct", 24, 36), [[0, H], [16, NB]], 0, 0)
    iota(r("ct", 96, 108), [[32 * NB, H], [0, NB]], 0, 0)
    iota(r("ct", 108, 120), [[16, H], [0, NB]], 0, 0)
    iota(r("ct", 120, 132), [[16, 12]], 0, 0)
    ts(r("ct", 36, 48), r("ct", 24, 36), p16, ALU.add)
    ts(r("t1"), r("ct", 36, 48), -(NB - 1) / 2.0, ALU.add, 1.0 / NB, ALU.mult)
    ts(r("ct", 48, 60), r("t1"), -float(NB), ALU.mult)
    tt(r("ct", 60, 72), r("ct", 48, 60), r("ct", 36, 48), ALU.add)
    cp(r("oE"), r("ct", 60, 72))
    tt(r("ct", 132, 144), r("ct", 60, 72), r("ct", 108, 120), ALU.add)
    cp(r("oG"), r("ct", 132, 144))
    ts(r("ct", 72, 84), r("ct", 60, 72), 32.0, ALU.mult, par, ALU.add)
    tt(r("ct", 84, 96), r("ct", 72, 84), r("t1"), ALU.add)
    tt(r("ct", 72, 84), r("ct", 84, 96), r("ct", 96, 108), ALU.add)
    cp(r("oN2"), r("ct", 72, 84))
    ms(r("dS"), 0.0)
    ms(r("nlf"), 0.0)
    for x, v in ((r("dS", 0, 12), NM), (r("dS", 12, 24), NM + LN), (r("dS", 24, 36), NM + LN + TW), (r("thX"), 2 ** 19 + NM + LN)):
        ts(x, r("ct", 120, 132), p16, ALU.add, float(v), ALU.add)
    if CFG["wide"]:
        ts(r("tF", 0, 4), r("ct", 120, 124), p16, ALU.add)
        ts(r("t2"), r("tF", 0, 4), -5.5, ALU.add, 1.0 / 12.0, ALU.mult)
        ts(r("tF", 4, 8), r("t2"), -12.0, ALU.mult)
        tt(r("tF", 8, 12), r("tF", 4, 8), r("tF", 0, 4), ALU.add)
        ts(r("oF"), r("tF", 8, 12), 16.0, ALU.mult, 15.0, ALU.add)
    cp(r("nmf"), r("nmi"))
    act(r("X1"), (r("nmf"), r("oN1")))
    turn(r("X2"), r("X1"))
    act(r("Lf"), (r("X2"), r("oN2")))
    cp(r("off0"), r("Lf"))
    for m in range(16):
        iota(r("wr", m, m + 1), [[0, 1]], WT[m], 0)
    iota(r("dg"), [[1, 16]], 0, 0)
    for m in range(16):
        iota(r("kap", NB * m, NB * m + NB), [[0, NB]], KA[m], 0)
    iota(r("K37"), [[0, H], [1184, 16], [0, NB]], 0, 0)
    iota(r("cu"), [[256 * NB, H], [0, 16], [256, NB]], 0, 0)
    iota(r("sm"), [[0, 12], [1, 16]], 0, 0)
    iota(r("zz"), [[0, 192]], 0, 0)
    iota(r("cv", 0, 128), [[16, 8], [0, 16]], 0, 0)
    iota(r("cv", 128, 152), [[16 * NB, H], [1, NB], [0, 2]], 0, 0)
    iota(r("cv", 152, 164), [[32, 12]], 0, 0)
    iota(r("IO"), [[1, TW]], 0, 0)
    iota(r("ONE"), [[0, 128]], 1, 0)
    for nme in ("u", "zer"):
        iota(r(nme), [[0, SB[nme][0]]], 0, 0)
    ts(r("dg2"), r("dg"), p16, ALU.is_equal)
    tt(r("wr"), r("wr"), r("dg2"), ALU.mult)
    red(r("cf", 3, 4), r("wr"), ALU.add)
    ts(r("Zw"), r("ramp"), g16, ALU.is_equal, r("cf", 3, 4), ALU.mult)
    ms(r("h16"), 0.5)
    scan(r("wp"), r("h16"), r("zer"), 2.0, ALU.mult, ALU.add)
    tt(r("wp"), r("wp"), r("dg2"), ALU.mult)
    red(r("cf", 4, 5), r("wp"), ALU.add)
    ts(r("cf", 5, 6), r("cf", 4, 5), float(2 ** 95), ALU.mult, 65536.0, ALU.mult)
    ms(r("h17"), 1.0 / 65536.0)
    scan(r("wD"), r("h17"), r("zer"), r("cf", 5, 6), ALU.mult, ALU.add)
    ms(r("hlf"), 0.5)
    scan(r("th2"), r("hlf"), r("zz"), float(2 ** 97), ALU.mult, ALU.add)
    ts(r("nd"), r("sm"), p16, ALU.not_equal, HUGE, ALU.mult)
    tt(r("thM"), r("th2"), r("nd"), ALU.max)
    act(r("thL"), r("thM"), scale=2.0)
    ts(r("cf", 6, 7), p16, 16.0, ALU.mult)
    ts(r("cf", 7, 8), p16, float(NB), ALU.mult)
    tt(r("cf", 8, 9), p16, par, ALU.add)
    ts(r("cu"), r("cu"), r("cf", 6, 7), ALU.add, 1184.0, ALU.mult)
    tt(r("K37"), r("K37"), r("cu"), ALU.add)
    ts(r("sm"), r("sm"), 0.0, ALU.is_gt)
    ts(r("BO"), r("cv", 0, 128), g16, ALU.is_equal)
    ts(r("oD1"), r("cv", 128, 152), r("cf", 7, 8), ALU.add)
    ts(r("oD2"), r("cv", 152, 164), r("cf", 8, 9), ALU.add)

    RB = 192.0 - 7.5 / 16.0
    c0, hb = 0, 0
    for i, n in enumerate(CH):
        ts(r("F", c0, c0 + n), r("E1", c0, c0 + n), 1.0 / 16.0, ALU.mult, RB, ALU.add)
        act(r("S1", c0, c0 + n), r("E2", c0, c0 + n), bias=RB, scale=1.0 / 16.0)
        tt(r("sel", c0, c0 + n), r("F", c0, c0 + n), r("S1", c0, c0 + n), ALU.is_gt)
        if i in CFG["S2V"]:
            ts(r("S", c0, c0 + n), r("S1", c0, c0 + n), -FO, ALU.add)
        else:
            act(r("S", c0, c0 + n), r("S1", c0, c0 + n), bias=-FO)
        for a in range(c0, c0 + n, 512):
            e = min(a + 512, c0 + n)
            b1 = r(("pk0", "pk1", "pa", "pU")[hb % 4], 0, e - a)
            b2 = r(("pT", "pm", "pb", "pK")[hb % 4], 0, e - a)
            hb += 1
            lin(b1, [("I1", r("E1", a, e)), ("In16", r("F", a, e)), ("In16", r("sel", a, e))])
            lin(b2, [("I1", r("E2", a, e)), ("I16", r("sel", a, e)), ("In16", r("S", a, e))])
            act(r("At", a, e), b1, bias=16.0 + 16.0 * FO)
            tt(r("Y", a, e), b2, r("At", a, e), ALU.max)
        c0 += n

    def scat(tab, o0, src, s0, b0, b1, step):
        for a in range(b0, b1, step):
            e = min(a + step, b1)
            cp((r(tab), r("so", o0 + a, o0 + e)), r(src, s0 + 16 * a, s0 + 16 * e))

    QW = CW // 4

    def of(nme, h, k, n=1):
        return r(nme, CW * h + QW * k, CW * h + QW * (k + n))

    def gq(nme, h, k, n=1):
        return r(nme, 16 * CW * h + 16 * QW * k, 16 * CW * h + 16 * QW * (k + n))

    def bl(nme, h, o=0):
        return r(nme, o + NB * h, o + NB * h + NB)

    def ln(nme, h, o=0):
        return r(nme, o + CW * h, o + CW * h + CW)

    for t in range(3):
        last = t == 2
        sep = CFG["sep"] and not last
        off, z, sz = "off%d" % t, "z%d" % t, "sz%d" % t
        z1 = r(z, ZP, ZP + LN)
        flagv = LIMS[t] - 12 - 1.0 / 128.0
        e0 = [0]

        def hits(r0, k0, b, a, e):
            x = r("EQ", e0[0], e0[0] + e - a)
            ts(x, r("R", r0 + a, r0 + e), r("nlf", k0 + b, k0 + b + 1), ALU.is_equal, r("wD", b, b + 1), ALU.mult)
            e0[0] += e - a
            return x[1]
        tag[0], tag[1] = "L", t
        if t > 0:
            op("X", None, [r(off), r(z)], [], 0.0, "arr%d" % t, 10)
            side(r("Lf"), r(off))
        n3 = 0
        for h in range(H):
            pk = "pk%d" % h
            zh = r(z, 4 * CW * h, 4 * CW * h + 4 * CW)
            tag[0] = "A%d" % h
            way = CFG["A"][t][h]
            for k in range(4):
                x = gq("GA", h, k)
                if way[k] == "b":
                    tt(x, (r("Y", 0, NM), of(off, h, k)), zh, ALU.subtract)
                    act(x, x, AF.Abs, bias=-YO)
                else:
                    if way[k] == "d":
                        n = 2 if way[k + 1:k + 2] == "D" else 1
                        act(gq("GA", h, k, n), (r("Y", 0, NM), of(off, h, k, n)))
                    for a in range(0, 4 * CW, 384):
                        pbuf = r(CFG["dbank"][n3 % 2], 0, 384); n3 += 1
                        xa = r("GA", x[1] + a, x[1] + a + 384)
                        lin(pbuf, [("In", r(z, zh[1] + a, zh[1] + a + 384)), ("I1", xa)])
                        act(xa, pbuf, AF.Abs, bias=-YO)
            mm(r(pk, 0, CW), r("If"), ln("Lf", h), True, False)
            for i, (k, n) in enumerate(CFG["Aseg"]):
                seg(r(pk, QW * k, QW * (k + n)), "Zn", gq("GA", h, k), 16 * QW * n, False, i == len(CFG["Aseg"]) - 1)
            tag[0] = "U%d" % h
            for b in range(NB):
                red(r("k12", NB * h + b, NB * h + b + 1), r(pk, b, CW, NB), ALU.min)
            ts(bl("wi", h), bl("k12", h), 4095, ALU.bitwise_and)
            cp(bl("woff", h), bl("wi", h))
            W = bl("woff", h)
            if CFG["ywA"]:
                act(ln("yw", h), (r("Y", 0, NM), W))
            else:
                cp(ln("yw", h), (r("Y", 0, NM), W))
            act(ln("W2", h), (r("F", 0, NM), W), bias=-FO)
            act(ln("W2", h, LN), (r("S", 0, NM), W))
            seg(r(pk, 256, 256 + NB), "Zw", ("yw", CW * h), CW, True, True)
            uh, qh = r("u", 16 * h, 16 * h + NB), r("q", 16 * h, 16 * h + NB)
            ts(bl("ui", h), r(pk, 256, 256 + NB), -YO * sum(WT), ALU.add)
            ts(uh, bl("ui", h), 4095, ALU.bitwise_and)
            tt(bl("u2", h), uh, uh, ALU.mult)
            tt(ln("ku", h), (uh, bl("oE", h)), r("kap"), ALU.mult)
            ts(qh, bl("u2", h), 1.0 / 32.0, ALU.mult, r("Acol") if t > 0 else -0.375, ALU.add)
            tt(ln("c1", h), (qh, bl("oE", h)), ln("ku", h), ALU.add)
            ts(ln("c2", h), ln("c1", h), 4095, ALU.bitwise_and)
            cp(ln("coff", h), ln("c2", h))
            side(ln("cfl", h), ln("c2", h))
            for nme, n, o in (("FW", RF, 0), ("SW", RS, LN)):
                a = CW * n * h
                for k in range(n):
                    if nme not in CFG["G"] or k == 0:
                        ts(r(nme, a + CW * k, a + CW * (k + 1)), ln("W2", h, o), flagv, ALU.min)
                    elif k in (1, 2):
                        side(r(nme, a + CW * k, a + CW * 2 * k), r(nme, a, a + CW * k))
            tag[0] = "R%d" % h
            side(bl("nlf", h), bl("wi", h))
            cp(ln("R", h), (r("IO"), W))
            tag[0] = "G%d" % h
            lin(r("pm", 0, CW), [("I1", r("FW", CW * RF * h, CW * RF * h + CW)), ("I1", r("SW", CW * RS * h, CW * RS * h + CW))])
            act(ln("flag", h), r("pm", 0, CW), AF.Relu, bias=0.5 - 2 * flagv)
            seg(r("pm", 256, 256 + NB), "Z1", ("flag", CW * h), CW, True, True)
            act(bl("nfD", h), r("pm", 256, 256 + NB), AF.Relu, bias=1.0, scale=-4.0)
            if not last:
                act(bl("nfB", h), r("pm", 256, 256 + NB), AF.Relu, bias=16384.0, scale=-65536.0)
            zl = r(z, 4 * CW * h, 4 * CW * h + CW)
            for k in range(H):
                lin(r("pa", CW * k, CW * k + CW), [("I1", ln("yw", h)), ("In", zl)])
            tag[0] = "Z%d" % h
            act(r(sz, H * CW * h, H * CW * (h + 1)), r("pa", 0, H * CW), AF.Abs, bias=-YO)
            if sep:
                act(ln("D", h), r("pa", 0, CW), bias=-YO)
        tag[0] = "W"
        same = {b: hits(0, 0, b, 16 * b, LN) for b in range(12)}
        if sep:
            for b in range(12):
                mm(r("pT", 256 + 16 * b, 256 + LN), r("BO"), r("EQ", same[b], same[b] + LN - 16 * b), b == 0, b == 11)
            tt(r("f1"), r("pT", 256, 256 + LN), r("thM"), ALU.is_ge)
            scan(r("f1s"), r("sm"), r("f1"), 0.0, ALU.mult, ALU.max)
            tt(r("ya"), r("f1s", 15, LN, 16), r("nfD"), ALU.is_ge)
            tt(r("yb"), r("ya"), r("dS", 0, 12), ALU.mult)
            tt(r("yc"), r("yb"), r("nlf", 0, 12), ALU.max)
            cp(r("sy"), r("yc"))
        tag[0] = "N"
        ue = 16 * (H - 1) + NB
        ts(r("m1", 0, ue), r("u", 0, ue), 1023, ALU.bitwise_and)
        ts(r("m2", 0, ue), r("m1", 0, ue), 2.0, ALU.mult, 33.0, ALU.add)
        tt(r("p1"), (r("m2", 0, ue), r("oG")), r("Lf"), ALU.mult)
        tt(r("p2"), r("p1"), r("K37"), ALU.add)
        ts(r("p3"), r("p2"), 5, ALU.arith_shift_right, 4095, ALU.bitwise_and)
        if not last:
            side(r("so%d" % t), r("p3"))
            dst = T.cores[(rank + STEP) % N]
            rid, pid, _s = topo.addr(dst)
            en = topo.engines(core, dst)
            prs = [(r("so%d" % t), r("off%d" % (t + 1)))]
            prs += [(r(sz, LN * (k * H // 4), LN * (k * H // 4) + LN), r("z%d" % (t + 1), LN * k, LN * k + LN)) for k in range(4)]

            def send(prs=prs, rid=rid, pid=pid, en=en, t=t):
                tr = [RemoteDMATransfer(dst_ids=[DstId(rid=rid, pnc=pid)],
                                        dma_engine_mask=(1 << en[2 * k]) | (1 << en[2 * k + 1]),
                                        remote_sem=T.sem["arr%d" % (t + 1)], src=ap(a), dst=ap(b))
                      for k, (a, b) in enumerate(prs)]
                g.remote_dma_fused(tr, local_sem=T.sem.sent)
            op("R", send, [], [a for a, b in prs], 500.0, "sent", 2 * len(prs), EST["remote"])
        else:
            side(r("sl2"), r("p3"))
            store(T.yz[:], r(sz, SP, SP + LN), "s0")
            act(r("X1"), (r("sl2"), r("oD1")))
            turn(r("X2"), r("X1"))
            act(r("ynf"), (r("X2"), r("oD2")))
            store(T.yn[:], r("ynf"), "s3")
        tag[0] = "V"
        nf, fw, sw, W = r("nf"), r("W2", 0, LN), r("W2", LN, 2 * LN), r("woff")
        mm(r("pb", 0, LN), r("BO"), r("flag"), True, True)
        act(nf, r("pb", 0, LN), AF.Relu, bias=1.0, scale=-4.0)
        lin(r("pb", 0, LN), [("I1", r("yw")), ("In", z1), ("I64", nf)])
        act(r("rv"), r("pb", 0, LN), AF.Relu, bias=-YO - 48.0)
        if sep:
            act(r("vv"), z1, bias=YO)
        tag[0] = "I"
        act(r("EW", 0, LN), (r("E1", 0, NM), W))
        act(r("EW", LN, 2 * LN), (r("E2", 0, NM), W))
        lin(r("pa", 0, 384), [("In16", r("W2")), ("In", z1), ("I1", r("EW"))])
        act(r("ab"), r("pa", 0, 384), AF.Abs, bias=-192.0)
        act(r("sat"), r("W2"), AF.Relu, bias=-2.0)
        act(r("bb"), r("ab"), AF.Relu, bias=1.0, scale=-1.0)
        lin(r("pb", 0, 384), [("In", r("sat")), ("I1", nf), ("In", r("bb"))])
        act(r("inc"), r("pb", 0, 384), AF.Relu)
        lin(r("pb", 0, LN), [("I1", sw), ("I1", r("inc", LN, 2 * LN))])
        act(r("S", NM + LN, TW), r("pb", 0, LN))
        if not last:
            lin(r("pm", 0, LN), [("I1", fw), ("I1", r("inc", 0, LN))])
            act(r("Y", NM + LN, TW), r("pm", 0, LN), bias=FO + 16.0)
        if not last and not sep:
            lin(r("pm", 0, LN), [("I1", z1), ("In", sw), ("I256", nf)])
            act(r("ra"), r("pm", 0, LN), AF.Relu, bias=YO - 256.0)
            lin(r("pm", 0, LN), [("I1", sw), ("I1", r("ra"))])
            act(r("vA"), r("pm", 0, LN))
        lin(r("pa", 0, LN), [("I16", fw), ("I1", r("yw")), ("In", r("rv")), ("I16", nf), ("I16", r("inc", 0, LN))])
        act(r("EN1", 0, LN), r("pa", 0, LN), bias=-16.0)
        kill = {}
        MG = 1.5 * 2 ** 27
        for h in range(H):
            pk, kb = "pk%d" % h, 256 * h
            tag[0] = "C%d" % h
            fwh = r("FW", CW * RF * h, CW * RF * (h + 1))
            swh = r("SW", CW * RS * h, CW * RS * (h + 1))
            for k in range(4):
                x = gq("GS", h, k)
                if CFG["C"][h][k] == "f":
                    act(x, (r("S", 0, NM), of("coff", h, k)))
                for a in range(0, 4, RF):
                    xa = r("GS", x[1] + CW * a, x[1] + CW * (a + RF))
                    o = of("coff", h, k)
                    oa = r("coff", o[1] + NB * a, o[1] + NB * (a + RF))
                    tt(xa, (r("S", 0, NM), oa) if CFG["C"][h][k] == "e" else xa, fwh, ALU.min)
            for k in range(0, 4, CFG["Fw"]):
                x = gq("GF", h, k, CFG["Fw"])
                act(x, (r("F", 0, NM), of("coff", h, k, CFG["Fw"])), bias=-FO)
                for a in range(0, width(x), CW * RS):
                    xa = r("GF", x[1] + a, x[1] + a + CW * RS)
                    tt(xa, xa, swh, ALU.min)
            ext = r("pK", kb + CW, kb + CW + NB)
            lin(ext, [("If", bl("thX", h)), ("Inf", bl("nfD", h))])
            mm(r("pK", kb, kb + CW), r("If"), ln("cfl", h), True, False)
            whole = CFG["Cseg"][0][2] == 4
            if not whole:
                mm(r(pk, 0, CW), r("I1"), r("zz", 0, CW), True, False)
            for i, (gb, k, n) in enumerate(CFG["Cseg"]):
                seg(r(pk, QW * k, QW * (k + n)), "Zp", gq(gb, h, k), 16 * QW * n, whole and i == 0, i == len(CFG["Cseg"]) - 1)
            tag[0] = "K%d" % h
            ts(ln("rr", h), r(pk, 0, CW), MG, ALU.add, -MG, ALU.add)
            tt(ln("dd", h), ln("rr", h), r(pk, 0, CW), ALU.subtract)
            mm(r("pK", kb, kb + CW), r("I512"), ln("rr", h), False, False)
            mm(r("pK", kb, kb + CW), r("Ipen"), ln("dd", h), False, True)
            for b in range(NB):
                red(r("kc", NB * h + b, NB * h + b + 1), r("pK", kb + b, kb + CW + NB, NB), ALU.min)
            ts(bl("cn", h), bl("kc", h), 8191, ALU.bitwise_and)
            cp(bl("nlf", h, 28), bl("cn", h))
            cp(bl("cno", h), bl("cn", h))
            for b in range(NB * h, NB * h + NB):
                kill[b] = hits(0, 28, b, 16 * b, LN)
                if sep:
                    for h2 in range(h, H):
                        a, e = max(16 * b, CW * h2), CW * h2 + CW
                        mm(r(("pT", "pU")[h2], a - CW * h2, CW), r("BO"), r("EQ", kill[b] + a - 16 * b, kill[b] + e - 16 * b),
                           b == 0, b == NB * h2 + NB - 1)
            calls = (cp, tt, ts, act, mm, lin, scan, scat)
            if CFG["vsplit"][t] or h == H - 1:
                values(t, (h, h + 1) if CFG["vsplit"][t] else (0, H), tag, calls)
            tag[0] = "K%d" % h
            if sep:
                tt(ln("fk", h), r(("pT", "pU")[h], 0, CW), ln("th2", h), ALU.is_ge)
                tt(ln("gk", h), ln("fk", h), ln("D", h), ALU.mult)
                tt((r("Y", 0, NM + LN), bl("sy", h)), ln("gk", h), ln("vv", h), ALU.add)
            cp(ln("R", h, LN), (r("IO"), bl("cno", h)))
            if CFG["split"][t] or h == H - 1:
                part(t, (h, h + 1) if CFG["split"][t] else (0, H), same, kill, hits, tag, calls)
        tag[0] = "end"
        if last:
            store(T.ys[:], r("E2", 0, NM), "s1")
            tt(r("fo"), r("E1", 0, 768), r("E1", 768, 1536), ALU.add)
            for j in range(24, 64):
                mm(r("pm", 0, 64), r("I1"), r("E1", 64 * j, 64 * j + 64), j == 24, False)
            for j in range(12):
                mm(r("pm", 0, 64), r("I1"), r("fo", 64 * j, 64 * j + 64), False, j == 11)
            cp(r("yfs"), r("pm", 0, 64))
            store(T.yf[:], r("yfs"), "s4")
    return ops


def values(t, hs, tag, c):
    cp, tt, ts, act, mm, lin, scan, scat = c
    last = t == 2
    tag[0] = "X%d" % hs[0]
    b0, b1 = NB * hs[0], NB * hs[1]
    l0, l1 = 16 * b0, 16 * b1
    n = l1 - l0

    def bl(nme, o=0):
        return r(nme, o + b0, o + b1)

    def ln(nme, o=0):
        return r(nme, o + l0, o + l1)
    C = bl("cno")
    nf, sw = ln("nf"), ln("W2", LN)
    yc, fc = ln("C3"), ln("C3", LN)
    act(yc, (r("Y"), C))
    act(ln("SN"), (r("S"), C))
    act(fc, (r("F"), C), bias=-FO)
    lin(r("pb", n, 2 * n), [("I16", sw), ("I1", yc)])
    lin(r("pb", 0, n), [("I1", ln("yw")), ("In", ln("rv")), ("I16", nf), ("I16", ln("SN"))])
    act(r("EN2", 2 * l0, 2 * l1), r("pb", 0, 2 * n), bias=-16.0)
    lin(r("pa", 0, n), [("I16", fc), ("I1", yc)])
    act(ln("EN1", LN), r("pa", 0, n), bias=-16.0)


def part(t, hs, same, kill, hits, tag, c):
    cp, tt, ts, act, mm, lin, scan, scat = c
    last = t == 2
    sep = CFG["sep"] and not last
    b0, b1 = NB * hs[0], NB * hs[1]
    l0, l1 = 16 * b0, 16 * b1
    n = l1 - l0

    def bl(nme, o=0):
        return r(nme, o + b0, o + b1)

    def ln(nme, o=0):
        return r(nme, o + l0, o + l1)
    tag[0] = "Q%d" % hs[0]
    bank, o = ("pT", 256) if sep else (("pT", "pU")[hs[0]], 0)
    if sep:
        mm(r(bank, o, o + n), r("Ihg"), ln("f1"), True, False)
        mm(r(bank, o, o + n), r("Ihg"), ln("fk"), False, False)
    else:
        for done in (same, kill):
            for b in range(b1):
                a = max(16 * b, l0)
                mm(r(bank, o + a - l0, o + n), r("BO"), r("EQ", done[b] + a - 16 * b, done[b] + l1 - 16 * b),
                   done is same and b == 0, False)
    for k0 in (0, 28):
        for b in range(b1):
            a = max(16 * b, l0)
            x = hits(LN, k0, b, a, l1)
            mm(r(bank, o + a - l0, o + n), r("BO"), r("EQ", x, x + l1 - a), False, k0 > 0 and b == b1 - 1)
    ts(bl("nh"), bl("cn"), float(NM), ALU.is_ge)
    tt(bl("y1"), bl("nh"), bl("nfD"), ALU.subtract)
    tt(bl("y2"), bl("y1"), bl("dS"), ALU.mult)
    tt(bl("nlf", 16), bl("y2"), bl("nlf"), ALU.max)
    tt(ln("fail"), r(bank, o, o + n), ln("thM" if sep else "thL"), ALU.is_ge)
    scan(ln("fsc"), ln("sm"), ln("fail"), 0.0, ALU.mult, ALU.max)
    fD = r("fsc", l0 + 15, l1, 16)
    if not last:
        ts(bl("la1"), bl("cn"), float(TW), ALU.add)
        tt(bl("la2"), bl("la1"), bl("nfB"), ALU.subtract)
        tt(bl("nlf", 40), bl("la2"), bl("nlf"), ALU.max)
    if n == LN and CFG["wide"]:
        tt(r("fd"), (r("fsc"), r("oF", 0, 3)), r("dS"), ALU.mult)
        tt(r("of"), r("fd"), r("nlf", 16, 64), ALU.max)
        cp(r("so"), r("of"))
    else:
        for o in (12, 0) if last else (24, 0, 12):
            tt(bl("fd", o), fD, bl("dS", o), ALU.mult)
            tt(bl("of", o), bl("fd", o), bl("nlf", 16 + o), ALU.max)
            cp(bl("so", o), bl("of", o))
    if not last:
        if not sep:
            scat("YS", 24, "vA", 0, b0, b1, 12)
        tag[0] = "S"
        scat("FE", 24, "EN1", LN, b0, b1, CFG["pf"])
        scat("S", 0, "SN", 0, b0, b1, CFG["pf"])
        if sep:
            scat("S", 12, "W2", LN, b0, b1, CFG["pf"])
        tt(bl("mx"), fD, bl("nh"), ALU.max)
        if b1 == 12:
            mm(r("pm", 0, 12), r("ONE"), r("mx"), True, True)
            act(r("ajk"), r("pm", 0, 12), bias=128.0 - 0.375 / 12, scale=-1.0, acc=r("Acol"))
    tag[0] = "E"
    step = 12 if last else CFG["pe"]
    for h0, h1 in [(h, h + 1) for h in range(hs[0], hs[1])] if CFG["vsplit"][t] else [hs]:
        scat("E2", 0, "EN2", CW * h0, NB * h0, NB * h1, step)
        scat("E2", 12, "EN2", CW * h1, NB * h0, NB * h1, step)
    scat("E1", 0, "EN1", 0, b0, b1, step)
    if last:
        scat("E1", 12, "EN1", LN, b0, b1, step)


def overlap(x, y):
    if x[0] in PS:
        return True
    return x[1] < y[2] and y[1] < x[2]


QN = {"V": "V", "A": "A", "P": "P", "G": "G", "R": "G", "S": "S", "X": "X"}
PLAN = {}


def plan(ops):
    n = len(ops)
    hist, deps, soft = {}, [], []
    lastr, lasts = None, None
    for i, o in enumerate(ops):
        d, s = set(), set()
        for x in o["r"]:
            for j, y, wr in hist.get(x[0], []):
                if overlap(x, y) and (wr or (x[0] in PS and ops[j]["e"] != o["e"])):
                    d.add(j)
        for x in o["w"]:
            for j, y, wr in hist.get(x[0], []):
                if overlap(x, y):
                    (s if o["e"] == ops[j]["e"] == "P" else d).add(j)
        for x in o["w"]:
            if x[3] == 1:
                hist[x[0]] = [h for h in hist.get(x[0], []) if not (
                    (x[1] <= h[1][1] and h[1][2] <= x[2]) and x[0] not in PS)]
            if x[0] in PS:
                hist[x[0]] = [h for h in hist.get(x[0], []) if not (ops[h[0]]["e"] == "P" or h[0] in d)]
        for x in o["r"]:
            hist.setdefault(x[0], []).append((i, x, False))
        for x in o["w"]:
            hist.setdefault(x[0], []).append((i, x, True))
        if o["e"] == "X":
            s.add(lastr)
        if o["e"] == "R":
            lastr = i
        if o["e"] == "S" and o["w"]:
            if lasts is not None:
                s.add(lasts)
            lasts = i
        d.discard(i); s.discard(i)
        deps.append(d); soft.append(s - d)
    tail, dfree, t0 = [o["lat"] for o in ops], 0.0, 0.0
    for i, o in enumerate(ops):
        if o["e"] == "S":
            tail[i] = EST["dfix"] + o["lat"] / EST["dbw"]
            if o["w"]:
                t0 += o["dur"]
                dfree = max(dfree, t0 + 0.6 * EST["dfix"]) + o["lat"] / EST["dbw"]
                tail[i] = dfree + 0.4 * EST["dfix"] - t0
    units, uof, begin = [], [], []
    for i, o in enumerate(ops):
        p = ops[i - 1]
        if i and o["e"] == p["e"] and o["e"] in CFG["units"] and o["tag"] == p["tag"] and o["w"][0][0] == p["w"][0][0] and (
                (o["bun"] and o["bun"] == p["bun"]) or (o["e"] == "V" and deps[i] <= deps[i - 1] and begin[-1] + p["dur"] + o["dur"] < 350)):
            units[-1].append(i)
            begin.append(begin[-1] + p["dur"])
        else:
            units.append([i])
            begin.append(0.0)
        uof.append(len(units) - 1)
    dur = [begin[u[-1]] + ops[u[-1]]["dur"] for u in units]
    edge = {}
    for k in range(n):
        for j in deps[k] | soft[k]:
            if uof[j] != uof[k]:
                lag = tail[j] + EST["wake"] if j in deps[k] else (tail[j] if ops[k]["e"] == "X" else 0.0)
                lag -= dur[uof[j]] - begin[j] - ops[j]["dur"] + begin[k]
                if ops[j]["e"] == ops[k]["e"]:
                    lag = max(lag, 0.0)
                edge[uof[j], uof[k]] = max(edge.get((uof[j], uof[k]), lag), lag)
    n = len(units)
    succ, pred = [[] for _ in range(n)], [[] for _ in range(n)]
    for (j, k), lag in sorted(edge.items()):
        succ[j].append((k, lag)); pred[k].append((j, lag))
    tail = [tail[u[-1]] for u in units]
    qn = [QN[ops[u[0]]["e"]] for u in units]

    def listed(after, before, ready, prio):
        left = [len(x) for x in before]
        cand = {q: [] for q in "VAPGSX"}
        for i in range(n):
            if left[i] == 0:
                cand[qn[i]].append(i)
        free = {q: 0.0 for q in cand}
        order, end = [], [0.0] * n
        while len(order) < n:
            tq, q = min((max(free[q], min(ready[i] for i in l)), q) for q, l in cand.items() if l)
            l = cand[q]
            c = max((i for i in l if ready[i] <= tq), key=lambda i: prio[i])
            hs = [i for i in l if ready[i] > tq and prio[i] > prio[c] and tq + dur[c] - ready[i] > CFG["theta"] * dur[c]]
            if hs:
                th = min(ready[i] for i in hs)
                fit = [i for i in l if ready[i] <= tq and tq + dur[i] * (1 - CFG["theta"]) <= th]
                if not fit:
                    free[q] = th
                    continue
                c = max(fit, key=lambda i: prio[i])
            l.remove(c)
            free[q] = end[c] = tq + dur[c]
            order.append(c)
            for k, lag in after[c]:
                ready[k] = max(ready[k], end[c] + lag)
                left[k] -= 1
                if left[k] == 0:
                    cand[qn[k]].append(k)
        return order, end
    prio = [0.0] * n
    for i in range(n - 1, -1, -1):
        prio[i] = dur[i] + max([tail[i]] + [prio[k] + lag for k, lag in succ[i]])
    tags = [ops[u[0]]["tag"] + ops[u[0]]["e"] for u in units]
    rnd = np.random.RandomState(CFG["seed"])
    best, cur = None, None
    for it in range(CFG["turns"]):
        order, end = listed(succ, pred, [0.0] * n, prio)
        span = max(e + x for e, x in zip(end, tail))
        if best is None or span < best[0]:
            best = (span, order)
        if cur is None or span < cur + CFG["give"] * rnd.exponential():
            cur, back = span, listed(pred, succ, list(tail), [e + x for e, x in zip(end, tail)])[1]
        step = {k: rnd.normal(0.0, CFG["tjit"]) for k in sorted(set(tags))}
        prio = [b + float(j) + step[k] for b, j, k in zip(back, rnd.uniform(0.0, CFG["jit"], n), tags)]
    new, cur = best[1], None
    for it in range(CFG["rounds"]):
        free, end, ready, span = {q: 0.0 for q in "VAPGSX"}, [0.0] * n, [0.0] * n, 0.0
        for i in new:
            m = 0.0
            for j, lag in pred[i]:
                if end[j] + lag > m:
                    m = end[j] + lag
            ready[i] = m
            free[qn[i]] = end[i] = max(m, free[qn[i]]) + dur[i]
            if end[i] + tail[i] > span:
                span = end[i] + tail[i]
        if span <= best[0]:
            best = (span, new)
            PLAN["span"] = span
        val = span + CFG["mean"] * sum(end) / n
        if cur is None or val <= cur + CFG["amp"] * (1.0 - it / CFG["rounds"]) * rnd.exponential():
            begun = {}
            for i in new:
                begun[i] = max([end[i] - dur[i]] + [begun[j] for j, lag in pred[i]])
            cur, order, seen = val, sorted(new, key=lambda i: begun[i]), (ready, end)
            late, nxt, held = [0.0] * n, {}, []
            for a in range(n - 1, -1, -1):
                i = order[a]
                m = span - tail[i]
                for k, lag in succ[i]:
                    if late[k] - dur[k] - lag < m:
                        m = late[k] - dur[k] - lag
                if qn[i] in nxt:
                    m = min(m, late[nxt[qn[i]]] - dur[nxt[qn[i]]])
                late[i] = m
                nxt[qn[i]] = i
                if m - end[i] < CFG["slack"] and end[i] - dur[i] > ready[i] + 1.0:
                    held.append(a)
        b = held[rnd.randint(len(held))] if rnd.uniform() < CFG["crit"] else rnd.randint(1, n)
        i = order[b]
        ahead = [a for a in range(max(0, b - 150), b) if qn[order[a]] == qn[i] and seen[1][order[a]] > seen[0][i]]
        new = order
        if ahead:
            a = ahead[rnd.randint(len(ahead))]
            if rnd.randint(2):
                moved = {order[a]}
                for k in order[a + 1:b + 1]:
                    if any(j in moved for j, lag in pred[k]):
                        moved.add(k)
                if i not in moved:
                    new = order[:a] + [k for k in order[a:b + 1] if k not in moved] + [k for k in order[a:b + 1] if k in moved] + order[b + 1:]
            else:
                moved = {i}
                for k in order[b - 1:a - 1 if a else None:-1]:
                    if any(j in moved for j, lag in succ[k]):
                        moved.add(k)
                if order[a] not in moved:
                    new = order[:a] + [k for k in order[a:b + 1] if k in moved] + [k for k in order[a:b + 1] if k not in moved] + order[b + 1:]
    return deps, [i for u in best[1] for i in units[u]]


def emit(ops, g, T):
    if "p" not in PLAN:
        PLAN["p"] = plan(ops)
    deps, order = PLAN["p"]
    queue = {"V": g.vector, "A": g.scalar, "P": g.tensor, "G": g, "R": g, "S": g.sync}
    clock = {q: {} for q in "VAPGS"}
    seq, at = {}, {}
    for a, i in enumerate(order):
        o = ops[i]
        at[i] = a
        key = o["sem"] or "e" + o["e"]
        seq[key] = seq.get(key, 0) + 1
        o["key"], o["pos"], o["need"], o["waits"] = key, seq[key], False, []
        if o["e"] == "X":
            o["clk"] = {key: o["pos"]}
            continue
        ck = clock[QN[o["e"]]]
        for j in sorted(deps[i], key=lambda j: -at[j]):
            d = ops[j]
            if ck.get(d["key"], 0) >= d["pos"]:
                continue
            d["need"] = True
            o["waits"].append(j)
            for k, v in d["clk"].items():
                if ck.get(k, 0) < v:
                    ck[k] = v
        o["clk"] = dict(ck)
        o["clk"][key] = o["pos"]
    total = {}
    for i in order:
        o = ops[i]
        if o["sem"] or o["need"]:
            total[o["key"]] = total.get(o["key"], 0) + o["inc"]
            o["val"] = total[o["key"]]
    seen = {}
    for i in order:
        o = ops[i]
        if o["e"] == "X":
            continue
        q = queue[o["e"]]
        for j in o["waits"]:
            d = ops[j]
            q.wait_ge(T.sem[d["key"]], d["val"])
            seen[d["key"]] = max(seen.get(d["key"], 0), d["val"])
        ins = o["f"]()
        if o["e"] != "R" and (o["sem"] or o["need"]):
            ins.then_inc(T.sem[o["key"]], o["inc"])
    for k, v in total.items():
        if seen.get(k, 0) < v:
            g.sync.wait_ge(T.sem[k], v)


def rank_program(g, core, T, topo):
    if T.rank_of(core) is None:
        return
    emit(build(T, g, core, topo), g, T)
